import numpy as np, ml_dtypes
CORES = [40,41,42,43,44,45,46,47]
N = 8
BF = ml_dtypes.bfloat16
def gentries(a):
    return np.ascontiguousarray(a.reshape(8, 16, -1).transpose(0, 2, 1)).reshape(8, -1)
def gtable(e):
    e = np.asarray(e); return np.ascontiguousarray(e.reshape(8, -1, 16).transpose(0, 2, 1)).reshape(128, -1).astype(np.int32)
W, K, L, V, C, WB = 4096, 4, 512, 6, 8, 12
SH = (N, 8, 16, W)
def join(d0, c0, d1, c1):
    return (d0 + W * c0) + 32768 * (d1 + W * c1)
def goals(rng, hub, share):
    j = rng.integers(0, hub.shape[3], SH)
    return np.where(rng.random(SH, dtype=np.float32) < share, np.take_along_axis(hub, j, 3), rng.integers(0, W, SH))
def field(rng):
    return rng.integers(0, W, (N, 8, 16, K // 2 + 1)), rng.choice(np.array([0.0, 0.25, 0.6, 0.95]), (N, 8, 16, 1))
def parts(rng):
    hub, share = field(rng)
    a = join(goals(rng, hub, share), rng.integers(0, C, SH), goals(rng, hub, share), rng.integers(0, C, SH))
    pay = (0.25 + 0.75 * rng.random(SH, dtype=np.float32)) * np.exp2(rng.integers(-1, 2, (N, 8, 16, 1)))
    ac = 4 * rng.random((N, 8, 16, L)); st = rng.integers(0, W, (N, 8, K, L)); rs = (64 * rng.random((N, 8, K, L)) ** 3).astype(np.int64)
    return a, pay, ac, st, rs
def pack(a, pay, ac, st, rs):
    return {"arcs": np.ascontiguousarray(a.reshape(N, 128, W)).astype(np.int32), "pay": np.ascontiguousarray(pay.reshape(N, 128, W)).astype(BF),
            "ac": np.ascontiguousarray(ac.reshape(N, 128, L)).astype(np.float32), "st0": np.stack([gtable(b) for b in st]), "rs0": np.ascontiguousarray(rs.reshape(N, 8, K * L)).astype(np.int32)}
def setup_inputs(rng):
    return pack(*parts(rng))
def setup_inputs_spread(rng):
    a, pay, ac, st, rs = parts(rng)
    a[:, ::2] = rng.integers(0, 2 ** 30, (N, 4, 16, W))
    pay = (0.25 + 0.75 * rng.random(SH, dtype=np.float32)) * np.exp2(rng.integers(-1, 2, (N, 8, 1, W)))
    ac = np.exp2(12 * rng.random((N, 8, 16, L)) - 6); rs = rng.integers(0, 64, (N, 8, K, L))
    return pack(a, pay, ac, st, rs)
def setup_inputs_ends(rng):
    a, pay, ac, st, rs = parts(rng); top = 2 ** 30 - 1
    low = rng.choice(np.array([0.3, 0.5, 0.7]), (N, 8, 16, 1))
    a = np.where(rng.random(SH, dtype=np.float32) < 0.72, np.where(rng.random(SH, dtype=np.float32) < low, 0, top), a)
    st = np.where(rng.random(st.shape) < 0.75, (W - 1) * rng.integers(0, 2, st.shape), st)
    rs = np.where(rng.random(rs.shape) < 0.8, 63 * rng.integers(0, 2, rs.shape), rs)
    ac = np.where(rng.random(ac.shape) < 0.5, 64.0 * rng.integers(0, 2, ac.shape), ac)
    z = [0] + [W - j for j in range(1, K + 1)]
    for j in range(K + 1):
        a[:, :, 14:, z[j]] = 0 if j == 0 else join(z[j], C - 1, z[min(j + 1, K)], C - 1)
        a[:, 1:V, 13, z[j]] = join(0, C - 1, 0, C - 1) if j == 0 else join(z[j], 0, z[j], 0)
    a[:, 7, :14, W - 1] = top
    l = np.arange(7, L, 8); kind = rng.integers(0, 3, (N, 8, len(l))); kind[:, :, -1] = np.arange(8) % 3
    for k in range(K):
        st[:, :, k, l] = z[k]
        rs[:, :, k, l] = 0 if k == 0 else np.where(kind == 0, 63, np.where(kind == 1, 62, 63 if k <= K // 2 else 62))
    ac[:, :, :14, l] = 64.0; ac[:, :, 14, l] = 64.0 * rng.integers(0, 2, kind.shape); ac[:, :, 15, l] = 0.0
    fall = l[1::4]
    ac[:, 0, :15, fall] = 64.0; ac[:, 0, 15, fall] = 0.0
    ac[:, 1:V, :, fall] = 64.0; ac[:, 1:V, 13, fall] = 0.0
    st[:, :, :, L - 2] = W - 1; rs[:, :, :, L - 2] = 63; ac[:, :, :, L - 2] = 64.0
    over = np.arange(L - 3, 0, -32); y = W // 2 + np.arange(K)
    a[:, :, :, y] = join(rng.integers(0, W, (N, 8, 16, K)), C - 1, rng.integers(0, W, (N, 8, 16, K)), C - 1)
    st[:, :, :, over] = y[:, None]; rs[:, :, :, over] = 63
    best = rng.integers(1, 16, (N, 8, 1, len(over)))
    ac[:, :, :, over] = np.where(np.arange(16)[:, None] == best, 64.0 - rng.integers(1, 5, best.shape), 64.0)
    return pack(a, pay, ac, st, rs)
def setup_inputs_corners(rng):
    a, pay, ac, st, rs = parts(rng); pay[:, :, :, W - 1] = 2.0
    j = np.arange(2 * K); hub = K * ((rng.integers(0, W // K, (N, 8, 16, 1)) + 17 * j) % (W // K)) + j % K
    n = rng.choice(np.array([1, 2, K - 1, K, K + 1, 2 * K]), (N, 8, 16, 1)); cls = np.arange(W) % K
    mode = rng.integers(0, 4, (N, 8, 16, 1)); cost = []
    for u in range(2):
        cost.append(np.where(mode == 0, 0, np.where(mode == 1, C - 1, np.where(mode == 2, (C - 1) * rng.integers(0, 2, SH), rng.integers(0, C, SH)))))
    a = join(np.take_along_axis(hub, np.minimum(cls, n - 1), 3), cost[0], np.take_along_axis(hub, np.minimum(cls + K, n - 1), 3), cost[1])
    k = np.arange(K)[:, None]; nil = np.zeros((K, L), np.int64)
    st = K * rng.integers(0, W // K, (N, 8, K, L)) + k
    ways = (nil, nil + 63, nil + np.where(k == 0, 0, 63), nil + np.where(k == K - 1, 0, 63))
    for q in range(N):
        p = rng.permutation(8); b = rng.permutation(8)
        for i in range(4): rs[q, p[i]] = ways[i]
        st[q, b[:2]] = st[q, b[:2], :1]
        st[q, b[2]] = (W - 1) * rng.integers(0, 2, (K, L))
    return pack(a, pay, ac, st, rs)
def setup_inputs_calm(rng):
    a, pay, ac, st, rs = parts(rng); hub, share = field(rng)
    hc = ((2 * np.arange(N)[:, None] + np.arange(8)) % 4)[:, :, None, None]
    c0 = (rng.random(SH) * (hc + 1)).astype(np.int64); c1 = (rng.random(SH) * (hc + 1)).astype(np.int64)
    a = join(goals(rng, hub, share), c0, goals(rng, hub, share), c1)
    rs = np.minimum(rng.integers(0, 4, rs.shape), hc); col = np.arange(L) % 4; s = ac.shape
    ac = np.where(col == 0, 1.0 * rng.integers(0, 3, s), np.where(col == 1, 1 + 2.0 ** -23 * rng.integers(0, 8, s), np.where(col == 2, 0.5 * rng.integers(0, 6, s), 0.0)))
    h = K // 2; z = rng.permutation(W - 1)[:4 * h]
    i = np.arange(4 * h); lab = np.arange(16)[:, None]
    to = np.where(i < 2 * h, 2 * h, 0) + h * (lab % 2); price = np.where(i < 2 * h, 3, 1)
    a[:, :, :, z] = join(z[to + rng.integers(0, h, (N, 8, 16, 4 * h))], price, z[to + rng.integers(0, h, (N, 8, 16, 4 * h))], price)
    l = np.arange(3, L, 8); k = np.arange(K)[:, None]; b = rng.integers(0, 2, (N, 8, 1, len(l)))
    st[:, :, :, l] = z[np.where(k < h, 0, 2 * h) + h * b + k % h]; rs[:, :, :, l] = np.where(k < h, 0, 1)
    p = rng.integers(0, 15, b.shape); q = p + 1 + 2 * (rng.random(b.shape) * ((16 - p) // 2)).astype(np.int64)
    pair = np.array([[11, 8], [8, 5], [16, 11], [5, 0]]); kind = rng.integers(0, 4, b.shape)
    base = 0.25 + 2.0 ** -21 * rng.integers(0, 2 ** 17, b.shape)
    ac[:, :, :, l] = np.where(lab == p, base + 2.0 ** -25 * pair[kind, 0], np.where(lab == q, base + 2.0 ** -25 * pair[kind, 1], 1 + rng.random((N, 8, 16, len(l)))))
    return pack(a, pay, ac, st, rs)
def check_ranges(d):
    bad = []
    for k, lo, hi in (("arcs", 0, 2 ** 30 - 1), ("st0", 0, W - 1), ("rs0", 0, 63)):
        if not (np.min(d[k]) >= lo and np.max(d[k]) <= hi): bad.append("range of " + k)
    e = np.asarray(d["ac"]).astype(np.float32)
    if not np.all((e == 0) | ((e >= 2.0 ** -51) & (e <= 64))): bad.append("range of ac (0, or from 2**-51 to 64)")
    e = np.asarray(d["pay"]).astype(np.float32)
    if not np.all((e >= 0.125) & (e <= 2)): bad.append("range of pay (from 0.125 to 2)")
    return bad
def reference(arcs, pay, ac, st0, rs0):
    A = arcs.astype(np.int32).reshape(N, 8, 16, W); P = pay.astype(np.float32).reshape(N, 8, 16, W); B = ac.astype(np.float32).reshape(N, 8, 16, L)
    s = np.stack([gentries(b) for b in st0]).astype(np.int64); r = rs0.astype(np.int32)
    no = np.arange(2 * K, dtype=np.int32)[:, None]
    ys = np.zeros((N, 8, 16, L)); ym = np.zeros((N, 8, 16, L))
    for t in range(V):
        back = (-t, -t)
        a = np.take_along_axis(np.roll(A, back, (0, 1)), s[:, :, None, :], 3)
        a = np.concatenate([a & 32767, a >> 15], axis=3).reshape(N, 8, 16, 2 * K, L)
        c = (a >> WB) + np.concatenate([r, r], axis=2).reshape(N, 8, 1, 2 * K, L)
        m = np.min(c, axis=3)
        lab = np.argmin(m.astype(np.float32) + np.roll(B, back, (0, 1)), axis=2)[:, :, None, :]
        d = np.take_along_axis(a, lab[:, :, :, None, :], 2)[:, :, 0] & (W - 1)
        x = np.take_along_axis(c, lab[:, :, :, None, :], 2)[:, :, 0] - np.take_along_axis(m, lab, 2)
        key = x * 16 + no
        dup = np.any((d[:, :, :, None] == d[:, :, None]) & (key[:, :, None] < key[:, :, :, None]), axis=3)
        o = np.argsort(np.where(dup, key + 65536, key), axis=2)[:, :, :K]
        gone = np.take_along_axis(dup, o, 2)
        s = np.where(gone, W - 1, np.take_along_axis(d, o, 2)).astype(np.int64).reshape(N, 8, K * L)
        r = np.where(gone, 64, np.take_along_axis(x, o, 2)).astype(np.int32).reshape(N, 8, K * L)
        v = np.take_along_axis(np.roll(P, back, (0, 1)), s[:, :, None, :], 3).reshape(N, 8, 16, K, L) * np.exp(r.astype(np.float64) * -0.125).reshape(N, 8, 1, K, L)
        ys = ys + np.add.reduce(v, axis=3); ym = ym + np.max(v, axis=3)
    return {"ys": ys.reshape(N, 128, L).astype(np.float32), "ym": ym.reshape(N, 128, L).astype(np.float32)}

def check_inputs(d):
    bad = list(check_ranges(d))
    if not bad:
        for name, y in reference(**d).items():
            for q in range(N):
                v = np.abs(np.asarray(y[q], np.float64)); s = np.sqrt(np.mean(v * v))
                if v.max() > 8 * s or s < 2.0 ** 0: bad.append('%s of rank %d is uneven or too small' % (name, q))
    return bad

@@ -1,0 +1,582 @@
+import numpy as np
+from concourse.bass import DstId, RemoteDMATransfer
+from concourse.mybir import AluOpType as A
+from concourse.mybir import ActivationFunctionType as F
+
+NV = 6
+MCV = 24
+MSV = 2
+FOLD = False
+CH = [0, 512, 1536, 2816, 3840, 4096]
+SW = [(0, 1536), (1536, 2816), (2816, 4096)]
+PC = 256
+TRIES = 1500
+SCRATCH = {}
+
+
+def _sb(n, w, d, where="sbuf"):
+    SCRATCH[n] = (where, [128, w], d)
+
+
+for _n, _w, _d in [
+        ("arc", 4096, "int32"), ("xt", 8192, "int32"), ("mn", 4096, "float32"),
+        ("mc", 4096, "bfloat16"), ("payr", 4096, "bfloat16"), ("acs", 512, "float32"), ("act", 512, "float32"),
+        ("sti", 128, "int32"), ("stf", 128, "float32"), ("off0", 128, "uint16"), ("rsi", 256, "int32"), ("r0", 256, "bfloat16"),
+        ("ci", 32, "int32"), ("cf", 40, "float32"), ("cm", 16, "float32"), ("i8", 16, "float32"),
+        ("colg", 128, "float32"), ("colk", 128, "float32"), ("coln", 132, "float32"), ("colf", 128, "float32"), ("colq", 128, "float32"),
+        ("one", 128, "bfloat16"), ("onef", 256, "float32"), ("pm", 4 * 132, "float32"), ("lm", 128, "bfloat16"), ("him", 512, "bfloat16"),
+        ("idb", 128, "bfloat16"), ("idn", 128, "bfloat16"), ("idf", 256, "float32"), ("ids", 128, "float32"),
+        ("idm", 128, "bfloat16"), ("idk", 128, "bfloat16"), ("bo64", 128, "bfloat16"), ("bo128", 128, "bfloat16"), ("bo2", 16, "float32"),
+        ("sel", 14 * 128, "bfloat16"), ("rm", 5 * 128, "bfloat16"),
+        ("cra", 128, "bfloat16"), ("crb", 128, "bfloat16"), ("lf", 24, "float32"), ("lu", 16, "uint16"),
+        ("z16", 256, "float32"), ("z8", 128, "float32"),
+        ("offo", 13 * 64, "uint16"), ("eo", 12 * 128, "bfloat16"), ("offi", 10 * 128, "uint16"), ("ei", 10 * 128, "bfloat16"),
+        ("smo", (12 * 1024 + 1024) if FOLD else 12 * 512, "float32"), ("smi", 10 * 512, "float32"), ("yo", 1024, "float32")]:
+    _sb(_n, _w, _d)
+for _h in "01":
+    for _n, _w, _d in [
+            ("mcg", 1024, "bfloat16"), ("c0s", 256, "bfloat16"), ("m1", 256, "bfloat16"), ("m2", 256, "bfloat16"),
+            ("m3", 256, "bfloat16"), ("sc", 256, "float32"), ("nwt", 256, "bfloat16"), ("nwl", 256, "bfloat16"),
+            ("msk", 1024, "bfloat16"), ("gm", 1024, "float32"), ("cst", 128, "bfloat16"),
+            ("ofl", 64, "float32"), ("ofh", 64, "float32"), ("ofm", 64, "float32"), ("of2", 64, "uint16"),
+            ("ds", 128, "float32"), ("af", 128, "float32"), ("so", 512, "float32"), ("eq", 128, "bfloat16"), ("mall", 64, "int32"),
+            ("sall", 72, "int32"), ("xq", 64, "bfloat16"), ("hh", 48, "float32"),
+            ("nrc", 128, "bfloat16"), ("z2", 136, "float32"), ("pg", 1024, "bfloat16")] + ([] if FOLD else [
+            ("rho", 1024, "float32"), ("os_", 1024, "float32"), ("om_", 1024, "float32")]):
+        _sb(_n + _h, _w, _d)
+for _n in ["pa0", "pb0", "pa1", "pb1", "pw0", "pw1", "py0", "py1"]:
+    _sb(_n, 512, "float32", "psum")
+
+SEMAPHORES = (["cV", "cS", "cP", "cG", "sent", "stored"] + ["ld%d" % i for i in range(10)] + ["sw%d" % i for i in range(2 * len(SW))]
+              + ["ar%d" % i for i in range(10)] + ["sm%d" % i for i in range(10)])
+
+CY, PCY = 1.0, 0.5
+HOP, NET, GA = 120.0, 3000.0, 1.5
+
+
+def ap(b, c0=0, c1=None, st=1, p0=0, p1=128):
+    return (b, c0, SCRATCH[b][1][1] if c1 is None else c1, st, p0, p1)
+
+
+def ncol(a):
+    return len(range(a[1], a[2], a[3]))
+
+
+def build(g, T, topo, rank):
+    ops, cur = [], [None]
+    q = {"V": g.vector, "S": g.scalar, "P": g.tensor, "G": g, "Y": g.sync}
+
+    def R(a):
+        if isinstance(a, (int, float)) or a is None:
+            return a
+        if a[0] == "ind":
+            return R(a[1]).indirect(R(a[2]))
+        if a[3] == 1:
+            return T[a[0]][a[4]:a[5], a[1]:a[2]]
+        return T[a[0]][a[4]:a[5], a[1]:a[2]:a[3]]
+
+    def op(eng, fn, rd, wr, dur, **kw):
+        flat = []
+        for a in rd:
+            if isinstance(a, tuple):
+                flat += [a[1], a[2]] if a[0] == "ind" else [a]
+        ops.append(dict(half=cur[0], eng=eng, fn=fn, rd=flat, wr=wr, dur=dur, **kw))
+
+    def vdur(out, ins, tt=False):
+        n = ncol(out)
+        if ins and ins[0][0] == "ind":
+            return 60 + n * GA * CY
+        c = 0.5 if all(SCRATCH[a[0]][2] in ("bfloat16", "uint16") for a in [out] + ins) else 1.0
+        if tt and not any(SCRATCH[a[0]][0] == "psum" for a in ins):
+            c *= 2
+        return 30 + max(64, n * c) * CY
+
+    def tt(out, i0, i1, o):
+        op("V", lambda: g.vector.tensor_tensor(R(out), R(i0), R(i1), o), [i0, i1], [out], vdur(out, [i0, i1], True))
+
+    def ts(out, i0, s1, o0, s2=None, o1=None):
+        if o1 is None:
+            fn = lambda: g.vector.tensor_scalar(R(out), R(i0), R(s1), None, o0)
+        else:
+            fn = lambda: g.vector.tensor_scalar(R(out), R(i0), R(s1), R(s2), o0, o1)
+        op("V", fn, [i0, s1, s2], [out], vdur(out, [i0]))
+
+    def cp(out, i0):
+        op("V", lambda: g.vector.tensor_copy(R(out), R(i0)), [i0], [out], vdur(out, [i0]))
+
+    def ms(out, v):
+        op("V", lambda: g.vector.memset(R(out), v), [], [out], vdur(out, []))
+
+    def scan(out, d0, d1, o0, o1):
+        op("V", lambda: g.vector.tensor_tensor_scan(R(out), R(d0), R(d1), 0.0, o0, o1), [d0, d1], [out], vdur(out, [d0, d1]))
+
+    def act(out, i0, f=F.Identity, bias=0.0, scale=1.0):
+        d = 100 + ncol(out) * CY * (GA if i0[0] == "ind" else 1)
+        op("S", lambda: g.scalar.activation(R(out), R(i0), f, bias=R(bias), scale=R(scale)), [i0, bias, scale], [out], d)
+
+    def mm(lst):
+        def fn():
+            h = None
+            for (o, l, r, s0, s1) in lst:
+                h = g.tensor.matmul(R(o), R(l), R(r), s0, s1)
+            return h
+        d = 40
+        for (o, l, r, s0, s1) in lst:
+            d += 15 + max(min(64, ncol(l)), ncol(r)) * PCY * (4 if SCRATCH[l[0]][2] == "float32" else 1)
+        op("P", fn, [x[1] for x in lst] + [x[2] for x in lst], [x[0] for x in lst], d)
+
+    def iota(out, pat, base, cmul):
+        if SCRATCH[out[0]][2] == "int32":
+            fn = lambda: g.iota(R(out), pat, base, cmul)
+        else:
+            fn = lambda: g.iota(R(out), pat, base, cmul, allow_small_or_imprecise_dtypes=True)
+        op("G", fn, [], [out], 150 + 2 * ncol(out) * CY)
+
+    def asel(out, i0, pat, o, base, cmul):
+        op("G", lambda: g.affine_select(R(out), R(i0), pat, o, 0.0, base, cmul), [i0], [out], 200 + 2 * ncol(out) * CY)
+
+    def load(sem, pairs, wr, lat, rd=()):
+        def fn():
+            for (o, i) in pairs:
+                g.sync.dma_start(o, i).then_inc(T.sem[sem], 16)
+        op("Y", fn, list(rd), wr, 60 * len(pairs), dma=(sem, 16 * len(pairs)), lat=lat)
+
+    ind = lambda w, o: ("ind", w, o)
+    col = lambda j: ap("cf", j, j + 1)
+    blk = lambda n, j, w=128, p1=128: ap(n, w * j, w * j + w, p1=p1)
+
+    for i in range(len(CH) - 1):
+        load("ld%d" % i, [(T.arc[:, CH[i]:CH[i + 1]], T.arcs[:, CH[i]:CH[i + 1]])], [ap("arc", CH[i], CH[i + 1])], 2200 + 2.2 * CH[i + 1])
+    load("ld7", [(T.sti[:], T.st0[:])] + [(T.rsi[16 * p:16 * p + 16, :], T.rs0[:, (3 - p) * 512:(4 - p) * 512]) for p in range(4)],
+         [ap("sti"), ap("rsi")], 12000)
+    load("ld6", [(T.acs[:], T.ac[:])], [ap("acs")], 12500)
+
+    iota(ap("ci", 0, 9), [[2, 9]], 0, 1)
+    iota(ap("i8"), [[1, 16]], 0, 0)
+    iota(ap("colg"), [[1, 8], [0, 16]], 0, 0)
+    iota(ap("colk"), [[1, 64], [0, 2]], 0, 0)
+    iota(ap("coln"), [[1, 132]], 0, 0)
+    iota(ap("colf"), [[8, 8], [0, 2], [1, 8]], 0, 0)
+    iota(ap("colq"), [[1, 32], [0, 4]], 0, 0)
+    iota(ap("crb"), [[0, 16], [-1, 4], [4, 2]], 3, 0)
+    iota(ap("lf", 0, 8), [[2, 8]], 0, 0)
+    ms(ap("onef"), 1.0)
+    act(ap("one"), ap("onef", 0, 128))
+    asel(ap("idf", 0, 128), ap("onef", 0, 128), [[-1, 128]], A.is_equal, 0, 1)
+    act(ap("idf", 128, 256), ap("idf", 0, 128))
+    sh, an = A.logical_shift_right, A.bitwise_and
+    for j, (src, s, m) in enumerate([(0, 1, 7), (0, 4, 7), (0, 0, 1), (0, 0, 15), (0, 0, 3), (0, 2, 1), (0, 3, 1), (1, 1, 7), (8, 4, 7),
+                                     (0, 0, 7), (0, 2, 3), (0, 1, 1)]):
+        ts(ap("ci", 16 + j, 17 + j), ap("ci", src, src + 1), s, sh, m, an)
+    cp(ap("cf", 0, 12), ap("ci", 16, 28))
+    G1, P4, B1, Q15, Q3, Q2, Q8, G1R, G4R, Q7, Q23, B2 = [col(j) for j in range(12)]
+    lin = lambda j, a, m, b: act(col(j), a, scale=m, bias=b)
+    lin(12, P4, 2.0, B1)
+    lin(13, G1R, 8.0, P4)
+    lin(14, col(13), 1.0, 4.0)
+    lin(15, B1, 4.0, col(13))
+    lin(16, B1, 2.0 ** -9, -2.0 ** -9)
+    lin(17, B1, -2.0 ** -9, 0.0)
+    ts(col(18), Q15, 0.0, A.is_equal)
+    lin(19, col(18), -1.0, 1.0)
+    lin(20, Q3, 16.0, Q2)
+    lin(21, Q8, -1.0, 1.0)
+    lin(22, Q8, 64.0, 0.0)
+    lin(23, Q8, 8.0, G4R)
+    lin(24, P4, 8.0, Q7)
+    lin(25, Q8, 4096.0, 0.0)
+    lin(26, P4, 4.0, 0.0)
+    act(ap("cf", 28, 32), ap("i8", 0, 4), bias=col(26))
+    lin(27, col(26), 1.0, Q3)
+    lin(32, col(27), 4.0, 3.0)
+    for j, (b, m) in enumerate([(B1, 1.0), (B2, 3.0), (Q2, 15.0), (Q8, 255.0)]):
+        lin(33 + j, b, m, 1.0)
+    lin(37, col(33), col(34), 0.0)
+    lin(38, col(35), col(36), 0.0)
+    lin(39, col(37), col(38), 0.0)
+    ts(ap("cm", 0, 8), ap("i8", 0, 8), col(12), A.is_equal, -1.0, A.mult)
+    ts(ap("bo64"), ap("colg"), G1, A.is_equal)
+    ts(ap("bo128"), ap("colg"), P4, A.is_equal)
+    ts(ap("bo2"), ap("i8"), col(23), A.is_equal)
+    ts(ap("lm"), ap("colf"), col(24), A.is_equal, 2.0, A.mult)
+    tt(ap("lm"), ap("lm"), ap("bo128"), A.subtract)
+    act(ap("lm"), ap("lm"), scale=col(39))
+    ts(ap("lf", 20, 24), ap("i8", 0, 4), Q23, A.is_equal)
+    for v in range(4):
+        ts(blk("him", v), ap("colq"), col(28 + v), A.is_equal, col(25), A.mult)
+        ts(blk("pm", v, 132), ap("coln"), col(32), A.is_equal, ap("lf", 20 + v, 21 + v), A.mult)
+    if not FOLD:
+        tt(ap("cm", 8, 14), ap("cm", 2, 8), ap("cm", 0, 6), A.subtract)
+    for j in range(8 if FOLD else 14):
+        act(blk("sel", j), ap("bo64"), scale=ap("cm", j, j + 1))
+    idf, idb = ap("idf", 0, 128), ap("idb")
+    for n, v in (("idb", 1.0), ("idn", -1.0), ("idm", -4096.0), ("idk", 7 * 2.0 ** -12), ("ids", 2.0 ** -24)):
+        act(ap(n), idf, scale=v)
+    act(ap("crb"), ap("crb"), scale=2.0 ** -12)
+    act(ap("cra"), ap("one"), scale=-35.0 / 128)
+    ts(blk("rm", 0), ap("colk"), col(15), A.is_equal, -2.0 ** -9, A.mult)
+    for h in range(2):
+        for b in range(2):
+            ts(blk("rm", 1 + 2 * h + b), ap("colk"), col(13 + b), A.is_equal, col(16 + h), A.mult)
+    act(ap("lf", 8, 16), ap("lf", 0, 8), bias=col(20))
+    act(ap("lf", 8, 16), ap("lf", 8, 16), scale=col(21), bias=col(22))
+    act(ap("lf", 0, 8), ap("lf", 0, 8), bias=Q8)
+    cp(ap("lu"), ap("lf", 0, 16))
+    L1, L3 = ap("lu", 0, 8), ap("lu", 8, 16)
+    act(ap("z16"), ap("onef"), scale=0.0)
+    act(ap("z16", 0, 256, 16), ap("onef", 0, 16), scale=1000.0)
+    act(ap("z8"), ap("onef", 0, 128), scale=0.0)
+    act(ap("z8", 0, 128, 8), ap("onef", 0, 16), scale=2.0)
+    ms(ap("offo", 0, 64), 0)
+    for h in "01":
+        if not FOLD:
+            act(ap("rho" + h, 0, 1024, 4), ap("onef"), scale=0.0)
+        act(ap("nwt" + h, 0, 1), ap("onef", 0, 1), scale=0.0)
+        act(ap("nrc" + h, 48, 128), ap("onef", 0, 80), scale=0.0)
+        act(ap("z2" + h, 0, 8), ap("onef", 0, 8), scale=0.0)
+        ms(ap("sall" + h, 64, 72), 0)
+    for i in range(len(CH) - 1):
+        c = (CH[i], CH[i + 1])
+        ts(ap("xt", *c), ap("arc", *c), 32767, an)
+        ts(ap("arc", *c), ap("arc", *c), 15, sh)
+        tt(ap("mn", *c), ap("xt", *c), ap("arc", *c), A.min)
+        act(ap("mc", *c), ap("mn", *c), bias=159.5 + 2.0 ** -13, scale=2.0 ** -12)
+    for i, (c0, c1) in enumerate(SW):
+        lo = lambda n, k, o: T[n][16 * k:16 * k + 8, o + c0:o + c1]
+        hi = lambda n, k, o: T[n][16 * k + 8:16 * k + 16, o + c0:o + c1]
+        load("sw%d" % (2 * i), [(lo("xt", k, 4096), hi("xt", k, 0)) for k in range(8)] + [(hi("xt", k, 4096), hi("arc", k, 0)) for k in range(8)],
+             [ap("xt", 4096 + c0, 4096 + c1)], 2200 + 2.2 * (c1 - c0), [ap("xt", c0, c1), ap("arc", c0, c1)])
+        load("sw%d" % (2 * i + 1), [(hi("xt", k, 0), lo("arc", k, 0)) for k in range(8)],
+             [ap("xt", c0, c1)], 2200 + 1.1 * (c1 - c0), [ap("arc", c0, c1)])
+    load("ld8", [(T.payr[16:128, :], T.pay[0:112, :]), (T.payr[0:16, :], T.pay[112:128, :])], [ap("payr")], 6000, [ap("mn", 2815, 2816)])
+    cp(ap("stf"), ap("sti"))
+    ts(ap("r0", p1=64), ap("rsi", p1=64), -1.0, A.mult)
+    for h in range(2):
+        bank = "pb%d" % h
+        mm([(ap(bank, c, 64, 4), ap("pm", 132 * c + 3 - p, 132 * c + 131 - p), ap("stf", 32 * (3 - p) + 16 * h, 32 * (3 - p) + 16 * h + 16),
+             p == 0, p == 3) for c in range(4) for p in range(4)])
+        cp(blk("off0", h, 64), ap(bank, 0, 64))
+        bank = "pa%d" % h
+        for b in range(2):
+            o, i = blk(bank, b), ap("acs", 256 * h + b, 256 * h + 256, 2)
+            op("P", lambda o=o, i=i: g.tensor.transpose(R(o), R(i), R(idf)), [i, idf], [o], 300)
+        act(blk("act", h, 256), ap(bank, 0, 256))
+
+    nr = len(T.cores)
+    me, nxt = T.cores[rank], T.cores[(rank + 1) % nr]
+
+    def dst(c):
+        a = topo.addr(c)
+        return DstId(rid=a[0], pnc=a[1])
+
+    def emask(c, part, of):
+        e = topo.engines(me, c)
+        k = len(e) // of
+        return int(sum(1 << x for x in e[part * k:part * k + k])), k
+
+    sent, late = [0], {}
+    for t in range(NV):
+        for h in range(2):
+            H = str(h)
+            cur[0] = h
+            PA, PB = "pa" + H, "pb" + H
+            s = 2 * t + h
+            cbank = {2: ap(PA, 0, 256), 1: ap(PB, 0, 256), 0: ap(PA, 256, 512), 3: ap(PB, 256, 512)}
+            if t == 0:
+                of = blk("off0", h, 64)
+            else:
+                of = ap("offi", 128 * (s - 2) + 64, 128 * (s - 1))
+                ein = blk("ei", s - 2, p1=48)
+            act(ap("mcg" + H, 16 * MCV, 1024), ind(ap("mc"), ap(of[0], of[1] + MCV, of[2])), bias=-160.0)
+            if MCV:
+                ts(ap("mcg" + H, 0, 16 * MCV), ind(ap("mc"), ap(of[0], of[1], of[1] + MCV)), -160.0, A.add)
+            cp(ap("ofl" + H), of)
+            act(ap("ofh" + H), ap("ofl" + H), bias=4096.0)
+            last = ap("mcg" + H, 3, 1024, 4)
+            for p in ([3, 2, 1, 0] if t == 0 else [2, 1, 0]):
+                c = cbank[p]
+                lst = [(c, idb, ap("mcg" + H, p, 1024, 4), True, False)]
+                if t == 0:
+                    lst.append((c, blk("sel", 2 * p + h, p1=64), ap("r0", p1=64), False, True))
+                else:
+                    for b in range(2):
+                        lst.append((ap(c[0], c[1] + b, c[2], 2), blk("sel", 2 * p + b, p1=48), ein, False, b == 1))
+                mm(lst)
+                if p == 3:
+                    last = ap("c0s" + H)
+                    act(last, c)
+                else:
+                    tt(ap("m%d" % (3 - p) + H), c, last, A.min)
+                    last = ap("m%d" % (3 - p) + H)
+            mm([(blk(PB, 2 + b), ap("m3" + H, b, 256, 2), idb, True, True) for b in range(2)])
+            tt(ap("sc" + H), ap(PB, 256, 512), blk("act", h, 256), A.add)
+            scan(ap(PA, 0, 256), ap("z16"), ap("sc" + H), A.add, A.min)
+            tt(ap("nwt" + H, 1, 256), ap(PA, 0, 255), ap("sc" + H, 1, 256), A.is_gt)
+            mm([(ap(PB, b, 256, 2), blk("nwt" + H, b), idb, True, True) for b in range(2)])
+            act(ap("nwl" + H), ap(PB, 0, 256), scale=col(19), bias=col(18))
+            LL, HI = ap(PA, 256, 512), ap(PB, 256, 320)
+            mm([(LL, ap("lm"), ap("nwl" + H), True, True)])
+            mm([(HI, idf, ap("ofl" + H), True, False)]
+               + [(HI, blk("him", v), ap("nwl" + H, v, 256, 4), False, v == 3) for v in range(4)])
+            for p in range(MSV):
+                ts(ap("msk" + H, p, 1024, 4), LL, 0.0, A.max, 1.0, A.min)
+            for p in range(MSV, 4):
+                act(ap("msk" + H, p, 1024, 4), ap("msk" + H, 0, 1024, 4))
+            tt(ap("ofm" + H), HI, ap("ofh" + H), A.min)
+            cp(ap("of2" + H), ap("ofm" + H))
+            K, AA, D = ap(PB, 0, 128), ap(PA, 0, 128), ap(PA, 128, 256)
+            lst = [(K, ap("one", p1=1), ap("cra", p1=1), True, False), (K, ap("one", p1=1), ap("crb", p1=1), False, False)]
+            if t == 0:
+                for b in range(2):
+                    lst.append((K, ap("r0", b, 256, 2, p1=64), blk("rm", 1 + 2 * h + b, p1=64), False, False))
+            else:
+                lst.append((K, ein, blk("rm", 0, p1=48), False, False))
+            mm(lst)
+            tt(ap("gm" + H), ind(ap("xt"), ap("of2" + H)), ap("msk" + H), A.mult)
+            mm([(ap(PA, e, 128, 8), ap("gm" + H, e, 1024, 8), ap("bo2"), True, True) for e in range(8)])
+            act(ap("af" + H), AA)
+            act(ap("cst" + H), AA, bias=159.5 + 2.0 ** -13, scale=2.0 ** -12)
+            mm([(ap(PB, u, 128, 2), ap("ids"), blk("af" + H, u, 64), False, False) for u in range(2)])
+            mm([(ap(PB, u, 128, 2), ap("idk"), blk("cst" + H, u, 64), False, u == 1) for u in range(2)])
+            mm([(ap(PA, 128 + u, 256, 2), (idf, ap("idm"))[z], blk(("af", "cst")[z] + H, u, 64), z == 0, z == 1)
+                for u in range(2) for z in range(2)])
+            act(ap("ds" + H), D, bias=160.0 * 4096)
+            for p in [3, 2, 1, 0]:
+                w = (16 * p, 16 * p + 16)
+                scan(blk("so" + H, p), ap("z8"), K, A.add, A.min)
+                ts(ap("mall" + H, *w), ap("so" + H, 128 * p + 7, 128 * p + 128, 8), 2.0 ** 24, A.mult, 2.0 ** 24 - 1, A.min)
+                ts(ap("sall" + H, *w), ap("mall" + H, *w), 4095, an)
+                if p:
+                    tt(ap("eq" + H), ind(ap("sall" + H, *w), L1), ap("ds" + H), A.is_equal)
+                    tt(K, K, ap("eq" + H), A.max)
+            cp(ap("z2" + H, 8, 136), ind(ap("sall" + H), L3))
+            mm([(ap(PB, 256, 320), ap("z2" + H, 8 - 8 * x, 136 - 8 * x), ap("idf", x, 128, 2), x == 0, x == 1) for x in range(2)])
+            oo, eo = blk("offo", s + 1, 64), blk("eo", s)
+            cp(oo, ap(PB, 256, 320))
+            act(ap("xq" + H), ap("so" + H, 7, 512, 8), bias=135.5 + 2.0 ** -16, scale=512.0)
+            act(ap("hh" + H), ap("xq" + H, 0, 48), bias=-712.0)
+            mm([(ap(PA, 384, 432), ap("idn"), ap("xq" + H, 0, 48), True, False)]
+               + [(ap(PA, 384 + 16 * p, 400 + 16 * p), idb, ap("xq" + H, 48, 64), False, p == 2) for p in range(3)])
+            tt(ap("nrc" + H, 0, 48), ap(PA, 384, 432), ap("hh" + H), A.max)
+            mm([(ap(PA, 256, 384), ap("nrc" + H), idb, True, True)])
+            act(eo, ap(PA, 256, 384))
+            if t < NV - 1:
+                oa = ap("offo", 64 * s, 64 * s + 128)
+                di, de = blk("offi", s), blk("ei", s)
+
+                def send(oa=oa, eo=eo, di=di, de=de, s=s):
+                    g.remote_dma_fused([
+                        RemoteDMATransfer(dst_ids=[dst(nxt)], dma_engine_mask=emask(nxt, k, 2)[0], remote_sem=T.sem["ar%d" % s],
+                                          src=R((oa, eo)[k]), dst=R((di, de)[k])) for k in range(2)], local_sem=T.sem.sent)
+                n = 2 * emask(nxt, 0, 2)[1]
+                op("G", send, [oa, eo], [di, de], 700, dma=("ar%d" % s, n), lat=NET)
+                sent[0] += n
+            e48 = blk("eo", s, p1=48)
+            wb = [ap("pw0", 0, 256), ap("pw1", 0, 256), ap("pw0", 256, 512)]
+            act(ap("pg" + H), ind(ap("payr"), oo))
+            own = T.cores[(rank - t) % nr]
+            land = blk("smi", s - 2, 512)
+            r = 16 * (t + 1) % 128
+            turn = ap("idf", r, r + 128)
+            if FOLD:
+                xs = [blk("smo", 4 * s + p, 256) for p in range(4)]
+                act(xs[3], ap("pg" + H, 3, 1024, 4))
+                for p in range(3):
+                    c = wb[p]
+                    mm([(ap(c[0], c[1] + b, c[2], 2), blk("sel", 2 * p + b, p1=48), e48, True, True) for b in range(2)])
+                act(ap("pw0"), ap("pw0"), F.Exp, scale=-0.125)
+                act(wb[1], wb[1], F.Exp, scale=-0.125)
+                for p in (0, 2, 1):
+                    tt(xs[p], wb[p], ap("pg" + H, p, 1024, 4), A.mult)
+                if t:
+                    def home(xs=xs, land=land, own=own, s=s):
+                        g.remote_dma_fused([
+                            RemoteDMATransfer(dst_ids=[dst(own)], dma_engine_mask=emask(own, k, 2)[0], remote_sem=T.sem["sm%d" % (s - 2)],
+                                              srcs=[R(x) for x in xs], dst=R(blk("smi", 2 * (s - 2) + k, 256)), alu_op=1 + k)
+                            for k in range(2)], local_sem=T.sem.sent)
+                    n = 2 * emask(own, 0, 2)[1]
+                    op("G", home, xs, [land], 700, dma=("sm%d" % (s - 2), n), lat=NET + 3000)
+                    sent[0] += n
+                    mm([(ap("py" + H), turn, land, t == 1, t == NV - 1)])
+                    if t == 1:
+                        mm(late[h])
+                else:
+                    mx = [blk("smo", 48 + 2 * h + k, 256) for k in range(2)]
+                    tt(mx[0], xs[0], xs[1], A.max)
+                    tt(mx[1], xs[2], xs[3], A.max)
+                    tt(mx[0], mx[0], mx[1], A.max)
+                    late[h] = ([(ap("py" + H, 0, 256), turn, x, False, False) for x in xs]
+                               + [(ap("py" + H, 256, 512), turn, mx[0], False, False)])
+            else:
+                for p in (1, 3, 2):
+                    c = wb[p - 1]
+                    mm([(ap(c[0], c[1] + b, c[2], 2), blk("sel", 8 + 2 * (p - 1) + b, p1=48), e48, True, True) for b in range(2)])
+                for p in (1, 3, 2):
+                    act(ap("rho" + H, p, 1024, 4), wb[p - 1], F.Exp, scale=0.125)
+                for (nm, o1, at) in (("os_", A.add, 0), ("om_", A.max, 1)):
+                    for c in range(1024 // PC):
+                        scan(blk(nm + H, c, PC), blk("rho" + H, c, PC), blk("pg" + H, c, PC), A.mult, o1)
+                    act(blk("smo", 2 * s + at, 256), ap(nm + H, 3, 1024, 4))
+                src = blk("smo", s, 512)
+                if t:
+                    def home(src=src, land=land, own=own, s=s):
+                        a = topo.addr(own)
+                        g.remote_dma(R(land), R(src), T.sem["sm%d" % (s - 2)], T.sem.sent, a[1], a[0], emask(own, 0, 1)[0])
+                    n = emask(own, 0, 1)[1]
+                    op("G", home, [src], [land], 700, dma=("sm%d" % (s - 2), n), lat=NET + 500)
+                    sent[0] += n
+                    src = land
+                mm([(ap("py" + H), turn, src, t == 0, t == NV - 1)])
+    for h in range(2):
+        cur[0] = h
+        for k, o in enumerate((T.ys, T.ym)):
+            a = blk("yo", 2 * h + k, 256)
+            cp(a, blk("py%d" % h, k, 256))
+
+            def store(o=o, a=a, h=h):
+                g.sync.dma_start(o[:, 256 * h:256 * h + 256], R(a)).then_inc(T.sem.stored, 16)
+            op("Y", store, [a], [], 60, dma=("stored", 64), lat=2500)
+    return ops, q, sent[0]
+
+
+def link(ops):
+    wr = {n: np.full(v[1][1], -1) for n, v in SCRATCH.items()}
+    rd = {n: [] for n in SCRATCH}
+    bank = {n: {} for n, v in SCRATCH.items() if v[0] == "psum"}
+    for i, o in enumerate(ops):
+        d = set()
+        for a in o["rd"] + o["wr"]:
+            d.update(int(x) for x in np.unique(wr[a[0]][a[1]:a[2]:a[3]]) if x >= 0)
+            if a[0] in bank:
+                d.update(j for e, j in bank[a[0]].items() if e != o["eng"] or e == "P")
+        for a in o["wr"]:
+            cols = set(range(a[1], a[2], a[3]))
+            d.update(j for (j, c) in rd[a[0]] if not cols.isdisjoint(c))
+            rd[a[0]] = [(j, c - cols) for (j, c) in rd[a[0]] if c - cols]
+        for a in o["rd"]:
+            rd[a[0]].append((i, set(range(a[1], a[2], a[3]))))
+        for a in o["wr"]:
+            wr[a[0]][a[1]:a[2]:a[3]] = i
+        for a in o["rd"] + o["wr"]:
+            if a[0] in bank:
+                bank[a[0]][o["eng"]] = i
+        d.discard(i)
+        o["deps"] = sorted(d)
+
+
+KEPT = {}
+
+
+def order(ops, tries=TRIES):
+    n = len(ops)
+    kids = [[] for _ in ops]
+    for i, o in enumerate(ops):
+        for j in o["deps"]:
+            kids[j].append(i)
+    eng = [o["eng"] for o in ops]
+    dur = [o["dur"] for o in ops]
+    lat = [o["dur"] + o.get("lat", HOP) for o in ops]
+    tail = [0.0] * n
+    for i in range(n - 1, -1, -1):
+        tail[i] = lat[i] + max([tail[k] for k in kids[i]], default=0.0)
+    fixed = [1e7 - 1e3 * i if eng[i] == "Y" else 0.0 for i in range(n)]
+
+    def run(pri, slack):
+        left = [len(o["deps"]) for o in ops]
+        rdy = [0.0] * n
+        ready = {e: [] for e in "VSPGY"}
+        for i in range(n):
+            if not left[i]:
+                ready[eng[i]].append(i)
+        free, seq, at, end = {e: 0.0 for e in ready}, [], [0.0] * n, 0.0
+        for _ in range(n):
+            t0, e = min((max(free[e], min([rdy[i] for i in r])), e) for e, r in ready.items() if r)
+            r = ready[e]
+            i = max([j for j in r if rdy[j] <= t0], key=pri.get)
+            lim = t0 + min(slack, 0.5 * dur[i])
+            soon = [j for j in r if t0 < rdy[j] <= lim and pri[j] > pri[i]]
+            if soon:
+                i = max(soon, key=pri.get)
+            r.remove(i)
+            seq.append(i)
+            a = at[i] = max(t0, rdy[i])
+            free[e] = a + dur[i]
+            end = max(end, a + lat[i])
+            for k in kids[i]:
+                rdy[k] = max(rdy[k], a + (dur[i] if e == "P" and eng[k] == "P" else lat[i]))
+                left[k] -= 1
+                if not left[k]:
+                    ready[eng[k]].append(k)
+        return end, seq, at
+
+    if "best" not in KEPT:
+        rng = np.random.default_rng(7)
+        best = None
+        for lag in (0.0, 4000.0, 8000.0, 12000.0):
+            for slack in (0.0, 130.0, 300.0, 600.0):
+                pri = {i: tail[i] + fixed[i] - (lag if ops[i]["half"] == 1 else 0.0) for i in range(n)}
+                got = run(pri, slack)
+                if best is None or got[0] < best[0][0]:
+                    best = (got, pri, slack)
+        for trial in range(tries):
+            got, pri, slack = best
+            t = rng.random() * got[0]
+            new = dict(pri)
+            span, amp = rng.choice([2000.0, 6000.0, 15000.0]), rng.choice([300.0, 1500.0, 6000.0])
+            shift = {0: rng.normal() * amp, 1: 0.0, None: 0.0}
+            for i in range(n):
+                if t <= got[2][i] < t + span:
+                    new[i] += shift[ops[i]["half"]] + rng.normal() * amp * 0.3
+            tried = run(new, slack)
+            if tried[0] <= got[0]:
+                best = (tried, new, slack)
+        KEPT["best"] = best[0]
+    end, seq, at = KEPT["best"]
+    for i in range(n):
+        ops[i]["at"] = at[i]
+    return seq, end
+
+
+def rank_program(g, core, T, topo):
+    rank = T.rank_of(core)
+    if rank is None:
+        return
+    ops, q, sent = build(g, T, topo, rank)
+    link(ops)
+    seq, _ = order(ops)
+    used = set()
+    for o in ops:
+        used.update(j for j in o["deps"] if not (o["eng"] == "P" and ops[j]["eng"] == "P"))
+    count, seen = {}, {e: {} for e in q}
+    for i in seq:
+        o = ops[i]
+        e = o["eng"]
+        know = seen[e]
+        need = {}
+        for j in o["deps"]:
+            if e == "P" and ops[j]["eng"] == "P":
+                continue
+            sem, val = ops[j]["sig"]
+            if know.get(sem, 0) < val and need.get(sem, (0, 0))[0] < val:
+                need[sem] = (val, j)
+        for sem, (val, j) in sorted(need.items(), key=lambda kv: -ops[kv[1][1]]["at"]):
+            if know.get(sem, 0) < val:
+                q[e].wait_ge(T.sem[sem], val)
+                know[sem] = val
+                for s2, v2 in ops[j]["knew"].items():
+                    if know.get(s2, 0) < v2:
+                        know[s2] = v2
+        h = o["fn"]()
+        o["knew"] = dict(know)
+        if "dma" in o:
+            o["sig"] = o["dma"]
+            if e == "G":
+                o["knew"] = {}
+        elif i in used:
+            count["c" + e] = count.get("c" + e, 0) + 1
+            h.then_inc(T.sem["c" + e], 1)
+            o["sig"] = ("c" + e, count["c" + e])
+    for sem, val in sorted(count.items()):
+        g.wait_ge(T.sem[sem], val)
+    g.wait_ge(T.sem.sent, sent)
+    g.sync.wait_ge(T.sem.stored, 64)

@@ -4,13 +4,15 @@ from concourse.mybir import AluOpType as A
 from concourse.mybir import ActivationFunctionType as F
 
 NV = 6
-MCV = 24
+MCV = 32
 MSV = 2
-FOLD = False
+FOLD = True
 CH = [0, 512, 1536, 2816, 3840, 4096]
 SW = [(0, 1536), (1536, 2816), (2816, 4096)]
 PC = 256
-TRIES = 1500
+GMC = 2
+PGC = 2
+TRIES = 2500
 SCRATCH = {}
 
 
@@ -48,10 +50,10 @@ for _n in ["pa0", "pb0", "pa1", "pb1", "pw0", "pw1", "py0", "py1"]:
     _sb(_n, 512, "float32", "psum")
 
 SEMAPHORES = (["cV", "cS", "cP", "cG", "sent", "stored"] + ["ld%d" % i for i in range(10)] + ["sw%d" % i for i in range(2 * len(SW))]
-              + ["ar%d" % i for i in range(10)] + ["sm%d" % i for i in range(10)])
+              + ["ar%d" % i for i in range(10)] + ["er%d" % i for i in range(10)] + ["sm%d" % i for i in range(10)])
 
-CY, PCY = 1.0, 0.5
-HOP, NET, GA = 120.0, 3000.0, 1.5
+CY, PCY = 0.92, 0.5
+HOP, NET, GA = 160.0, 3300.0, 1.5
 
 
 def ap(b, c0=0, c1=None, st=1, p0=0, p1=128):
@@ -227,7 +229,6 @@ def build(g, T, topo, rank):
     act(ap("z16", 0, 256, 16), ap("onef", 0, 16), scale=1000.0)
     act(ap("z8"), ap("onef", 0, 128), scale=0.0)
     act(ap("z8", 0, 128, 8), ap("onef", 0, 16), scale=2.0)
-    ms(ap("offo", 0, 64), 0)
     for h in "01":
         if not FOLD:
             act(ap("rho" + h, 0, 1024, 4), ap("onef"), scale=0.0)
@@ -332,7 +333,8 @@ def build(g, T, topo, rank):
             else:
                 lst.append((K, ein, blk("rm", 0, p1=48), False, False))
             mm(lst)
-            tt(ap("gm" + H), ind(ap("xt"), ap("of2" + H)), ap("msk" + H), A.mult)
+            for c in range(GMC):
+                tt(blk("gm" + H, c, 1024 // GMC), ind(ap("xt"), blk("of2" + H, c, 64 // GMC)), blk("msk" + H, c, 1024 // GMC), A.mult)
             mm([(ap(PA, e, 128, 8), ap("gm" + H, e, 1024, 8), ap("bo2"), True, True) for e in range(8)])
             act(ap("af" + H), AA)
             act(ap("cst" + H), AA, bias=159.5 + 2.0 ** -13, scale=2.0 ** -12)
@@ -361,19 +363,17 @@ def build(g, T, topo, rank):
             mm([(ap(PA, 256, 384), ap("nrc" + H), idb, True, True)])
             act(eo, ap(PA, 256, 384))
             if t < NV - 1:
-                oa = ap("offo", 64 * s, 64 * s + 128)
-                di, de = blk("offi", s), blk("ei", s)
-
-                def send(oa=oa, eo=eo, di=di, de=de, s=s):
-                    g.remote_dma_fused([
-                        RemoteDMATransfer(dst_ids=[dst(nxt)], dma_engine_mask=emask(nxt, k, 2)[0], remote_sem=T.sem["ar%d" % s],
-                                          src=R((oa, eo)[k]), dst=R((di, de)[k])) for k in range(2)], local_sem=T.sem.sent)
-                n = 2 * emask(nxt, 0, 2)[1]
-                op("G", send, [oa, eo], [di, de], 700, dma=("ar%d" % s, n), lat=NET)
-                sent[0] += n
+                for (src, to, sem) in ((oo, ap("offi", 128 * s + 64, 128 * s + 128), "ar%d" % s), (eo, blk("ei", s), "er%d" % s)):
+                    def send(src=src, to=to, sem=sem):
+                        a = topo.addr(nxt)
+                        g.remote_dma(R(to), R(src), T.sem[sem], T.sem.sent, a[1], a[0], emask(nxt, 0, 1)[0])
+                    n = emask(nxt, 0, 1)[1]
+                    op("G", send, [src], [to], 700, dma=(sem, n), lat=NET - 600)
+                    sent[0] += n
             e48 = blk("eo", s, p1=48)
             wb = [ap("pw0", 0, 256), ap("pw1", 0, 256), ap("pw0", 256, 512)]
-            act(ap("pg" + H), ind(ap("payr"), oo))
+            for c in range(PGC):
+                act(blk("pg" + H, c, 1024 // PGC), ind(ap("payr"), ap(oo[0], oo[1] + 64 // PGC * c, oo[1] + 64 // PGC * (c + 1))))
             own = T.cores[(rank - t) % nr]
             land = blk("smi", s - 2, 512)
             r = 16 * (t + 1) % 128
@@ -395,11 +395,15 @@ def build(g, T, topo, rank):
                                               srcs=[R(x) for x in xs], dst=R(blk("smi", 2 * (s - 2) + k, 256)), alu_op=1 + k)
                             for k in range(2)], local_sem=T.sem.sent)
                     n = 2 * emask(own, 0, 2)[1]
-                    op("G", home, xs, [land], 700, dma=("sm%d" % (s - 2), n), lat=NET + 3000)
+                    op("G", home, xs, [land], 3500, dma=("sm%d" % (s - 2), n), lat=NET)
                     sent[0] += n
-                    mm([(ap("py" + H), turn, land, t == 1, t == NV - 1)])
                     if t == 1:
-                        mm(late[h])
+                        mm([(ap("py" + H), turn, land, True, False)])
+                        for x in late[h]:
+                            mm([x])
+                    else:
+                        for k in range(2):
+                            mm([(blk("py" + H, k, 256), turn, ap("smi", land[1] + 256 * k, land[1] + 256 * k + 256), False, t == NV - 1 and k == 1)])
                 else:
                     mx = [blk("smo", 48 + 2 * h + k, 256) for k in range(2)]
                     tt(mx[0], xs[0], xs[1], A.max)
@@ -493,7 +497,7 @@ def order(ops, tries=TRIES):
             t0, e = min((max(free[e], min([rdy[i] for i in r])), e) for e, r in ready.items() if r)
             r = ready[e]
             i = max([j for j in r if rdy[j] <= t0], key=pri.get)
-            lim = t0 + min(slack, 0.5 * dur[i])
+            lim = t0 + (1.2 * dur[i] if e == "G" else min(slack, 0.5 * dur[i]))
             soon = [j for j in r if t0 < rdy[j] <= lim and pri[j] > pri[i]]
             if soon:
                 i = max(soon, key=pri.get)

@@ -4,64 +4,71 @@ from concourse.mybir import AluOpType as A
 from concourse.mybir import ActivationFunctionType as F
 
 NV = 6
-MCV = 32
-MSV = 2
-FOLD = True
+PARTS = 1
+MCE = "SVSS"
+CONV = [(0, 3)]
 CH = [0, 512, 1536, 2816, 3840, 4096]
 SW = [(0, 1536), (1536, 2816), (2816, 4096)]
-PC = 256
-GMC = 2
-PGC = 2
 TRIES = 2500
 SCRATCH = {}
+GONE = 106.0
+TOP = 3584.0
+NONE = TOP - (16 * 176 + 2047.0 / 4096)
+ROUND2 = 1.5 * 2 ** 24
 
 
 def _sb(n, w, d, where="sbuf"):
-    SCRATCH[n] = (where, [128, w], d)
+    SCRATCH[n] = (where, [128] + (list(w) if isinstance(w, tuple) else [w]), d)
 
 
 for _n, _w, _d in [
         ("arc", 4096, "int32"), ("xt", 8192, "int32"), ("mn", 4096, "float32"),
         ("mc", 4096, "bfloat16"), ("payr", 4096, "bfloat16"), ("acs", 512, "float32"), ("act", 512, "float32"),
-        ("sti", 128, "int32"), ("stf", 128, "float32"), ("off0", 128, "uint16"), ("rsi", 256, "int32"), ("r0", 256, "bfloat16"),
-        ("ci", 32, "int32"), ("cf", 40, "float32"), ("cm", 16, "float32"), ("i8", 16, "float32"),
-        ("colg", 128, "float32"), ("colk", 128, "float32"), ("coln", 132, "float32"), ("colf", 128, "float32"), ("colq", 128, "float32"),
-        ("one", 128, "bfloat16"), ("onef", 256, "float32"), ("pm", 4 * 132, "float32"), ("lm", 128, "bfloat16"), ("him", 512, "bfloat16"),
-        ("idb", 128, "bfloat16"), ("idn", 128, "bfloat16"), ("idf", 256, "float32"), ("ids", 128, "float32"),
-        ("idm", 128, "bfloat16"), ("idk", 128, "bfloat16"), ("bo64", 128, "bfloat16"), ("bo128", 128, "bfloat16"), ("bo2", 16, "float32"),
-        ("sel", 14 * 128, "bfloat16"), ("rm", 5 * 128, "bfloat16"),
-        ("cra", 128, "bfloat16"), ("crb", 128, "bfloat16"), ("lf", 24, "float32"), ("lu", 16, "uint16"),
-        ("z16", 256, "float32"), ("z8", 128, "float32"),
-        ("offo", 13 * 64, "uint16"), ("eo", 12 * 128, "bfloat16"), ("offi", 10 * 128, "uint16"), ("ei", 10 * 128, "bfloat16"),
-        ("smo", (12 * 1024 + 1024) if FOLD else 12 * 512, "float32"), ("smi", 10 * 512, "float32"), ("yo", 1024, "float32")]:
+        ("sti", (4, 32), "int32"), ("off0", 128, "uint16"), ("rsi", 256, "int32"), ("r0", 256, "bfloat16"),
+        ("ci", 48, "int32"), ("cf", 16, "float32"), ("i16", 16, "float32"),
+        ("onef", 256, "float32"), ("one", 128, "bfloat16"), ("idf", 256, "float32"), ("idb", 128, "bfloat16"),
+        ("idq", 128, "float16"), ("idn", 128, "bfloat16"), ("i15", 128, "bfloat16"), ("ids", 128, "float32"),
+        ("bo2", 16, "float32"), ("lm", 128, "bfloat16"), ("hsel", 512, "bfloat16"), ("sel0", 1024, "bfloat16"), ("sel", 768, "bfloat16"),
+        ("ua", 128, "bfloat16"), ("ub", 128, "bfloat16"), ("uc", 128, "bfloat16"), ("ud", 128, "bfloat16"),
+        ("rm0", 128, "bfloat16"), ("rm", 128, "bfloat16"), ("ca", 128, "bfloat16"),
+        ("lu", 32, "uint16"), ("z16", 256, "float32"), ("z8", 128, "float32"),
+        ("mo", 12 * 64, "uint16"), ("mi", 10 * 64, "uint16"), ("ro", 12 * 256, "bfloat16"), ("ri", 10 * 256, "bfloat16"),
+        ("smo", 12 * 1024, "float32"), ("smi", 10 * 512, "float32"), ("yo", 1024, "float32")]:
     _sb(_n, _w, _d)
 for _h in "01":
     for _n, _w, _d in [
             ("mcg", 1024, "bfloat16"), ("c0s", 256, "bfloat16"), ("m1", 256, "bfloat16"), ("m2", 256, "bfloat16"),
-            ("m3", 256, "bfloat16"), ("sc", 256, "float32"), ("nwt", 256, "bfloat16"), ("nwl", 256, "bfloat16"),
-            ("msk", 1024, "bfloat16"), ("gm", 1024, "float32"), ("cst", 128, "bfloat16"),
-            ("ofl", 64, "float32"), ("ofh", 64, "float32"), ("ofm", 64, "float32"), ("of2", 64, "uint16"),
-            ("ds", 128, "float32"), ("af", 128, "float32"), ("so", 512, "float32"), ("eq", 128, "bfloat16"), ("mall", 64, "int32"),
-            ("sall", 72, "int32"), ("xq", 64, "bfloat16"), ("hh", 48, "float32"),
-            ("nrc", 128, "bfloat16"), ("z2", 136, "float32"), ("pg", 1024, "bfloat16")] + ([] if FOLD else [
-            ("rho", 1024, "float32"), ("os_", 1024, "float32"), ("om_", 1024, "float32")]):
+            ("m3", 256, "bfloat16"), ("rr", 256, "float32"), ("ff", 256, "bfloat16"), ("ft", 256, "bfloat16"),
+            ("msk", 256, "bfloat16"), ("gm", 1024, "float32"), ("cst", 128, "bfloat16"), ("zh", 144, "bfloat16"),
+            ("ofl", 64, "float32"), ("of2", 64, "uint16"), ("ds", 128, "float32"), ("so", 512, "float32"), ("eq", 128, "bfloat16"),
+            ("fl", 64, "float32"), ("sall", (3, 16), "float32"), ("zl", 528, "float16"),
+            ("xq", 128, "bfloat16"), ("x0", 128, "bfloat16"), ("af", 128, "float32"), ("loc", 512, "float32")]:
         _sb(_n + _h, _w, _d)
 for _n in ["pa0", "pb0", "pa1", "pb1", "pw0", "pw1", "py0", "py1"]:
     _sb(_n, 512, "float32", "psum")
 
 SEMAPHORES = (["cV", "cS", "cP", "cG", "sent", "stored"] + ["ld%d" % i for i in range(10)] + ["sw%d" % i for i in range(2 * len(SW))]
-              + ["ar%d" % i for i in range(10)] + ["er%d" % i for i in range(10)] + ["sm%d" % i for i in range(10)])
+              + ["%s%d" % (n, i) for n in ("ar", "br", "er", "fr", "sm") for i in range(10)])
 
 CY, PCY = 0.92, 0.5
 HOP, NET, GA = 160.0, 3300.0, 1.5
 
 
 def ap(b, c0=0, c1=None, st=1, p0=0, p1=128):
-    return (b, c0, SCRATCH[b][1][1] if c1 is None else c1, st, p0, p1)
+    return (b, (slice(c0, SCRATCH[b][1][1] if c1 is None else c1, st),), p0, p1)
+
+
+def apx(b, *idx):
+    return (b, idx, 0, 128)
+
+
+def cols(a):
+    s = SCRATCH[a[0]][1][1:]
+    return np.arange(int(np.prod(s))).reshape(s)[a[1]].reshape(-1)
 
 
 def ncol(a):
-    return len(range(a[1], a[2], a[3]))
+    return len(cols(a))
 
 
 def build(g, T, topo, rank):
@@ -73,9 +80,8 @@ def build(g, T, topo, rank):
             return a
         if a[0] == "ind":
             return R(a[1]).indirect(R(a[2]))
-        if a[3] == 1:
-            return T[a[0]][a[4]:a[5], a[1]:a[2]]
-        return T[a[0]][a[4]:a[5], a[1]:a[2]:a[3]]
+        idx = tuple(slice(x.start, x.stop) if isinstance(x, slice) and x.step == 1 else x for x in a[1])
+        return T[a[0]][(slice(a[2], a[3]),) + idx]
 
     def op(eng, fn, rd, wr, dur, **kw):
         flat = []
@@ -88,7 +94,7 @@ def build(g, T, topo, rank):
         n = ncol(out)
         if ins and ins[0][0] == "ind":
             return 60 + n * GA * CY
-        c = 0.5 if all(SCRATCH[a[0]][2] in ("bfloat16", "uint16") for a in [out] + ins) else 1.0
+        c = 0.5 if all(SCRATCH[a[0]][2] in ("bfloat16", "uint16", "float16") for a in [out] + ins) else 1.0
         if tt and not any(SCRATCH[a[0]][0] == "psum" for a in ins):
             c *= 2
         return 30 + max(64, n * c) * CY
@@ -109,8 +115,8 @@ def build(g, T, topo, rank):
     def ms(out, v):
         op("V", lambda: g.vector.memset(R(out), v), [], [out], vdur(out, []))
 
-    def scan(out, d0, d1, o0, o1):
-        op("V", lambda: g.vector.tensor_tensor_scan(R(out), R(d0), R(d1), 0.0, o0, o1), [d0, d1], [out], vdur(out, [d0, d1]))
+    def scan(out, d0, d1, o0, o1, first=0.0):
+        op("V", lambda: g.vector.tensor_tensor_scan(R(out), R(d0), R(d1), first, o0, o1), [d0, d1], [out], vdur(out, [d0, d1]))
 
     def act(out, i0, f=F.Identity, bias=0.0, scale=1.0):
         d = 100 + ncol(out) * CY * (GA if i0[0] == "ind" else 1)
@@ -132,10 +138,13 @@ def build(g, T, topo, rank):
             fn = lambda: g.iota(R(out), pat, base, cmul)
         else:
             fn = lambda: g.iota(R(out), pat, base, cmul, allow_small_or_imprecise_dtypes=True)
-        op("G", fn, [], [out], 150 + 2 * ncol(out) * CY)
+        op("G", fn, [], [out], 130 + 2 * ncol(out) * CY)
 
-    def asel(out, i0, pat, o, base, cmul):
-        op("G", lambda: g.affine_select(R(out), R(i0), pat, o, 0.0, base, cmul), [i0], [out], 200 + 2 * ncol(out) * CY)
+    def asel(out, i0, pat, o, base, cmul, fill=0.0):
+        op("G", lambda: g.affine_select(R(out), R(i0), pat, o, fill, base, cmul), [i0], [out], 170 + 2 * ncol(out) * CY)
+
+    def paint(x, pat, base, v):
+        asel(x, x, pat, A.not_equal, base, -1, v)
 
     def load(sem, pairs, wr, lat, rd=()):
         def fn():
@@ -145,97 +154,77 @@ def build(g, T, topo, rank):
 
     ind = lambda w, o: ("ind", w, o)
     col = lambda j: ap("cf", j, j + 1)
-    blk = lambda n, j, w=128, p1=128: ap(n, w * j, w * j + w, p1=p1)
+    blk = lambda n, j, w=128, p0=0, p1=128: ap(n, w * j, w * j + w, p0=p0, p1=p1)
+    every = slice(None)
 
     for i in range(len(CH) - 1):
         load("ld%d" % i, [(T.arc[:, CH[i]:CH[i + 1]], T.arcs[:, CH[i]:CH[i + 1]])], [ap("arc", CH[i], CH[i + 1])], 2200 + 2.2 * CH[i + 1])
-    load("ld7", [(T.sti[:], T.st0[:])] + [(T.rsi[16 * p:16 * p + 16, :], T.rs0[:, (3 - p) * 512:(4 - p) * 512]) for p in range(4)],
-         [ap("sti"), ap("rsi")], 12000)
+    load("ld7", [(T.sti[:], T.st0[:])] + [(T.rsi[8 * j:8 * j + 8, :], T.rs0[:, 256 * j:256 * j + 256]) for j in range(8)],
+         [apx("sti", every, every), ap("rsi")], 12000)
     load("ld6", [(T.acs[:], T.ac[:])], [ap("acs")], 12500)
 
-    iota(ap("ci", 0, 9), [[2, 9]], 0, 1)
-    iota(ap("i8"), [[1, 16]], 0, 0)
-    iota(ap("colg"), [[1, 8], [0, 16]], 0, 0)
-    iota(ap("colk"), [[1, 64], [0, 2]], 0, 0)
-    iota(ap("coln"), [[1, 132]], 0, 0)
-    iota(ap("colf"), [[8, 8], [0, 2], [1, 8]], 0, 0)
-    iota(ap("colq"), [[1, 32], [0, 4]], 0, 0)
-    iota(ap("crb"), [[0, 16], [-1, 4], [4, 2]], 3, 0)
-    iota(ap("lf", 0, 8), [[2, 8]], 0, 0)
     ms(ap("onef"), 1.0)
-    act(ap("one"), ap("onef", 0, 128))
-    asel(ap("idf", 0, 128), ap("onef", 0, 128), [[-1, 128]], A.is_equal, 0, 1)
-    act(ap("idf", 128, 256), ap("idf", 0, 128))
-    sh, an = A.logical_shift_right, A.bitwise_and
-    for j, (src, s, m) in enumerate([(0, 1, 7), (0, 4, 7), (0, 0, 1), (0, 0, 15), (0, 0, 3), (0, 2, 1), (0, 3, 1), (1, 1, 7), (8, 4, 7),
-                                     (0, 0, 7), (0, 2, 3), (0, 1, 1)]):
-        ts(ap("ci", 16 + j, 17 + j), ap("ci", src, src + 1), s, sh, m, an)
-    cp(ap("cf", 0, 12), ap("ci", 16, 28))
-    G1, P4, B1, Q15, Q3, Q2, Q8, G1R, G4R, Q7, Q23, B2 = [col(j) for j in range(12)]
-    lin = lambda j, a, m, b: act(col(j), a, scale=m, bias=b)
-    lin(12, P4, 2.0, B1)
-    lin(13, G1R, 8.0, P4)
-    lin(14, col(13), 1.0, 4.0)
-    lin(15, B1, 4.0, col(13))
-    lin(16, B1, 2.0 ** -9, -2.0 ** -9)
-    lin(17, B1, -2.0 ** -9, 0.0)
-    ts(col(18), Q15, 0.0, A.is_equal)
-    lin(19, col(18), -1.0, 1.0)
-    lin(20, Q3, 16.0, Q2)
-    lin(21, Q8, -1.0, 1.0)
-    lin(22, Q8, 64.0, 0.0)
-    lin(23, Q8, 8.0, G4R)
-    lin(24, P4, 8.0, Q7)
-    lin(25, Q8, 4096.0, 0.0)
-    lin(26, P4, 4.0, 0.0)
-    act(ap("cf", 28, 32), ap("i8", 0, 4), bias=col(26))
-    lin(27, col(26), 1.0, Q3)
-    lin(32, col(27), 4.0, 3.0)
-    for j, (b, m) in enumerate([(B1, 1.0), (B2, 3.0), (Q2, 15.0), (Q8, 255.0)]):
-        lin(33 + j, b, m, 1.0)
-    lin(37, col(33), col(34), 0.0)
-    lin(38, col(35), col(36), 0.0)
-    lin(39, col(37), col(38), 0.0)
-    ts(ap("cm", 0, 8), ap("i8", 0, 8), col(12), A.is_equal, -1.0, A.mult)
-    ts(ap("bo64"), ap("colg"), G1, A.is_equal)
-    ts(ap("bo128"), ap("colg"), P4, A.is_equal)
-    ts(ap("bo2"), ap("i8"), col(23), A.is_equal)
-    ts(ap("lm"), ap("colf"), col(24), A.is_equal, 2.0, A.mult)
-    tt(ap("lm"), ap("lm"), ap("bo128"), A.subtract)
-    act(ap("lm"), ap("lm"), scale=col(39))
-    ts(ap("lf", 20, 24), ap("i8", 0, 4), Q23, A.is_equal)
-    for v in range(4):
-        ts(blk("him", v), ap("colq"), col(28 + v), A.is_equal, col(25), A.mult)
-        ts(blk("pm", v, 132), ap("coln"), col(32), A.is_equal, ap("lf", 20 + v, 21 + v), A.mult)
-    if not FOLD:
-        tt(ap("cm", 8, 14), ap("cm", 2, 8), ap("cm", 0, 6), A.subtract)
-    for j in range(8 if FOLD else 14):
-        act(blk("sel", j), ap("bo64"), scale=ap("cm", j, j + 1))
     idf, idb = ap("idf", 0, 128), ap("idb")
-    for n, v in (("idb", 1.0), ("idn", -1.0), ("idm", -4096.0), ("idk", 7 * 2.0 ** -12), ("ids", 2.0 ** -24)):
+    asel(idf, ap("onef", 0, 128), [[-1, 128]], A.is_equal, 0, 1)
+    for n in ("sel0", "hsel", "zl0", "zl1"):
+        ms(ap(n), 0.0)
+    for n in ("ua", "ub", "ff0", "ff1", "zh0", "zh1", "xq0", "xq1", "x00", "x01"):
+        act(ap(n), ap("onef", 0, SCRATCH[n][1][1]), scale=0.0)
+    iota(ap("ci", 0, 2), [[16, 2]], 0, 1)
+    iota(ap("ci", 8, 16), [[2, 8]], 0, 0)
+    iota(ap("i16"), [[1, 16]], 0, 0)
+    paint(ap("sel0"), [[1, 64], [0, 16]], 0, 1.0)
+    act(ap("one"), ap("onef", 0, 128))
+    act(ap("idf", 128, 256), idf)
+    for n, v in (("idb", 1.0), ("i15", -15.0), ("idn", -1.0), ("ids", -1.0)):
         act(ap(n), idf, scale=v)
-    act(ap("crb"), ap("crb"), scale=2.0 ** -12)
-    act(ap("cra"), ap("one"), scale=-35.0 / 128)
-    ts(blk("rm", 0), ap("colk"), col(15), A.is_equal, -2.0 ** -9, A.mult)
-    for h in range(2):
-        for b in range(2):
-            ts(blk("rm", 1 + 2 * h + b), ap("colk"), col(13 + b), A.is_equal, col(16 + h), A.mult)
-    act(ap("lf", 8, 16), ap("lf", 0, 8), bias=col(20))
-    act(ap("lf", 8, 16), ap("lf", 8, 16), scale=col(21), bias=col(22))
-    act(ap("lf", 0, 8), ap("lf", 0, 8), bias=Q8)
-    cp(ap("lu"), ap("lf", 0, 16))
-    L1, L3 = ap("lu", 0, 8), ap("lu", 8, 16)
+    ts(ap("idq"), idf, -4096.0, A.mult)
+    sh, an = A.logical_shift_right, A.bitwise_and
+    ts(ap("ci", 2, 3), ap("ci", 1, 2), 3, sh, 15, an)
+    ts(ap("ci", 3, 4), ap("ci", 0, 1), 3, sh, 1, an)
+    ts(ap("ci", 4, 5), ap("ci", 0, 1), 4, sh)
+    ts(ap("ci", 5, 6), ap("ci", 0, 1), 15, an)
+    cp(ap("cf", 0, 6), ap("ci", 0, 6))
+    PN, NEXT, Q8 = col(0), col(2), col(3)
+    ts(ap("bo2"), ap("i16"), NEXT, A.is_equal, 2.0 ** -12, A.mult)
+    ts(ap("lu", 0, 8), ap("ci", 8, 16), Q8, A.add)
+    L1 = ap("lu", 0, 8)
+    act(col(10), PN, scale=-160.5, bias=160.0)
+    act(ap("ca", p1=2), ap("onef", 0, 128, p1=2), scale=ap("cf", 10, 11, p1=2))
     act(ap("z16"), ap("onef"), scale=0.0)
     act(ap("z16", 0, 256, 16), ap("onef", 0, 16), scale=1000.0)
-    act(ap("z8"), ap("onef", 0, 128), scale=0.0)
-    act(ap("z8", 0, 128, 8), ap("onef", 0, 16), scale=2.0)
-    for h in "01":
-        if not FOLD:
-            act(ap("rho" + h, 0, 1024, 4), ap("onef"), scale=0.0)
-        act(ap("nwt" + h, 0, 1), ap("onef", 0, 1), scale=0.0)
-        act(ap("nrc" + h, 48, 128), ap("onef", 0, 80), scale=0.0)
-        act(ap("z2" + h, 0, 8), ap("onef", 0, 8), scale=0.0)
-        ms(ap("sall" + h, 64, 72), 0)
+    act(ap("z8"), ap("onef", 0, 128), scale=2 * TOP)
+    act(ap("z8", 0, 128, 8), ap("onef", 0, 16), scale=NONE)
+    iota(ap("lm"), [[1, 8], [0, 16]], 0, 0)
+    ts(ap("lm"), ap("lm"), col(4), A.is_equal, -1.0, A.mult)
+    for base in (0, 8):
+        paint(ap("lm"), [[16, 8], [0, 2], [1, 8]], base, 1.0)
+    act(col(6), col(5), F.Exp, scale=0.8)
+    act(ap("lm"), ap("lm"), scale=col(6))
+    ts(col(7), col(5), 0.0, A.is_equal)
+    act(col(8), col(7), scale=-1.0, bias=1.0)
+    paint(ap("hsel"), [[1, 8], [0, 4], [8, 16]], 0, 4096.0)
+    mend = (GONE - 64) / 2
+    bygroup, byrow = [[0, 2], [1, 8], [0, 8]], [[1, 16], [0, 2], [16, 4]]
+    for (n, base) in (("uc", 0), ("ud", -int(16 * mend))):
+        iota(ap(n), [[0, 16], [2, 8]], base, 0)
+        asel(ap(n), ap(n), bygroup, A.is_equal, 120, -1)
+        paint(ap(n), bygroup, 112, -(TOP + 2560))
+    act(ap("ud", 0, 128, 4), ap("uc", 0, 128, 4))
+    paint(ap("ua"), byrow, 0, -16.0)
+    paint(ap("ub"), byrow, -16, 16.0)
+    paint(ap("ub"), byrow, 48, 16 * mend)
+    paint(ap("ub"), bygroup, 48, -16.0)
+    act(ap("ub", 0, 128, 4), ap("onef", 0, 32), scale=0.0)
+    tt(ap("ub"), ap("ub"), ap("ud"), A.add)
+    for (n, u) in (("rm0", "ua"), ("rm", "ub")):
+        for b in range(2):
+            act(ap(n, 64 * b + 8, 64 * b + 64), ap(u, 64 * b, 64 * b + 56))
+            act(ap(n, 64 * b, 64 * b + 8), ap(u, 64 * b + 56, 64 * b + 64))
+    act(ap("sel"), ap("sel0", 0, 768), scale=-1.0)
+    paint(ap("sel"), [[1, 48], [0, 16]], 64, -mend)
+    paint(ap("sel"), [[0, 6], [1, 8], [0, 16]], 48, 1.0)
+    paint(ap("sel"), [[0, 6], [1, 8], [0, 16]], 112, mend)
     for i in range(len(CH) - 1):
         c = (CH[i], CH[i + 1])
         ts(ap("xt", *c), ap("arc", *c), 32767, an)
@@ -250,13 +239,10 @@ def build(g, T, topo, rank):
         load("sw%d" % (2 * i + 1), [(hi("xt", k, 0), lo("arc", k, 0)) for k in range(8)],
              [ap("xt", c0, c1)], 2200 + 1.1 * (c1 - c0), [ap("arc", c0, c1)])
     load("ld8", [(T.payr[16:128, :], T.pay[0:112, :]), (T.payr[0:16, :], T.pay[112:128, :])], [ap("payr")], 6000, [ap("mn", 2815, 2816)])
-    cp(ap("stf"), ap("sti"))
-    ts(ap("r0", p1=64), ap("rsi", p1=64), -1.0, A.mult)
+    ms(ap("r0", p0=64), -1.0)
+    cp(ap("r0", p1=64), ap("rsi", p1=64))
     for h in range(2):
-        bank = "pb%d" % h
-        mm([(ap(bank, c, 64, 4), ap("pm", 132 * c + 3 - p, 132 * c + 131 - p), ap("stf", 32 * (3 - p) + 16 * h, 32 * (3 - p) + 16 * h + 16),
-             p == 0, p == 3) for c in range(4) for p in range(4)])
-        cp(blk("off0", h, 64), ap(bank, 0, 64))
+        cp(blk("off0", h, 64), apx("sti", every, slice(16 * h, 16 * h + 16)))
         bank = "pa%d" % h
         for b in range(2):
             o, i = blk(bank, b), ap("acs", 256 * h + b, 256 * h + 256, 2)
@@ -275,195 +261,201 @@ def build(g, T, topo, rank):
         k = len(e) // of
         return int(sum(1 << x for x in e[part * k:part * k + k])), k
 
-    sent, late = [0], {}
+    sent = [0]
     for t in range(NV):
         for h in range(2):
             H = str(h)
             cur[0] = h
             PA, PB = "pa" + H, "pb" + H
             s = 2 * t + h
-            cbank = {2: ap(PA, 0, 256), 1: ap(PB, 0, 256), 0: ap(PA, 256, 512), 3: ap(PB, 256, 512)}
-            if t == 0:
-                of = blk("off0", h, 64)
-            else:
-                of = ap("offi", 128 * (s - 2) + 64, 128 * (s - 1))
-                ein = blk("ei", s - 2, p1=48)
-            act(ap("mcg" + H, 16 * MCV, 1024), ind(ap("mc"), ap(of[0], of[1] + MCV, of[2])), bias=-160.0)
-            if MCV:
-                ts(ap("mcg" + H, 0, 16 * MCV), ind(ap("mc"), ap(of[0], of[1], of[1] + MCV)), -160.0, A.add)
-            cp(ap("ofl" + H), of)
-            act(ap("ofh" + H), ap("ofl" + H), bias=4096.0)
-            last = ap("mcg" + H, 3, 1024, 4)
-            for p in ([3, 2, 1, 0] if t == 0 else [2, 1, 0]):
-                c = cbank[p]
-                lst = [(c, idb, ap("mcg" + H, p, 1024, 4), True, False)]
-                if t == 0:
-                    lst.append((c, blk("sel", 2 * p + h, p1=64), ap("r0", p1=64), False, True))
+            lb, l0 = ("off0", 64 * h) if t == 0 else ("mi", 64 * (s - 2))
+            SC = ap(PB, 256, 512)
+            for k in range(4):
+                i0 = ind(ap("mc"), ap(lb, l0 + 16 * k, l0 + 16 * k + 16))
+                if MCE[k] == "S":
+                    act(blk("mcg" + H, k, 256), i0, bias=-160.0)
                 else:
+                    ts(blk("mcg" + H, k, 256), i0, -160.0, A.add)
+            cp(ap("ofl" + H), ap(lb, l0, l0 + 64))
+            cbank = [ap("py" + H, 0, 256), ap(PA, 0, 256), ap(PB, 0, 256), ap(PA, 256, 512)]
+            last = blk("mcg" + H, 0, 256)
+            for k in range(1 if t else 0, 4):
+                c = cbank[k]
+                lst = [(c, idb, blk("mcg" + H, k, 256), True, False)]
+                if t == 0:
+                    lst.append((c, blk("sel0", 2 * k + h, p1=64), ap("r0", p1=64), False, True))
+                else:
+                    x = blk("ri", 2 * (s - 2) + (0 if PARTS == 2 and k < 3 else 1), p1=64)
                     for b in range(2):
-                        lst.append((ap(c[0], c[1] + b, c[2], 2), blk("sel", 2 * p + b, p1=48), ein, False, b == 1))
+                        lst.append((ap(c[0], c[1][0].start + b, c[1][0].stop, 2), blk("sel", 2 * k - 2 + b, p1=64), x, False, b == 1))
                 mm(lst)
-                if p == 3:
+                if k == 0:
                     last = ap("c0s" + H)
                     act(last, c)
                 else:
-                    tt(ap("m%d" % (3 - p) + H), c, last, A.min)
-                    last = ap("m%d" % (3 - p) + H)
-            mm([(blk(PB, 2 + b), ap("m3" + H, b, 256, 2), idb, True, True) for b in range(2)])
-            tt(ap("sc" + H), ap(PB, 256, 512), blk("act", h, 256), A.add)
-            scan(ap(PA, 0, 256), ap("z16"), ap("sc" + H), A.add, A.min)
-            tt(ap("nwt" + H, 1, 256), ap(PA, 0, 255), ap("sc" + H, 1, 256), A.is_gt)
-            mm([(ap(PB, b, 256, 2), blk("nwt" + H, b), idb, True, True) for b in range(2)])
-            act(ap("nwl" + H), ap(PB, 0, 256), scale=col(19), bias=col(18))
-            LL, HI = ap(PA, 256, 512), ap(PB, 256, 320)
-            mm([(LL, ap("lm"), ap("nwl" + H), True, True)])
-            mm([(HI, idf, ap("ofl" + H), True, False)]
-               + [(HI, blk("him", v), ap("nwl" + H, v, 256, 4), False, v == 3) for v in range(4)])
-            for p in range(MSV):
-                ts(ap("msk" + H, p, 1024, 4), LL, 0.0, A.max, 1.0, A.min)
-            for p in range(MSV, 4):
-                act(ap("msk" + H, p, 1024, 4), ap("msk" + H, 0, 1024, 4))
-            tt(ap("ofm" + H), HI, ap("ofh" + H), A.min)
-            cp(ap("of2" + H), ap("ofm" + H))
-            K, AA, D = ap(PB, 0, 128), ap(PA, 0, 128), ap(PA, 128, 256)
-            lst = [(K, ap("one", p1=1), ap("cra", p1=1), True, False), (K, ap("one", p1=1), ap("crb", p1=1), False, False)]
+                    tt(ap("m%d" % k + H), c, last, A.min)
+                    last = ap("m%d" % k + H)
+                if k == 2:
+                    mm([(SC, idf, blk("act", h, 256), True, False)])
+            mm([(blk(PB, 2 + b), ap("m3" + H, b, 256, 2), idb, False, b == 1) for b in range(2)])
+            scan(ap("rr" + H), ap("z16"), SC, A.add, A.min)
+            tt(ap("ff" + H, 1, 256), ap("rr" + H, 0, 255), ap(PB, 257, 512), A.is_gt)
+            for b in range(2):
+                tt(ap("zh" + H, 16 + b, 144, 16), ap("rr" + H, 128 * b + 7, 128 * b + 128, 16), ap("rr" + H, 128 * b + 15, 128 * b + 128, 16), A.is_gt)
+            mm([(ap(PA, b, 256, 2), blk("ff" + H, b), idb, True, True) for b in range(2)])
+            act(ap("ft" + H), ap(PA, 0, 256), scale=col(8), bias=col(7))
+            mm([(ap(PB, 0, 64), idf, ap("ofl" + H), True, False)]
+               + [(ap(PB, 0, 64), ap("zh" + H, 16 - 2 * x, 144 - 2 * x), blk("hsel", x, 64), False, x == 7) for x in range(8)])
+            cp(ap("of2" + H), ap(PB, 0, 64))
+            mm([(ap(PA, 256, 512), ap("lm"), ap("ft" + H), True, True)])
+            act(ap("msk" + H), ap(PA, 256, 512), F.Relu, scale=65536.0)
+            K, AA = ap(PA, 0, 128), ap(PB, 256, 384)
+            mm([(AA, ap("one", p1=2), ap("ca", p1=2), True, False)])
             if t == 0:
-                for b in range(2):
-                    lst.append((K, ap("r0", b, 256, 2, p1=64), blk("rm", 1 + 2 * h + b, p1=64), False, False))
+                mm([(K, ap("r0", 0, 128), ap("uc"), True, False)]
+                   + [(ap(PA, 64 * b, 64 * b + 64), ap("r0", b, 256, 2), blk("rm0", h, 64), False, False) for b in range(2)])
             else:
-                lst.append((K, ein, blk("rm", 0, p1=48), False, False))
-            mm(lst)
-            for c in range(GMC):
-                tt(blk("gm" + H, c, 1024 // GMC), ind(ap("xt"), blk("of2" + H, c, 64 // GMC)), blk("msk" + H, c, 1024 // GMC), A.mult)
-            mm([(ap(PA, e, 128, 8), ap("gm" + H, e, 1024, 8), ap("bo2"), True, True) for e in range(8)])
+                mm([(K, blk("ri", 2 * (s - 2) + 1), ap("rm"), True, False)])
+            for k in range(4):
+                tt(blk("gm" + H, k, 256), ind(ap("xt"), blk("of2" + H, k, 16)), ap("msk" + H), A.min)
+                mm([(ap(PB, 256 + 64 * b + k, 320 + 64 * b, 4), ap("gm" + H, 256 * k + b, 256 * k + 256, 2), ap("bo2"), False, k == 3 and b == 1)
+                    for b in range(2)])
+            act(ap("cst" + H), AA, bias=2.0 ** -13)
             act(ap("af" + H), AA)
-            act(ap("cst" + H), AA, bias=159.5 + 2.0 ** -13, scale=2.0 ** -12)
-            mm([(ap(PB, u, 128, 2), ap("ids"), blk("af" + H, u, 64), False, False) for u in range(2)])
-            mm([(ap(PB, u, 128, 2), ap("idk"), blk("cst" + H, u, 64), False, u == 1) for u in range(2)])
-            mm([(ap(PA, 128 + u, 256, 2), (idf, ap("idm"))[z], blk(("af", "cst")[z] + H, u, 64), z == 0, z == 1)
-                for u in range(2) for z in range(2)])
-            act(ap("ds" + H), D, bias=160.0 * 4096)
-            for p in [3, 2, 1, 0]:
-                w = (16 * p, 16 * p + 16)
-                scan(blk("so" + H, p), ap("z8"), K, A.add, A.min)
-                ts(ap("mall" + H, *w), ap("so" + H, 128 * p + 7, 128 * p + 128, 8), 2.0 ** 24, A.mult, 2.0 ** 24 - 1, A.min)
-                ts(ap("sall" + H, *w), ap("mall" + H, *w), 4095, an)
-                if p:
-                    tt(ap("eq" + H), ind(ap("sall" + H, *w), L1), ap("ds" + H), A.is_equal)
-                    tt(K, K, ap("eq" + H), A.max)
-            cp(ap("z2" + H, 8, 136), ind(ap("sall" + H), L3))
-            mm([(ap(PB, 256, 320), ap("z2" + H, 8 - 8 * x, 136 - 8 * x), ap("idf", x, 128, 2), x == 0, x == 1) for x in range(2)])
-            oo, eo = blk("offo", s + 1, 64), blk("eo", s)
-            cp(oo, ap(PB, 256, 320))
-            act(ap("xq" + H), ap("so" + H, 7, 512, 8), bias=135.5 + 2.0 ** -16, scale=512.0)
-            act(ap("hh" + H), ap("xq" + H, 0, 48), bias=-712.0)
-            mm([(ap(PA, 384, 432), ap("idn"), ap("xq" + H, 0, 48), True, False)]
-               + [(ap(PA, 384 + 16 * p, 400 + 16 * p), idb, ap("xq" + H, 48, 64), False, p == 2) for p in range(3)])
-            tt(ap("nrc" + H, 0, 48), ap(PA, 384, 432), ap("hh" + H), A.max)
-            mm([(ap(PA, 256, 384), ap("nrc" + H), idb, True, True)])
-            act(eo, ap(PA, 256, 384))
-            if t < NV - 1:
-                for (src, to, sem) in ((oo, ap("offi", 128 * s + 64, 128 * s + 128), "ar%d" % s), (eo, blk("ei", s), "er%d" % s)):
-                    def send(src=src, to=to, sem=sem):
+            mm([(K, ap("i15"), ap("cst" + H), False, False)])
+            mm([(K, ap("ids"), ap("af" + H), False, True)])
+            tt(ap("ds" + H), ap("cst" + H), AA, A.subtract)
+            xq, x0 = "xq" + H, "x0" + H
+
+            def costs(o, k0, k1):
+                act(o, ap("so" + H, 128 * k0 + 7, 128 * k1, 8), scale=-1.0 / 16, bias=130 + TOP / 16 - 0.4375)
+
+            def lists(k):
+                mm([(ap(PB, 16 * k, 16 * k + 16), ap("zl" + H, 16 + 128 * k - 2 * x, 144 + 128 * k - 2 * x), ap("idq", x, 128, 8), x == 0, x == 7)
+                    for x in range(8)])
+
+            def send(src, to, sem):
+                if t < NV - 1:
+                    def fn():
                         a = topo.addr(nxt)
                         g.remote_dma(R(to), R(src), T.sem[sem], T.sem.sent, a[1], a[0], emask(nxt, 0, 1)[0])
                     n = emask(nxt, 0, 1)[1]
-                    op("G", send, [src], [to], 700, dma=(sem, n), lat=NET - 600)
+                    op("G", fn, [src], [to], 700, dma=(sem, n), lat=NET - 600)
                     sent[0] += n
-            e48 = blk("eo", s, p1=48)
-            wb = [ap("pw0", 0, 256), ap("pw1", 0, 256), ap("pw0", 256, 512)]
-            for c in range(PGC):
-                act(blk("pg" + H, c, 1024 // PGC), ind(ap("payr"), ap(oo[0], oo[1] + 64 // PGC * c, oo[1] + 64 // PGC * (c + 1))))
-            own = T.cores[(rank - t) % nr]
-            land = blk("smi", s - 2, 512)
-            r = 16 * (t + 1) % 128
+
+            def states(k0, k1, sem):
+                c = (64 * s + 16 * k0, 64 * s + 16 * k1)
+                ts(ap("mo", *c), ap(PB, 16 * k0, 16 * k1), 2048.0, A.add)
+                send(ap("mo", *c), ap("mi", *c), sem)
+
+            for k in range(4):
+                win, fl = ap("so" + H, 128 * k + 7, 128 * k + 128, 8), blk("fl" + H, k, 16)
+                scan(blk("so" + H, k), ap("z8"), K, A.min, A.max, 2 * TOP)
+                ts(fl, win, ROUND2, A.add, -ROUND2, A.add)
+                if k == 0:
+                    for j in range(3):
+                        costs(blk(x0, j, 16), 0, 1)
+                if k < 3:
+                    d = apx("sall" + H, k, every)
+                    tt(d, win, fl, A.subtract)
+                    tt(ap("eq" + H), ind(d, L1), ap("ds" + H), A.not_equal)
+                    tt(K, K, ap("eq" + H), A.mult)
+                for (k0, k1) in CONV:
+                    if k1 == k + 1:
+                        for b in range(2):
+                            cp(ap("zl" + H, 16 + 128 * k0 + b, 16 + 128 * k1, 16), apx("sall" + H, slice(k0, k1), slice(8 * b, 8 * b + 8)))
+                        for j in range(k0, k1):
+                            lists(j)
+                if k == 2:
+                    costs(ap(xq, 0, 32), 1, 3)
+                    if PARTS == 2:
+                        states(0, 3, "er%d" % s)
+                        if t < NV - 1:
+                            mm([(ap(PB, 128, 256), ap(xq), idb, True, False), (ap(PB, 128, 256), ap(x0), ap("idn"), False, True)])
+                            act(blk("ro", 2 * s), ap(PB, 128, 256), F.Relu, scale=-1.0, bias=GONE)
+                            send(blk("ro", 2 * s), blk("ri", 2 * s), "fr%d" % s)
+            for b in range(2):
+                tt(ap("zl" + H, 400 + b, 528, 16), ap("so" + H, 384 + 64 * b + 7, 448 + 64 * b, 8), ap("fl" + H, 48 + 8 * b, 56 + 8 * b), A.subtract)
+            costs(ap(xq, 32, 48), 3, 4)
+            lists(3)
+            states(3 if PARTS == 2 else 0, 4, "ar%d" % s)
+            for p in (0, 64):
+                o = ap(PA, 128, 256, p0=p, p1=p + 64)
+                mm([(o, ap(xq, 0, 64), idb, True, False), (o, ap(x0, 0, 64), ap("idn"), False, True)])
+            rows = blk("ro", 2 * s + 1)
+            act(blk("ro", 2 * s + 1, p1=64), ap(PA, 128, 256, p1=64), F.Relu, scale=-1.0, bias=GONE)
+            act(blk("ro", 2 * s + 1, p0=64), ap(PA, 128, 256, p0=64), F.Sign, bias=0.5 - GONE)
+            send(rows, blk("ri", 2 * s + 1), "br%d" % s)
+            xs = [blk("smo", 4 * s + k, 256) for k in range(4)]
+            for k in range(4):
+                act(xs[k], ind(ap("payr"), ap("mo", 64 * s + 16 * k, 64 * s + 16 * k + 16)))
+            wb = [None, ap("pw0", 0, 256), ap("pw0", 256, 512), ap("pw1", 0, 256)]
+            for k in range(1, 4):
+                c = wb[k]
+                mm([(ap(c[0], c[1][0].start + b, c[1][0].stop, 2), blk("sel", 2 * k - 2 + b), rows, True, True) for b in range(2)])
+            act(ap("pw0"), ap("pw0"), F.Exp, scale=-0.125)
+            act(wb[3], wb[3], F.Exp, scale=-0.125)
+            for k in range(1, 4):
+                tt(xs[k] if t else wb[k], wb[k], xs[k], A.mult)
+            r = 16 * (t - (NV - 1)) % 128
             turn = ap("idf", r, r + 128)
-            if FOLD:
-                xs = [blk("smo", 4 * s + p, 256) for p in range(4)]
-                act(xs[3], ap("pg" + H, 3, 1024, 4))
-                for p in range(3):
-                    c = wb[p]
-                    mm([(ap(c[0], c[1] + b, c[2], 2), blk("sel", 2 * p + b, p1=48), e48, True, True) for b in range(2)])
-                act(ap("pw0"), ap("pw0"), F.Exp, scale=-0.125)
-                act(wb[1], wb[1], F.Exp, scale=-0.125)
-                for p in (0, 2, 1):
-                    tt(xs[p], wb[p], ap("pg" + H, p, 1024, 4), A.mult)
-                if t:
-                    def home(xs=xs, land=land, own=own, s=s):
-                        g.remote_dma_fused([
-                            RemoteDMATransfer(dst_ids=[dst(own)], dma_engine_mask=emask(own, k, 2)[0], remote_sem=T.sem["sm%d" % (s - 2)],
-                                              srcs=[R(x) for x in xs], dst=R(blk("smi", 2 * (s - 2) + k, 256)), alu_op=1 + k)
-                            for k in range(2)], local_sem=T.sem.sent)
-                    n = 2 * emask(own, 0, 2)[1]
-                    op("G", home, xs, [land], 3500, dma=("sm%d" % (s - 2), n), lat=NET)
-                    sent[0] += n
-                    if t == 1:
-                        mm([(ap("py" + H), turn, land, True, False)])
-                        for x in late[h]:
-                            mm([x])
-                    else:
-                        for k in range(2):
-                            mm([(blk("py" + H, k, 256), turn, ap("smi", land[1] + 256 * k, land[1] + 256 * k + 256), False, t == NV - 1 and k == 1)])
-                else:
-                    mx = [blk("smo", 48 + 2 * h + k, 256) for k in range(2)]
-                    tt(mx[0], xs[0], xs[1], A.max)
-                    tt(mx[1], xs[2], xs[3], A.max)
-                    tt(mx[0], mx[0], mx[1], A.max)
-                    late[h] = ([(ap("py" + H, 0, 256), turn, x, False, False) for x in xs]
-                               + [(ap("py" + H, 256, 512), turn, mx[0], False, False)])
+            if t:
+                own = T.cores[(rank - t) % nr]
+                land = blk("smi", s - 2, 512)
+
+                def home(xs=xs, own=own, s=s):
+                    g.remote_dma_fused([
+                        RemoteDMATransfer(dst_ids=[dst(own)], dma_engine_mask=emask(own, k, 2)[0], remote_sem=T.sem["sm%d" % (s - 2)],
+                                          srcs=[R(x) for x in xs], dst=R(blk("smi", 2 * (s - 2) + k, 256)), alu_op=1 + k)
+                        for k in range(2)], local_sem=T.sem.sent)
+                n = 2 * emask(own, 0, 2)[1]
+                op("G", home, xs, [land], 3500, dma=("sm%d" % (s - 2), n), lat=NET)
+                sent[0] += n
+                if t < NV - 1:
+                    for k in range(2):
+                        mm([(blk("py" + H, k, 256), turn, blk("smi", 2 * (s - 2) + k, 256), False, t == NV - 2 and k == 1)])
             else:
-                for p in (1, 3, 2):
-                    c = wb[p - 1]
-                    mm([(ap(c[0], c[1] + b, c[2], 2), blk("sel", 8 + 2 * (p - 1) + b, p1=48), e48, True, True) for b in range(2)])
-                for p in (1, 3, 2):
-                    act(ap("rho" + H, p, 1024, 4), wb[p - 1], F.Exp, scale=0.125)
-                for (nm, o1, at) in (("os_", A.add, 0), ("om_", A.max, 1)):
-                    for c in range(1024 // PC):
-                        scan(blk(nm + H, c, PC), blk("rho" + H, c, PC), blk("pg" + H, c, PC), A.mult, o1)
-                    act(blk("smo", 2 * s + at, 256), ap(nm + H, 3, 1024, 4))
-                src = blk("smo", s, 512)
-                if t:
-                    def home(src=src, land=land, own=own, s=s):
-                        a = topo.addr(own)
-                        g.remote_dma(R(land), R(src), T.sem["sm%d" % (s - 2)], T.sem.sent, a[1], a[0], emask(own, 0, 1)[0])
-                    n = emask(own, 0, 1)[1]
-                    op("G", home, [src], [land], 700, dma=("sm%d" % (s - 2), n), lat=NET + 500)
-                    sent[0] += n
-                    src = land
-                mm([(ap("py" + H), turn, src, t == 0, t == NV - 1)])
+                for j, o in enumerate((A.add, A.max)):
+                    a = blk("loc" + H, j, 256)
+                    for k in range(1, 4):
+                        tt(a, wb[k], xs[0] if k == 1 else a, o)
+                mm([(ap("py" + H), turn, ap("loc" + H), True, False)])
+    r = 16 * NV % 128
     for h in range(2):
         cur[0] = h
         for k, o in enumerate((T.ys, T.ym)):
             a = blk("yo", 2 * h + k, 256)
-            cp(a, blk("py%d" % h, k, 256))
+            tt(a, blk("py%d" % h, k, 256), blk("smi", 2 * (2 * NV - 4 + h) + k, 256), A.add)
 
-            def store(o=o, a=a, h=h):
-                g.sync.dma_start(o[:, 256 * h:256 * h + 256], R(a)).then_inc(T.sem.stored, 16)
-            op("Y", store, [a], [], 60, dma=("stored", 64), lat=2500)
+            def store(o=o, j=2 * h + k, h=h):
+                g.sync.dma_start(o[128 - r:128, 256 * h:256 * h + 256], R(blk("yo", j, 256, p1=r))).then_inc(T.sem.stored, 16)
+                g.sync.dma_start(o[0:128 - r, 256 * h:256 * h + 256], R(blk("yo", j, 256, p0=r))).then_inc(T.sem.stored, 16)
+            op("Y", store, [a], [], 120, dma=("stored", 128), lat=2500)
     return ops, q, sent[0]
 
 
 def link(ops):
-    wr = {n: np.full(v[1][1], -1) for n, v in SCRATCH.items()}
+    wr = {n: np.full(int(np.prod(v[1][1:])), -1) for n, v in SCRATCH.items()}
     rd = {n: [] for n in SCRATCH}
-    bank = {n: {} for n, v in SCRATCH.items() if v[0] == "psum"}
+    bank = {n: [None, [], []] for n, v in SCRATCH.items() if v[0] == "psum"}
     for i, o in enumerate(ops):
         d = set()
         for a in o["rd"] + o["wr"]:
-            d.update(int(x) for x in np.unique(wr[a[0]][a[1]:a[2]:a[3]]) if x >= 0)
-            if a[0] in bank:
-                d.update(j for e, j in bank[a[0]].items() if e != o["eng"] or e == "P")
+            d.update(int(x) for x in np.unique(wr[a[0]][cols(a)]) if x >= 0)
+        for n in {a[0] for a in o["rd"] + o["wr"] if a[0] in bank}:
+            b = bank[n]
+            if b[0] != o["eng"]:
+                b[:] = [o["eng"], [], b[1]]
+            d.update(b[2] + (b[1][-1:] if o["eng"] == "P" else []))
+            b[1].append(i)
         for a in o["wr"]:
-            cols = set(range(a[1], a[2], a[3]))
-            d.update(j for (j, c) in rd[a[0]] if not cols.isdisjoint(c))
-            rd[a[0]] = [(j, c - cols) for (j, c) in rd[a[0]] if c - cols]
+            cs = set(cols(a).tolist())
+            d.update(j for (j, c) in rd[a[0]] if not cs.isdisjoint(c))
+            rd[a[0]] = [(j, c - cs) for (j, c) in rd[a[0]] if c - cs]
         for a in o["rd"]:
-            rd[a[0]].append((i, set(range(a[1], a[2], a[3]))))
+            rd[a[0]].append((i, set(cols(a).tolist())))
         for a in o["wr"]:
-            wr[a[0]][a[1]:a[2]:a[3]] = i
-        for a in o["rd"] + o["wr"]:
-            if a[0] in bank:
-                bank[a[0]][o["eng"]] = i
+            wr[a[0]][cols(a)] = i
         d.discard(i)
         o["deps"] = sorted(d)
 
@@ -583,4 +575,4 @@ def rank_program(g, core, T, topo):
     for sem, val in sorted(count.items()):
         g.wait_ge(T.sem[sem], val)
     g.wait_ge(T.sem.sent, sent)
-    g.sync.wait_ge(T.sem.stored, 64)
+    g.sync.wait_ge(T.sem.stored, 128)

@@ -4,17 +4,23 @@ from concourse.mybir import AluOpType as A
 from concourse.mybir import ActivationFunctionType as F
 
 NV = 6
-PARTS = 1
-MCE = "SVSS"
-CONV = [(0, 3)]
+CFG = dict(
+    parts=1,
+    mce="VSSS",
+    i32=True, conv=[(0, 2), (2, 3), (3, 4)],
+    strikes=0,
+    pay=("fuse", "fuse"), late=(True, True),
+    fold=(False, False),
+    si32=True, tail=True, q7="Y", sx="l2zm", own=False,
+    sw=[(0, 1536), (1536, 2816), (2816, 4096)], nat=False,
+)
 CH = [0, 512, 1536, 2816, 3840, 4096]
-SW = [(0, 1536), (1536, 2816), (2816, 4096)]
-TRIES = 2500
+TRIES = 1500
 SCRATCH = {}
 GONE = 106.0
+U = 4096.0
 TOP = 3584.0
-NONE = TOP - (16 * 176 + 2047.0 / 4096)
-ROUND2 = 1.5 * 2 ** 24
+NONE = U * (TOP - 16 * 176) + 4095
 
 
 def _sb(n, w, d, where="sbuf"):
@@ -25,10 +31,12 @@ for _n, _w, _d in [
         ("arc", 4096, "int32"), ("xt", 8192, "int32"), ("mn", 4096, "float32"),
         ("mc", 4096, "bfloat16"), ("payr", 4096, "bfloat16"), ("acs", 512, "float32"), ("act", 512, "float32"),
         ("sti", (4, 32), "int32"), ("off0", 128, "uint16"), ("rsi", 256, "int32"), ("r0", 256, "bfloat16"),
-        ("ci", 48, "int32"), ("cf", 16, "float32"), ("i16", 16, "float32"),
+        ("ci", 48, "int32"), ("cf", 24, "float32"), ("bo0", 8, "float32"), ("lm0", 128, "bfloat16"), ("i16", 16, "float32"),
         ("onef", 256, "float32"), ("one", 128, "bfloat16"), ("idf", 256, "float32"), ("idb", 128, "bfloat16"),
-        ("idq", 128, "float16"), ("idn", 128, "bfloat16"), ("i15", 128, "bfloat16"), ("ids", 128, "float32"),
-        ("bo2", 16, "float32"), ("lm", 128, "bfloat16"), ("hsel", 512, "bfloat16"), ("sel0", 1024, "bfloat16"), ("sel", 768, "bfloat16"),
+        ("idq", 128, "float16"), ("idn", 128, "bfloat16"), ("i15", 128, "bfloat16"),
+        ("idk", 128, "bfloat16"),
+        ("bo2", 16, "float32"), ("lm", 128, "bfloat16"), ("hsel", 512, "bfloat16"), ("sel0", 1024, "bfloat16"),
+        ("sell", 768, "bfloat16"), ("selp", 768, "bfloat16"),
         ("ua", 128, "bfloat16"), ("ub", 128, "bfloat16"), ("uc", 128, "bfloat16"), ("ud", 128, "bfloat16"),
         ("rm0", 128, "bfloat16"), ("rm", 128, "bfloat16"), ("ca", 128, "bfloat16"),
         ("lu", 32, "uint16"), ("z16", 256, "float32"), ("z8", 128, "float32"),
@@ -40,18 +48,20 @@ for _h in "01":
             ("mcg", 1024, "bfloat16"), ("c0s", 256, "bfloat16"), ("m1", 256, "bfloat16"), ("m2", 256, "bfloat16"),
             ("m3", 256, "bfloat16"), ("rr", 256, "float32"), ("ff", 256, "bfloat16"), ("ft", 256, "bfloat16"),
             ("msk", 256, "bfloat16"), ("gm", 1024, "float32"), ("cst", 128, "bfloat16"), ("zh", 144, "bfloat16"),
-            ("ofl", 64, "float32"), ("of2", 64, "uint16"), ("ds", 128, "float32"), ("so", 512, "float32"), ("eq", 128, "bfloat16"),
-            ("fl", 64, "float32"), ("sall", (3, 16), "float32"), ("zl", 528, "float16"),
-            ("xq", 128, "bfloat16"), ("x0", 128, "bfloat16"), ("af", 128, "float32"), ("loc", 512, "float32")]:
+            ("ofl", 64, "float32"), ("of2", 64, "uint16"), ("ds", 128, "float32"), ("eq", 384, "bfloat16"),
+            ("so", 512, "int32" if CFG["i32"] else "float32"), ("fl", 64, "int32"), ("sall", (4, 16), "int32"), ("zl", 528, "float16"),
+            ("xx", 112, "bfloat16"), ("af", 128, "float32"), ("loc", 512, "float32"), ("wt", 768, "float32")]:
         _sb(_n + _h, _w, _d)
-for _n in ["pa0", "pb0", "pa1", "pb1", "pw0", "pw1", "py0", "py1"]:
+for _n in ["pa0", "pb0", "pc0", "pa1", "pb1", "pc1", "py0", "py1"]:
     _sb(_n, 512, "float32", "psum")
 
-SEMAPHORES = (["cV", "cS", "cP", "cG", "sent", "stored"] + ["ld%d" % i for i in range(10)] + ["sw%d" % i for i in range(2 * len(SW))]
+SEMAPHORES = (["cV", "cS", "cP", "cG", "sent", "stored"] + ["ld%d" % i for i in range(10)] + ["sw%d" % i for i in range(10)]
               + ["%s%d" % (n, i) for n in ("ar", "br", "er", "fr", "sm") for i in range(10)])
 
-CY, PCY = 0.92, 0.5
-HOP, NET, GA = 160.0, 3300.0, 1.5
+GUESS = [dict(cy=0.86, ga=1.5, tti=0, v=20, s=60, m=12, g=300, hop=190, hs=100, net=1300, row=40, rate=350, dl=1500, di=180),
+         dict(cy=0.83, ga=1.2, tti=0, v=50, s=40, m=5, g=200, hop=260, hs=40, net=1000, row=20, rate=350, dl=1300, di=170),
+         dict(cy=0.86, ga=1.6, tti=2, v=0, s=20, m=5, g=470, hop=150, hs=60, net=3000, row=40, rate=500, dl=1000, di=230),
+         dict(cy=1.05, ga=1.8, tti=0, v=20, s=80, m=10, g=400, hop=150, hs=150, net=1400, row=60, rate=250, dl=2000, di=100)]
 
 
 def ap(b, c0=0, c1=None, st=1, p0=0, p1=128):
@@ -72,6 +82,7 @@ def ncol(a):
 
 
 def build(g, T, topo, rank):
+    C = CFG
     ops, cur = [], [None]
     q = {"V": g.vector, "S": g.scalar, "P": g.tensor, "G": g, "Y": g.sync}
 
@@ -83,21 +94,21 @@ def build(g, T, topo, rank):
         idx = tuple(slice(x.start, x.stop) if isinstance(x, slice) and x.step == 1 else x for x in a[1])
         return T[a[0]][(slice(a[2], a[3]),) + idx]
 
-    def op(eng, fn, rd, wr, dur, **kw):
+    def op(eng, fn, rd, wr, cost, **kw):
         flat = []
         for a in rd:
             if isinstance(a, tuple):
                 flat += [a[1], a[2]] if a[0] == "ind" else [a]
-        ops.append(dict(half=cur[0], eng=eng, fn=fn, rd=flat, wr=wr, dur=dur, **kw))
+        ops.append(dict(half=cur[0], eng=eng, fn=fn, rd=flat, wr=wr, cost=cost, **kw))
 
     def vdur(out, ins, tt=False):
         n = ncol(out)
         if ins and ins[0][0] == "ind":
-            return 60 + n * GA * CY
+            return (0, n, 1, 30, tt)
         c = 0.5 if all(SCRATCH[a[0]][2] in ("bfloat16", "uint16", "float16") for a in [out] + ins) else 1.0
         if tt and not any(SCRATCH[a[0]][0] == "psum" for a in ins):
             c *= 2
-        return 30 + max(64, n * c) * CY
+        return (max(64, n * c), 0, 1, 0)
 
     def tt(out, i0, i1, o):
         op("V", lambda: g.vector.tensor_tensor(R(out), R(i0), R(i1), o), [i0, i1], [out], vdur(out, [i0, i1], True))
@@ -119,8 +130,9 @@ def build(g, T, topo, rank):
         op("V", lambda: g.vector.tensor_tensor_scan(R(out), R(d0), R(d1), first, o0, o1), [d0, d1], [out], vdur(out, [d0, d1]))
 
     def act(out, i0, f=F.Identity, bias=0.0, scale=1.0):
-        d = 100 + ncol(out) * CY * (GA if i0[0] == "ind" else 1)
-        op("S", lambda: g.scalar.activation(R(out), R(i0), f, bias=R(bias), scale=R(scale)), [i0, bias, scale], [out], d)
+        n = ncol(out)
+        op("S", lambda: g.scalar.activation(R(out), R(i0), f, bias=R(bias), scale=R(scale)), [i0, bias, scale], [out],
+           (0, n, 1, 0) if i0[0] == "ind" else (n, 0, 1, 0))
 
     def mm(lst):
         def fn():
@@ -128,29 +140,27 @@ def build(g, T, topo, rank):
             for (o, l, r, s0, s1) in lst:
                 h = g.tensor.matmul(R(o), R(l), R(r), s0, s1)
             return h
-        d = 40
-        for (o, l, r, s0, s1) in lst:
-            d += 15 + max(min(64, ncol(l)), ncol(r)) * PCY * (4 if SCRATCH[l[0]][2] == "float32" else 1)
-        op("P", fn, [x[1] for x in lst] + [x[2] for x in lst], [x[0] for x in lst], d)
+        d = sum(max(min(64, ncol(l)), ncol(r)) * (2 if SCRATCH[l[0]][2] == "float32" else 0.5) for (o, l, r, s0, s1) in lst)
+        op("P", fn, [x[1] for x in lst] + [x[2] for x in lst], [x[0] for x in lst], (d, 0, len(lst), 30))
 
     def iota(out, pat, base, cmul):
         if SCRATCH[out[0]][2] == "int32":
             fn = lambda: g.iota(R(out), pat, base, cmul)
         else:
             fn = lambda: g.iota(R(out), pat, base, cmul, allow_small_or_imprecise_dtypes=True)
-        op("G", fn, [], [out], 130 + 2 * ncol(out) * CY)
+        op("G", fn, [], [out], (2 * ncol(out), 0, 0, 130))
 
     def asel(out, i0, pat, o, base, cmul, fill=0.0):
-        op("G", lambda: g.affine_select(R(out), R(i0), pat, o, fill, base, cmul), [i0], [out], 170 + 2 * ncol(out) * CY)
+        op("G", lambda: g.affine_select(R(out), R(i0), pat, o, fill, base, cmul), [i0], [out], (2 * ncol(out), 0, 0, 170))
 
     def paint(x, pat, base, v):
         asel(x, x, pat, A.not_equal, base, -1, v)
 
-    def load(sem, pairs, wr, lat, rd=()):
+    def load(sem, pairs, wr, lat, rd=(), e="Y", by=0):
         def fn():
             for (o, i) in pairs:
-                g.sync.dma_start(o, i).then_inc(T.sem[sem], 16)
-        op("Y", fn, list(rd), wr, 60 * len(pairs), dma=(sem, 16 * len(pairs)), lat=lat)
+                q[e].dma_start(o, i).then_inc(T.sem[sem], 16)
+        op(e, fn, list(rd), wr, (0, 0, 0, 80 * len(pairs)), dma=(sem, 16 * len(pairs)), lat=lat, by=by, nd=len(pairs))
 
     ind = lambda w, o: ("ind", w, o)
     col = lambda j: ap("cf", j, j + 1)
@@ -158,95 +168,130 @@ def build(g, T, topo, rank):
     every = slice(None)
 
     for i in range(len(CH) - 1):
-        load("ld%d" % i, [(T.arc[:, CH[i]:CH[i + 1]], T.arcs[:, CH[i]:CH[i + 1]])], [ap("arc", CH[i], CH[i + 1])], 2200 + 2.2 * CH[i + 1])
+        load("ld%d" % i, [(T.arc[:, CH[i]:CH[i + 1]], T.arcs[:, CH[i]:CH[i + 1]])], [ap("arc", CH[i], CH[i + 1])], 2200 + 2.2 * CH[i + 1],
+             by=512 * (CH[i + 1] - CH[i]))
     load("ld7", [(T.sti[:], T.st0[:])] + [(T.rsi[8 * j:8 * j + 8, :], T.rs0[:, 256 * j:256 * j + 256]) for j in range(8)],
-         [apx("sti", every, every), ap("rsi")], 12000)
-    load("ld6", [(T.acs[:], T.ac[:])], [ap("acs")], 12500)
+         [apx("sti", every, every), ap("rsi")], 2500, by=1 << 17, e=C["q7"])
+    load("ld6", [(T.acs[:], T.ac[:])], [ap("acs")], 12500, by=1 << 18)
 
+    start = len(ops)
     ms(ap("onef"), 1.0)
     idf, idb = ap("idf", 0, 128), ap("idb")
-    asel(idf, ap("onef", 0, 128), [[-1, 128]], A.is_equal, 0, 1)
-    for n in ("sel0", "hsel", "zl0", "zl1"):
-        ms(ap(n), 0.0)
-    for n in ("ua", "ub", "ff0", "ff1", "zh0", "zh1", "xq0", "xq1", "x00", "x01"):
-        act(ap(n), ap("onef", 0, SCRATCH[n][1][1]), scale=0.0)
     iota(ap("ci", 0, 2), [[16, 2]], 0, 1)
     iota(ap("ci", 8, 16), [[2, 8]], 0, 0)
+    iota(ap("ci", 16, 19), [[0, 3]], 7, 0)
+    iota(ap("ci", 19, 22), [[128, 3]], 7, 0)
     iota(ap("i16"), [[1, 16]], 0, 0)
-    paint(ap("sel0"), [[1, 64], [0, 16]], 0, 1.0)
+    asel(idf, ap("onef", 0, 128), [[-1, 128]], A.is_equal, 0, 1)
+    iota(ap("lm"), [[1, 8], [0, 16]], 0, 0)
+    iota(ap("ua"), [[0, 16], [1, 8]], 0, 0)
+    iota(ap("ub"), [[1, 16], [0, 2], [16, 4]], 0, 0)
+    for n in ("uc", "sel0", "hsel", "zl0", "zl1"):
+        ms(ap(n), 0.0)
+    ms(ap("r0", p0=64), 1.0)
+    for n in ("ff0", "ff1", "zh0", "zh1", "xx0", "xx1"):
+        act(ap(n), ap("onef", 0, SCRATCH[n][1][1]), scale=0.0)
     act(ap("one"), ap("onef", 0, 128))
     act(ap("idf", 128, 256), idf)
-    for n, v in (("idb", 1.0), ("i15", -15.0), ("idn", -1.0), ("ids", -1.0)):
+    for n, v in (("idb", 1.0), ("i15", -17.0), ("idn", -1.0), ("idk", -U * U)):
         act(ap(n), idf, scale=v)
-    ts(ap("idq"), idf, -4096.0, A.mult)
+    cp(ap("idq"), idf)
     sh, an = A.logical_shift_right, A.bitwise_and
     ts(ap("ci", 2, 3), ap("ci", 1, 2), 3, sh, 15, an)
     ts(ap("ci", 3, 4), ap("ci", 0, 1), 3, sh, 1, an)
     ts(ap("ci", 4, 5), ap("ci", 0, 1), 4, sh)
     ts(ap("ci", 5, 6), ap("ci", 0, 1), 15, an)
-    cp(ap("cf", 0, 6), ap("ci", 0, 6))
+    ts(ap("ci", 6, 7), ap("ci", 0, 1), 4, sh, 3, an)
+    ts(ap("ci", 7, 8), ap("ci", 0, 1), 6, sh)
+    cp(ap("cf", 0, 8), ap("ci", 0, 8))
     PN, NEXT, Q8 = col(0), col(2), col(3)
-    ts(ap("bo2"), ap("i16"), NEXT, A.is_equal, 2.0 ** -12, A.mult)
+    ts(ap("bo2"), ap("i16"), NEXT, A.is_equal)
     ts(ap("lu", 0, 8), ap("ci", 8, 16), Q8, A.add)
-    L1 = ap("lu", 0, 8)
-    act(col(10), PN, scale=-160.5, bias=160.0)
-    act(ap("ca", p1=2), ap("onef", 0, 128, p1=2), scale=ap("cf", 10, 11, p1=2))
+    act(col(9), col(5), scale=8.0)
+    ts(ap("lu", 8, 14), ap("ci", 16, 22), col(9), A.add)
+    L1, LX = ap("lu", 0, 8), ap("lu", 8, 14)
+    act(ap("ca", p1=1), ap("onef", 0, 128, p1=1), scale=160 * U)
     act(ap("z16"), ap("onef"), scale=0.0)
     act(ap("z16", 0, 256, 16), ap("onef", 0, 16), scale=1000.0)
-    act(ap("z8"), ap("onef", 0, 128), scale=2 * TOP)
+    act(ap("z8"), ap("onef", 0, 128), scale=2 * TOP * U)
     act(ap("z8", 0, 128, 8), ap("onef", 0, 16), scale=NONE)
-    iota(ap("lm"), [[1, 8], [0, 16]], 0, 0)
     ts(ap("lm"), ap("lm"), col(4), A.is_equal, -1.0, A.mult)
-    for base in (0, 8):
-        paint(ap("lm"), [[16, 8], [0, 2], [1, 8]], base, 1.0)
-    act(col(6), col(5), F.Exp, scale=0.8)
-    act(ap("lm"), ap("lm"), scale=col(6))
-    ts(col(7), col(5), 0.0, A.is_equal)
-    act(col(8), col(7), scale=-1.0, bias=1.0)
+    ts(ap("ci", 22, 23), ap("ci", 1, 2), 4, sh, 7, an)
+    ts(ap("ci", 23, 24), ap("ci", 0, 1), 7, an)
+    ts(ap("ci", 24, 25), ap("ci", 0, 1), 63, an)
+    cp(ap("cf", 16, 19), ap("ci", 22, 25))
+    act(col(11), col(5), F.Exp, scale=0.8)
+    ops[-1]["cost"] = (1, 0, 1, 1300)
+    if C["nat"]:
+        asel(ap("lm0"), ap("lm"), [[1, 128]], A.not_equal, 0, -1, 1.0)
+        act(ap("lm0"), ap("lm0"), scale=col(11))
+        ts(ap("bo0"), ap("i16", 0, 8), col(16), A.is_equal)
+    ts(ap("ua"), ap("ua"), col(17), A.not_equal, 0.5, A.subtract)
+    tt(ap("lm"), ap("lm"), ap("ua"), A.mult)
+    act(ap("lm"), ap("lm"), scale=col(11))
+    ts(col(12), col(5), 0.0, A.is_equal)
+    act(col(8), col(12), scale=-1.0, bias=1.0)
+    ts(col(13), col(6), 0.0, A.is_gt)
+    act(col(14), col(7), scale=-1.0, bias=GONE - 1)
+    act(col(15), col(13), scale=col(14), bias=1.0)
+    RB = col(15)
+    ms(ap("uc", p0=64, p1=66), (TOP + 2560) * U)
+    iota(ap("ud"), [[0, 16], [-2 * int(U), 8]], 0, 0)
+    act(ap("uc", p0=64, p1=65), ap("ud", p0=64, p1=65))
+    paint(ap("sel0"), [[1, 64], [0, 16]], 0, 1.0)
     paint(ap("hsel"), [[1, 8], [0, 4], [8, 16]], 0, 4096.0)
-    mend = (GONE - 64) / 2
-    bygroup, byrow = [[0, 2], [1, 8], [0, 8]], [[1, 16], [0, 2], [16, 4]]
-    for (n, base) in (("uc", 0), ("ud", -int(16 * mend))):
-        iota(ap(n), [[0, 16], [2, 8]], base, 0)
-        asel(ap(n), ap(n), bygroup, A.is_equal, 120, -1)
-        paint(ap(n), bygroup, 112, -(TOP + 2560))
-    act(ap("ud", 0, 128, 4), ap("uc", 0, 128, 4))
-    paint(ap("ua"), byrow, 0, -16.0)
-    paint(ap("ub"), byrow, -16, 16.0)
-    paint(ap("ub"), byrow, 48, 16 * mend)
-    paint(ap("ub"), bygroup, 48, -16.0)
+    act(col(19), col(7), scale=16 * U, bias=-16 * U)
+    act(col(20), col(7), scale=16 * U * 83, bias=-16 * U * 41)
+    ts(ap("ua"), ap("ub"), col(18), A.is_equal, col(19), A.mult)
+    ts(ap("ub"), ap("ub"), col(18), A.is_equal, col(20), A.mult)
+    act(ap("ub", p1=1), ap("onef", 0, 128, p1=1), scale=-16 * U * 64)
     act(ap("ub", 0, 128, 4), ap("onef", 0, 32), scale=0.0)
-    tt(ap("ub"), ap("ub"), ap("ud"), A.add)
+    tt(ap("ub"), ap("ub"), ap("uc"), A.add)
     for (n, u) in (("rm0", "ua"), ("rm", "ub")):
         for b in range(2):
             act(ap(n, 64 * b + 8, 64 * b + 64), ap(u, 64 * b, 64 * b + 56))
             act(ap(n, 64 * b, 64 * b + 8), ap(u, 64 * b + 56, 64 * b + 64))
-    act(ap("sel"), ap("sel0", 0, 768), scale=-1.0)
-    paint(ap("sel"), [[1, 48], [0, 16]], 64, -mend)
-    paint(ap("sel"), [[0, 6], [1, 8], [0, 16]], 48, 1.0)
-    paint(ap("sel"), [[0, 6], [1, 8], [0, 16]], 112, mend)
+    for i in range(start, len(ops)):
+        ops[i]["soon"] = True
+    act(ap("sell"), ap("sel0", 256, 1024), scale=-1.0)
+    act(ap("selp"), ap("sel0", 256, 1024), scale=41.0)
+    paint(ap("selp"), [[1, 48], [0, 16]], 80, -42.0)
+    for n, v in (("sell", GONE), ("selp", 64.0)):
+        paint(ap(n), [[0, 768]], 0, v)
+    banks, turn_no = ["pa0", "pa1", "pb0", "pb1", "pc0", "pc1"], [0]
     for i in range(len(CH) - 1):
         c = (CH[i], CH[i + 1])
         ts(ap("xt", *c), ap("arc", *c), 32767, an)
         ts(ap("arc", *c), ap("arc", *c), 15, sh)
-        tt(ap("mn", *c), ap("xt", *c), ap("arc", *c), A.min)
+        if C["si32"]:
+            for c0 in range(c[0], c[1], 512):
+                c1 = min(c0 + 512, c[1])
+                b = ap(banks[turn_no[0] % 6], 0, c1 - c0)
+                turn_no[0] += 1
+                act(b, ap("arc", c0, c1))
+                tt(ap("mn", c0, c1), b, ap("xt", c0, c1), A.min)
+        else:
+            tt(ap("mn", *c), ap("xt", *c), ap("arc", *c), A.min)
         act(ap("mc", *c), ap("mn", *c), bias=159.5 + 2.0 ** -13, scale=2.0 ** -12)
-    for i, (c0, c1) in enumerate(SW):
+    for i, (c0, c1) in enumerate(C["sw"]):
         lo = lambda n, k, o: T[n][16 * k:16 * k + 8, o + c0:o + c1]
         hi = lambda n, k, o: T[n][16 * k + 8:16 * k + 16, o + c0:o + c1]
         load("sw%d" % (2 * i), [(lo("xt", k, 4096), hi("xt", k, 0)) for k in range(8)] + [(hi("xt", k, 4096), hi("arc", k, 0)) for k in range(8)],
-             [ap("xt", 4096 + c0, 4096 + c1)], 2200 + 2.2 * (c1 - c0), [ap("xt", c0, c1), ap("arc", c0, c1)])
-        load("sw%d" % (2 * i + 1), [(hi("xt", k, 0), lo("arc", k, 0)) for k in range(8)],
-             [ap("xt", c0, c1)], 2200 + 1.1 * (c1 - c0), [ap("arc", c0, c1)])
-    load("ld8", [(T.payr[16:128, :], T.pay[0:112, :]), (T.payr[0:16, :], T.pay[112:128, :])], [ap("payr")], 6000, [ap("mn", 2815, 2816)])
-    ms(ap("r0", p0=64), -1.0)
-    cp(ap("r0", p1=64), ap("rsi", p1=64))
+             [ap("xt", 4096 + c0, 4096 + c1)], 2200 + 2.2 * (c1 - c0), [ap("xt", c0, c1), ap("arc", c0, c1)], by=512 * (c1 - c0))
+        last_move = [(hi("xt", k, 0), lo("arc", k, 0)) for k in range(8)]
+        if not C["nat"]:
+            load("sw%d" % (2 * i + 1), last_move, [ap("xt", c0, c1)], 2200 + 1.1 * (c1 - c0), [ap("arc", c0, c1)], by=256 * (c1 - c0))
+    c0, c1 = 0, 4096
+    last_move = [(hi("xt", k, 0), lo("arc", k, 0)) for k in range(8)]
+    load("ld8", [(T.payr[16:128, :], T.pay[0:112, :]), (T.payr[0:16, :], T.pay[112:128, :])], [ap("payr")], 9000, by=1 << 20)
+    ops[-1]["soft"] = [len(ops) - 2]
+    act(ap("r0", p1=64), ap("rsi", p1=64))
     for h in range(2):
         cp(blk("off0", h, 64), apx("sti", every, slice(16 * h, 16 * h + 16)))
-        bank = "pa%d" % h
+        bank = "py%d" % h
         for b in range(2):
             o, i = blk(bank, b), ap("acs", 256 * h + b, 256 * h + 256, 2)
-            op("P", lambda o=o, i=i: g.tensor.transpose(R(o), R(i), R(idf)), [i, idf], [o], 300)
+            op("P", lambda o=o, i=i: g.tensor.transpose(R(o), R(i), R(idf)), [i, idf], [o], (256, 0, 1, 30))
         act(blk("act", h, 256), ap(bank, 0, 256))
 
     nr = len(T.cores)
@@ -261,23 +306,84 @@ def build(g, T, topo, rank):
         k = len(e) // of
         return int(sum(1 << x for x in e[part * k:part * k + k])), k
 
-    sent = [0]
+    sent, first = [0], [0]
+
+    def write(core, src, to, sem):
+        def fn():
+            a = topo.addr(core)
+            g.remote_dma(R(to), R(src), T.sem[sem], T.sem.sent, a[1], a[0], emask(core, 0, 1)[0])
+        n = emask(core, 0, 1)[1]
+        op("G", fn, [src], [to], (0, 0, 1, 0), dma=(sem, n), rows=(8, 128 * ncol(src) * (4 if SCRATCH[src[0]][2] == "float32" else 2)))
+        sent[0] += n
+
+    def payload(t, h, late, steps=((1, 2), (3,)), early=False):
+        H, s = str(h), 2 * t + h
+        cur[0] = h
+        PA, PC = "pa" + H, "pc" + H
+        rows = blk("ro", 2 * s + (0 if early else 1))
+        folded = t > 0 and (t < NV - 1 or C["fold"][h])
+        fuse = folded and C["pay"][h] == "fuse"
+        xs = [blk("smo", 4 * s + k, 256) for k in range(4)]
+        lst = [ind(ap("payr"), ap("mo", 64 * s + 16 * k, 64 * s + 16 * k + 16)) for k in range(4)]
+        wb = [None, ap(PC, 0, 256), ap(PC, 256, 512), ap(PC, 0, 256) if late else ap(PA, 256, 512)]
+        loc = [blk("loc" + H, j, 256) for j in range(2)]
+        for ks in steps:
+            for k in ((0,) if ks[0] == 1 else ()) + (() if fuse else ks):
+                act(xs[k], lst[k])
+            for k in ks:
+                c = wb[k]
+                mm([(ap(c[0], c[1][0].start + b, c[1][0].stop, 2), blk("selp", 2 * k - 2 + b), rows, True, True) for b in range(2)])
+            w = ap(PC) if ks[0] == 1 else wb[3]
+            act(ap("wt" + H, 256 * ks[0] - 256, 256 * ks[-1]) if fuse else w, w, F.Exp, scale=-0.125)
+            for k in ks:
+                if fuse:
+                    tt(xs[k], lst[k], blk("wt" + H, k - 1, 256), A.mult)
+                else:
+                    tt(xs[k] if folded else wb[k], wb[k], xs[k], A.mult)
+            if not folded:
+                for k in ks:
+                    for j, o in enumerate((A.add, A.max)):
+                        tt(loc[j], wb[k], xs[0] if k == 1 else loc[j], o)
+        if early:
+            return
+        r = 16 * (t - (NV - 1)) % 128
+        turn = ap("idf", r, r + 128)
+        own = T.cores[(rank - t) % nr]
+        land = blk("smi", s - 2, 512)
+        if t == 0:
+            mm([(ap("py" + H), turn, ap("loc" + H), True, False)])
+            return
+        if folded:
+            def home():
+                g.remote_dma_fused([
+                    RemoteDMATransfer(dst_ids=[dst(own)], dma_engine_mask=emask(own, k, 2)[0], remote_sem=T.sem["sm%d" % (s - 2)],
+                                      srcs=[R(x) for x in xs], dst=R(blk("smi", 2 * (s - 2) + k, 256)), alu_op=1 + k)
+                    for k in range(2)], local_sem=T.sem.sent)
+            n = 2 * emask(own, 0, 2)[1]
+            op("G", home, xs, [land], (0, 0, 1.5, 0), dma=("sm%d" % (s - 2), n), rows=(24, 400000))
+            sent[0] += n
+        else:
+            write(own, ap("loc" + H), land, "sm%d" % (s - 2))
+        if t < NV - 1:
+            for k in range(2):
+                mm([(blk("py" + H, k, 256), turn, blk("smi", 2 * (s - 2) + k, 256), False, t == NV - 2 and k == 1)])
+
     for t in range(NV):
         for h in range(2):
             H = str(h)
             cur[0] = h
-            PA, PB = "pa" + H, "pb" + H
+            PA, PB, PC = "pa" + H, "pb" + H, "pc" + H
             s = 2 * t + h
             lb, l0 = ("off0", 64 * h) if t == 0 else ("mi", 64 * (s - 2))
             SC = ap(PB, 256, 512)
+            mm([(SC, idf, blk("act", h, 256), True, False)])
             for k in range(4):
                 i0 = ind(ap("mc"), ap(lb, l0 + 16 * k, l0 + 16 * k + 16))
-                if MCE[k] == "S":
+                if C["mce"][k] == "S":
                     act(blk("mcg" + H, k, 256), i0, bias=-160.0)
                 else:
                     ts(blk("mcg" + H, k, 256), i0, -160.0, A.add)
-            cp(ap("ofl" + H), ap(lb, l0, l0 + 64))
-            cbank = [ap("py" + H, 0, 256), ap(PA, 0, 256), ap(PB, 0, 256), ap(PA, 256, 512)]
+            cbank = [ap("py" + H, 0, 256), ap(PA, 0, 256), ap(PC, 0, 256), ap(PA, 256, 512)]
             last = blk("mcg" + H, 0, 256)
             for k in range(1 if t else 0, 4):
                 c = cbank[k]
@@ -285,9 +391,9 @@ def build(g, T, topo, rank):
                 if t == 0:
                     lst.append((c, blk("sel0", 2 * k + h, p1=64), ap("r0", p1=64), False, True))
                 else:
-                    x = blk("ri", 2 * (s - 2) + (0 if PARTS == 2 and k < 3 else 1), p1=64)
+                    x = blk("ri", 2 * (s - 2) + (0 if C["parts"] == 2 and k < 3 else 1), p1=64)
                     for b in range(2):
-                        lst.append((ap(c[0], c[1][0].start + b, c[1][0].stop, 2), blk("sel", 2 * k - 2 + b, p1=64), x, False, b == 1))
+                        lst.append((ap(c[0], c[1][0].start + b, c[1][0].stop, 2), blk("sell", 2 * k - 2 + b, p1=64), x, False, b == 1))
                 mm(lst)
                 if k == 0:
                     last = ap("c0s" + H)
@@ -295,131 +401,140 @@ def build(g, T, topo, rank):
                 else:
                     tt(ap("m%d" % k + H), c, last, A.min)
                     last = ap("m%d" % k + H)
-                if k == 2:
-                    mm([(SC, idf, blk("act", h, 256), True, False)])
+            HI = ap(PC, 256, 320)
+            nat = C["nat"] and t == 0
+            if not nat:
+                (act if "l" in C["sx"] else cp)(ap("ofl" + H), ap(lb, l0, l0 + 64))
+                mm([(HI, idf, ap("ofl" + H), True, False)])
             mm([(blk(PB, 2 + b), ap("m3" + H, b, 256, 2), idb, False, b == 1) for b in range(2)])
             scan(ap("rr" + H), ap("z16"), SC, A.add, A.min)
             tt(ap("ff" + H, 1, 256), ap("rr" + H, 0, 255), ap(PB, 257, 512), A.is_gt)
-            for b in range(2):
+            for b in range(0 if nat else 2):
                 tt(ap("zh" + H, 16 + b, 144, 16), ap("rr" + H, 128 * b + 7, 128 * b + 128, 16), ap("rr" + H, 128 * b + 15, 128 * b + 128, 16), A.is_gt)
             mm([(ap(PA, b, 256, 2), blk("ff" + H, b), idb, True, True) for b in range(2)])
-            act(ap("ft" + H), ap(PA, 0, 256), scale=col(8), bias=col(7))
-            mm([(ap(PB, 0, 64), idf, ap("ofl" + H), True, False)]
-               + [(ap(PB, 0, 64), ap("zh" + H, 16 - 2 * x, 144 - 2 * x), blk("hsel", x, 64), False, x == 7) for x in range(8)])
-            cp(ap("of2" + H), ap(PB, 0, 64))
-            mm([(ap(PA, 256, 512), ap("lm"), ap("ft" + H), True, True)])
+            act(ap("ft" + H), ap(PA, 0, 256), scale=col(8), bias=col(12))
+            if not nat:
+                mm([(HI, ap("zh" + H, 16 - 2 * x, 144 - 2 * x), blk("hsel", x, 64), False, x == 7) for x in range(8)])
+                (act if "2" in C["sx"] else cp)(ap("of2" + H), HI)
+            mm([(ap(PA, 256, 512), ap("lm0" if nat else "lm"), ap("ft" + H), True, True)])
             act(ap("msk" + H), ap(PA, 256, 512), F.Relu, scale=65536.0)
-            K, AA = ap(PA, 0, 128), ap(PB, 256, 384)
-            mm([(AA, ap("one", p1=2), ap("ca", p1=2), True, False)])
-            if t == 0:
-                mm([(K, ap("r0", 0, 128), ap("uc"), True, False)]
-                   + [(ap(PA, 64 * b, 64 * b + 64), ap("r0", b, 256, 2), blk("rm0", h, 64), False, False) for b in range(2)])
-            else:
-                mm([(K, blk("ri", 2 * (s - 2) + 1), ap("rm"), True, False)])
-            for k in range(4):
+            if t and C["late"][h]:
+                payload(t - 1, h, True)
+            AA = ap(PB, 256, 384)
+            mm([(AA, ap("one", p1=1), ap("ca", p1=1), True, False)])
+
+            def keys(bank, part):
+                K = ap(bank, 0, 128)
+                if part == 0 and t == 0:
+                    return ([(K, ap("r0", 0, 128), ap("uc"), True, False)]
+                            + [(ap(bank, 64 * b, 64 * b + 64), ap("r0", b, 256, 2), blk("rm0", h, 64), False, False) for b in range(2)])
+                if part == 0:
+                    return [(K, blk("ri", 2 * (s - 2) + 1), ap("rm"), True, False)]
+                if part == 1:
+                    return [(K, ap("i15"), ap("cst" + H), False, False)]
+                return [(K, idf, ap("af" + H), False, False)]
+
+            def closed(lst):
+                return lst[:-1] + [lst[-1][:4] + (True,)]
+
+            mm(keys(PA, 0))
+            for k in range(4 if nat else 0):
+                for u, table in enumerate((ap("xt", 0, 4096), ap("arc"))):
+                    n, o = (("gm" + H, 256 * k), ("smo", 1024 * (2 + h) + 256 * k))[u]
+                    tt(ap(n, o, o + 256), ind(table, ap(lb, l0 + 16 * k, l0 + 16 * k + 16)), ap("msk" + H), A.min)
+                    mm([(ap(PB, 256 + 64 * b + 4 * u + k, 320 + 64 * b, 8), ap(n, o + b, o + 256, 2), ap("bo0"), False, (k, u, b) == (3, 1, 1))
+                        for b in range(2)])
+            if nat and h == 1:
+                load("sw9", last_move, [ap("xt", 0, 4096)], 0, [ap("arc")], by=1 << 20)
+            for k in range(0 if nat else 4):
                 tt(blk("gm" + H, k, 256), ind(ap("xt"), blk("of2" + H, k, 16)), ap("msk" + H), A.min)
                 mm([(ap(PB, 256 + 64 * b + k, 320 + 64 * b, 4), ap("gm" + H, 256 * k + b, 256 * k + 256, 2), ap("bo2"), False, k == 3 and b == 1)
                     for b in range(2)])
-            act(ap("cst" + H), AA, bias=2.0 ** -13)
+            act(ap("cst" + H), AA, bias=0.5 - U / 2)
             act(ap("af" + H), AA)
-            mm([(K, ap("i15"), ap("cst" + H), False, False)])
-            mm([(K, ap("ids"), ap("af" + H), False, True)])
-            tt(ap("ds" + H), ap("cst" + H), AA, A.subtract)
-            xq, x0 = "xq" + H, "x0" + H
-
-            def costs(o, k0, k1):
-                act(o, ap("so" + H, 128 * k0 + 7, 128 * k1, 8), scale=-1.0 / 16, bias=130 + TOP / 16 - 0.4375)
+            mm(keys(PA, 1))
+            mm(closed(keys(PA, 2)))
+            tt(ap("ds" + H), AA, ap("cst" + H), A.subtract)
+            xx = "xx" + H
+            cost = dict(scale=-1.0 / (16 * U), bias=130 + TOP / 16 - 0.4)
 
             def lists(k):
                 mm([(ap(PB, 16 * k, 16 * k + 16), ap("zl" + H, 16 + 128 * k - 2 * x, 144 + 128 * k - 2 * x), ap("idq", x, 128, 8), x == 0, x == 7)
                     for x in range(8)])
 
-            def send(src, to, sem):
-                if t < NV - 1:
-                    def fn():
-                        a = topo.addr(nxt)
-                        g.remote_dma(R(to), R(src), T.sem[sem], T.sem.sent, a[1], a[0], emask(nxt, 0, 1)[0])
-                    n = emask(nxt, 0, 1)[1]
-                    op("G", fn, [src], [to], 700, dma=(sem, n), lat=NET - 600)
-                    sent[0] += n
-
             def states(k0, k1, sem):
                 c = (64 * s + 16 * k0, 64 * s + 16 * k1)
-                ts(ap("mo", *c), ap(PB, 16 * k0, 16 * k1), 2048.0, A.add)
-                send(ap("mo", *c), ap("mi", *c), sem)
+                if "m" in C["sx"]:
+                    act(ap("mo", *c), ap(PB, 16 * k0, 16 * k1), bias=2048.0)
+                else:
+                    ts(ap("mo", *c), ap(PB, 16 * k0, 16 * k1), 2048.0, A.add)
+                if t < NV - 1:
+                    write(nxt, ap("mo", *c), ap("mi", *c), sem)
+                    first[0] = len(ops) - 1
 
+            def residuals(bank, j, sem):
+                for p in (0, 64):
+                    o = ap(bank, 128, 256, p0=p, p1=p + 64)
+                    mm([(o, ap(xx, 48, 112), idb, True, False), (o, ap(xx, 0, 64), ap("idn"), False, True)])
+                act(blk("ro", j), ap(bank, 128, 256), F.Relu, scale=-1.0, bias=RB)
+                if t < NV - 1:
+                    write(nxt, blk("ro", j), blk("ri", j), sem)
+                    ops[-1]["soft"] = [first[0]]
+
+            kb = PA
+            two = C["tail"] if t == NV - 1 else C["parts"] == 2
+            strikes = 0 if t == NV - 1 and two else C["strikes"]
             for k in range(4):
+                K = ap(kb, 0, 128)
+                onpe = k < strikes
+                nb = PC if kb == PA else PA
+                if onpe and k == 0:
+                    mm(keys(nb, 0) + keys(nb, 1) + keys(nb, 2))
                 win, fl = ap("so" + H, 128 * k + 7, 128 * k + 128, 8), blk("fl" + H, k, 16)
-                scan(blk("so" + H, k), ap("z8"), K, A.min, A.max, 2 * TOP)
-                ts(fl, win, ROUND2, A.add, -ROUND2, A.add)
-                if k == 0:
-                    for j in range(3):
-                        costs(blk(x0, j, 16), 0, 1)
+                scan(blk("so" + H, k), ap("z8"), K, A.min, A.max, 2 * TOP * U)
+                if k + 1 < strikes:
+                    mm(keys(kb, 0) + keys(kb, 1) + keys(kb, 2)
+                       + [(K, ap("idk"), blk("eq" + H, j), False, False) for j in range(k)])
+                if not C["i32"]:
+                    cp(fl, win)
+                d = apx("sall" + H, k, every)
+                ts(d, win if C["i32"] else fl, int(U) - 1, an)
                 if k < 3:
-                    d = apx("sall" + H, k, every)
-                    tt(d, win, fl, A.subtract)
-                    tt(ap("eq" + H), ind(d, L1), ap("ds" + H), A.not_equal)
-                    tt(K, K, ap("eq" + H), A.mult)
-                for (k0, k1) in CONV:
+                    tt(blk("eq" + H, k), ind(d, L1), ap("ds" + H), A.is_equal if onpe else A.not_equal)
+                    if onpe:
+                        mm([(ap(nb, 0, 128), ap("idk"), blk("eq" + H, k), False, True)])
+                        if k + 1 < strikes:
+                            mm([(K, ap("idk"), blk("eq" + H, k), False, False)])
+                        kb = nb
+                    else:
+                        tt(K, K, blk("eq" + H, k), A.mult)
+                for k0, k1 in C["conv"]:
                     if k1 == k + 1:
                         for b in range(2):
-                            cp(ap("zl" + H, 16 + 128 * k0 + b, 16 + 128 * k1, 16), apx("sall" + H, slice(k0, k1), slice(8 * b, 8 * b + 8)))
-                        for j in range(k0, k1):
+                            o, i0 = ap("zl" + H, 16 + 128 * k0 + b, 16 + 128 * k1, 16), apx("sall" + H, slice(k0, k1), slice(8 * b, 8 * b + 8))
+                            if ("y" if k == 3 else "z") in C["sx"]:
+                                act(o, i0, bias=-U / 2)
+                            else:
+                                ts(o, i0, -U / 2, A.add)
+                        for j in range(k0, min(k1, 3)):
                             lists(j)
                 if k == 2:
-                    costs(ap(xq, 0, 32), 1, 3)
-                    if PARTS == 2:
+                    act(ap(xx, 0, 96), ind(ap("so" + H, 0, 384), LX), **cost)
+                    if two:
                         states(0, 3, "er%d" % s)
-                        if t < NV - 1:
-                            mm([(ap(PB, 128, 256), ap(xq), idb, True, False), (ap(PB, 128, 256), ap(x0), ap("idn"), False, True)])
-                            act(blk("ro", 2 * s), ap(PB, 128, 256), F.Relu, scale=-1.0, bias=GONE)
-                            send(blk("ro", 2 * s), blk("ri", 2 * s), "fr%d" % s)
-            for b in range(2):
-                tt(ap("zl" + H, 400 + b, 528, 16), ap("so" + H, 384 + 64 * b + 7, 448 + 64 * b, 8), ap("fl" + H, 48 + 8 * b, 56 + 8 * b), A.subtract)
-            costs(ap(xq, 32, 48), 3, 4)
+                        residuals(PB, 2 * s, "fr%d" % s)
+                        if t == NV - 1:
+                            payload(t, h, False, ((1, 2),), True)
+            act(ap(xx, 96, 112), ap("so" + H, 384 + 7, 512, 8), **cost)
             lists(3)
-            states(3 if PARTS == 2 else 0, 4, "ar%d" % s)
-            for p in (0, 64):
-                o = ap(PA, 128, 256, p0=p, p1=p + 64)
-                mm([(o, ap(xq, 0, 64), idb, True, False), (o, ap(x0, 0, 64), ap("idn"), False, True)])
-            rows = blk("ro", 2 * s + 1)
-            act(blk("ro", 2 * s + 1, p1=64), ap(PA, 128, 256, p1=64), F.Relu, scale=-1.0, bias=GONE)
-            act(blk("ro", 2 * s + 1, p0=64), ap(PA, 128, 256, p0=64), F.Sign, bias=0.5 - GONE)
-            send(rows, blk("ri", 2 * s + 1), "br%d" % s)
-            xs = [blk("smo", 4 * s + k, 256) for k in range(4)]
-            for k in range(4):
-                act(xs[k], ind(ap("payr"), ap("mo", 64 * s + 16 * k, 64 * s + 16 * k + 16)))
-            wb = [None, ap("pw0", 0, 256), ap("pw0", 256, 512), ap("pw1", 0, 256)]
-            for k in range(1, 4):
-                c = wb[k]
-                mm([(ap(c[0], c[1][0].start + b, c[1][0].stop, 2), blk("sel", 2 * k - 2 + b), rows, True, True) for b in range(2)])
-            act(ap("pw0"), ap("pw0"), F.Exp, scale=-0.125)
-            act(wb[3], wb[3], F.Exp, scale=-0.125)
-            for k in range(1, 4):
-                tt(xs[k] if t else wb[k], wb[k], xs[k], A.mult)
-            r = 16 * (t - (NV - 1)) % 128
-            turn = ap("idf", r, r + 128)
-            if t:
-                own = T.cores[(rank - t) % nr]
-                land = blk("smi", s - 2, 512)
-
-                def home(xs=xs, own=own, s=s):
-                    g.remote_dma_fused([
-                        RemoteDMATransfer(dst_ids=[dst(own)], dma_engine_mask=emask(own, k, 2)[0], remote_sem=T.sem["sm%d" % (s - 2)],
-                                          srcs=[R(x) for x in xs], dst=R(blk("smi", 2 * (s - 2) + k, 256)), alu_op=1 + k)
-                        for k in range(2)], local_sem=T.sem.sent)
-                n = 2 * emask(own, 0, 2)[1]
-                op("G", home, xs, [land], 3500, dma=("sm%d" % (s - 2), n), lat=NET)
-                sent[0] += n
-                if t < NV - 1:
-                    for k in range(2):
-                        mm([(blk("py" + H, k, 256), turn, blk("smi", 2 * (s - 2) + k, 256), False, t == NV - 2 and k == 1)])
-            else:
-                for j, o in enumerate((A.add, A.max)):
-                    a = blk("loc" + H, j, 256)
-                    for k in range(1, 4):
-                        tt(a, wb[k], xs[0] if k == 1 else a, o)
-                mm([(ap("py" + H), turn, ap("loc" + H), True, False)])
+            states(3 if two else 0, 4, "ar%d" % s)
+            if t == NV - 1 and two:
+                residuals(PB, 2 * s + 1, None)
+                payload(t, h, False, ((3,),))
+                continue
+            residuals(PC if kb == PA else PA, 2 * s + 1, "br%d" % s)
+            if t == NV - 1 or not C["late"][h]:
+                payload(t, h, False)
     r = 16 * NV % 128
     for h in range(2):
         cur[0] = h
@@ -430,7 +545,7 @@ def build(g, T, topo, rank):
             def store(o=o, j=2 * h + k, h=h):
                 g.sync.dma_start(o[128 - r:128, 256 * h:256 * h + 256], R(blk("yo", j, 256, p1=r))).then_inc(T.sem.stored, 16)
                 g.sync.dma_start(o[0:128 - r, 256 * h:256 * h + 256], R(blk("yo", j, 256, p0=r))).then_inc(T.sem.stored, 16)
-            op("Y", store, [a], [], 120, dma=("stored", 128), lat=2500)
+            op("Y", store, [a], [], (0, 0, 0, 120), dma=("stored", 128), lat=2500, by=1 << 17, nd=2)
     return ops, q, sent[0]
 
 
@@ -463,19 +578,67 @@ def link(ops):
 KEPT = {}
 
 
+def times(ops, m):
+    dur, pre, wire, post = [], [], [], []
+    for o in ops:
+        c, ga, n, ns = o["cost"][:4]
+        if "by" in o:
+            x = (m["di"] * o["nd"], m["di"] + 0.6 * m["dl"], o["by"] / m["rate"], 0.4 * m["dl"])
+        elif "rows" in o:
+            x = (n * m["g"], n * m["g"] + 0.6 * m["net"], o["rows"][0] * m["row"] + o["rows"][1] / m["rate"], 0.4 * m["net"])
+        else:
+            if len(o["cost"]) > 4 and o["cost"][4]:
+                ga *= max(m["ga"], m["tti"]) / m["ga"]
+            if o["eng"] == "G":
+                c, ns = 1.6 * c, 1.6 * ns
+            x = ((c + ga * m["ga"]) * m["cy"] + n * m[{"V": "v", "S": "s", "P": "m", "G": "g"}[o["eng"]]] + ns, 0.0, 0.0, m["hop"])
+        for lst, v in zip((dur, pre, wire, post), x):
+            lst.append(v)
+    return dur, pre, wire, post, m["hop"] - m["hs"]
+
+
+def replay(ops, seq, tm, at=None):
+    dur, pre, wire, post, near = tm
+    free, done, line, end = {e: 0.0 for e in "VSPGY"}, [0.0] * len(ops), 0.0, 0.0
+    for i in seq:
+        o = ops[i]
+        e = o["eng"]
+        a = free[e]
+        for j in o["other"]:
+            if done[j] > a:
+                a = done[j]
+        for j in o["own"]:
+            if done[j] - near > a:
+                a = done[j] - near
+        if at is not None:
+            at[i] = a
+        free[e] = b = a + dur[i]
+        if wire[i]:
+            line = max(a + pre[i], line) + wire[i]
+            b = max(b, line)
+        done[i] = b = b + post[i]
+        if b > end:
+            end = b
+    return end
+
+
 def order(ops, tries=TRIES):
     n = len(ops)
     kids = [[] for _ in ops]
     for i, o in enumerate(ops):
+        o["far"] = [j for j in o["deps"] if not (o["eng"] == "P" and ops[j]["eng"] == "P")]
+        o["own"] = [j for j in o["far"] if ops[j]["eng"] == o["eng"] and "dma" not in ops[j]]
+        o["other"] = [j for j in o["far"] if j not in o["own"]]
+        o["deps"] = sorted(set(o["deps"]) | set(o.get("soft", [])))
         for j in o["deps"]:
             kids[j].append(i)
     eng = [o["eng"] for o in ops]
-    dur = [o["dur"] for o in ops]
-    lat = [o["dur"] + o.get("lat", HOP) for o in ops]
+    tms = [times(ops, m) for m in GUESS]
+    dur, pre, wire, post, near = tms[0]
     tail = [0.0] * n
     for i in range(n - 1, -1, -1):
-        tail[i] = lat[i] + max([tail[k] for k in kids[i]], default=0.0)
-    fixed = [1e7 - 1e3 * i if eng[i] == "Y" else 0.0 for i in range(n)]
+        tail[i] = max(dur[i], pre[i] + wire[i]) + post[i] + max([tail[k] for k in kids[i]], default=0.0)
+    fixed = [1e9 - 1e6 * i if "soon" in o or "by" in o and not o["deps"] else 0.0 for i, o in enumerate(ops)]
 
     def run(pri, slack):
         left = [len(o["deps"]) for o in ops]
@@ -484,31 +647,35 @@ def order(ops, tries=TRIES):
         for i in range(n):
             if not left[i]:
                 ready[eng[i]].append(i)
-        free, seq, at, end = {e: 0.0 for e in ready}, [], [0.0] * n, 0.0
+        free, seq, at, line = {e: 0.0 for e in ready}, [], [0.0] * n, 0.0
         for _ in range(n):
             t0, e = min((max(free[e], min([rdy[i] for i in r])), e) for e, r in ready.items() if r)
             r = ready[e]
             i = max([j for j in r if rdy[j] <= t0], key=pri.get)
-            lim = t0 + (1.2 * dur[i] if e == "G" else min(slack, 0.5 * dur[i]))
+            lim = t0 + (1.2 * (dur[i] + wire[i]) if e == "G" else min(slack, 0.5 * dur[i]))
             soon = [j for j in r if t0 < rdy[j] <= lim and pri[j] > pri[i]]
             if soon:
                 i = max(soon, key=pri.get)
             r.remove(i)
             seq.append(i)
             a = at[i] = max(t0, rdy[i])
-            free[e] = a + dur[i]
-            end = max(end, a + lat[i])
+            free[e] = done = a + dur[i]
+            if wire[i]:
+                line = max(a + pre[i], line) + wire[i]
+                done = max(done, line)
+            done += post[i]
             for k in kids[i]:
-                rdy[k] = max(rdy[k], a + (dur[i] if e == "P" and eng[k] == "P" else lat[i]))
+                rdy[k] = max(rdy[k], done if i in ops[k]["other"] else done - near if i in ops[k]["own"] else a + dur[i])
                 left[k] -= 1
                 if not left[k]:
                     ready[eng[k]].append(k)
-        return end, seq, at
+        ends = [replay(ops, seq, tm) for tm in tms]
+        return sum(ends) / len(ends), seq, at, ends
 
     if "best" not in KEPT:
         rng = np.random.default_rng(7)
         best = None
-        for lag in (0.0, 4000.0, 8000.0, 12000.0):
+        for lag in (0.0, 2000.0, 4000.0, 8000.0):
             for slack in (0.0, 130.0, 300.0, 600.0):
                 pri = {i: tail[i] + fixed[i] - (lag if ops[i]["half"] == 1 else 0.0) for i in range(n)}
                 got = run(pri, slack)
@@ -516,7 +683,7 @@ def order(ops, tries=TRIES):
                     best = (got, pri, slack)
         for trial in range(tries):
             got, pri, slack = best
-            t = rng.random() * got[0]
+            t = rng.random() * got[3][0]
             new = dict(pri)
             span, amp = rng.choice([2000.0, 6000.0, 15000.0]), rng.choice([300.0, 1500.0, 6000.0])
             shift = {0: rng.normal() * amp, 1: 0.0, None: 0.0}
@@ -527,10 +694,10 @@ def order(ops, tries=TRIES):
             if tried[0] <= got[0]:
                 best = (tried, new, slack)
         KEPT["best"] = best[0]
-    end, seq, at = KEPT["best"]
+    end, seq, at, ends = KEPT["best"]
     for i in range(n):
         ops[i]["at"] = at[i]
-    return seq, end
+    return seq, ends
 
 
 def rank_program(g, core, T, topo):
@@ -542,16 +709,14 @@ def rank_program(g, core, T, topo):
     seq, _ = order(ops)
     used = set()
     for o in ops:
-        used.update(j for j in o["deps"] if not (o["eng"] == "P" and ops[j]["eng"] == "P"))
+        used.update(o["far"])
     count, seen = {}, {e: {} for e in q}
     for i in seq:
         o = ops[i]
         e = o["eng"]
         know = seen[e]
         need = {}
-        for j in o["deps"]:
-            if e == "P" and ops[j]["eng"] == "P":
-                continue
+        for j in o["far"]:
             sem, val = ops[j]["sig"]
             if know.get(sem, 0) < val and need.get(sem, (0, 0))[0] < val:
                 need[sem] = (val, j)

@@ -5,22 +5,23 @@ from concourse.mybir import ActivationFunctionType as F
 
 NV = 6
 CFG = dict(
-    parts=1,
-    mce="VSSS",
-    i32=True, conv=[(0, 2), (2, 3), (3, 4)],
-    strikes=0,
-    pay=("fuse", "fuse"), late=(True, True),
-    fold=(False, False),
-    si32=True, tail=True, q7="Y", sx="l2zm", own=False,
-    sw=[(0, 1536), (1536, 2816), (2816, 4096)], nat=False,
+    mce=("VSSS", "VSSS"),
+    conv=[(0, 2), (2, 3), (3, 4)],
+    late=("11110", "11111"),
+    fuse=("13", "13"), rb="C", pet="", hbm=1.0,
+    mcv=(2, 3, 4),
+    ch=[0, 512, 1536, 2816, 3840, 4096],
+    sw=[(0, 1536), (1536, 2816), (2816, 4096)],
+    lags=(1700.0, 2000.0, 2300.0, 2000.0), z3="VV", um=("", ""), pre="0", sx="l2", pes=("", ""),
 )
-CH = [0, 512, 1536, 2816, 3840, 4096]
-TRIES = 1500
+HOME = 4
+TRIES = 240
 SCRATCH = {}
 GONE = 106.0
 U = 4096.0
-TOP = 3584.0
-NONE = U * (TOP - 16 * 176) + 4095
+STEP, TOP = 12.0, 2176.0
+NONE = U * (TOP - STEP * 176) + 4095
+LIFT = 136.0
 
 
 def _sb(n, w, d, where="sbuf"):
@@ -28,40 +29,40 @@ def _sb(n, w, d, where="sbuf"):
 
 
 for _n, _w, _d in [
-        ("arc", 4096, "int32"), ("xt", 8192, "int32"), ("mn", 4096, "float32"),
-        ("mc", 4096, "bfloat16"), ("payr", 4096, "bfloat16"), ("acs", 512, "float32"), ("act", 512, "float32"),
+        ("arc", 4096, "int32"), ("xt", 8192, "int32"), ("mn", 4096, "float32"), ("mc", 4096, "bfloat16"),
+        ("payr", 4096, "bfloat16"), ("payo", 4096, "bfloat16"), ("acs", 512, "float32"), ("act", 512, "float32"),
         ("sti", (4, 32), "int32"), ("off0", 128, "uint16"), ("rsi", 256, "int32"), ("r0", 256, "bfloat16"),
-        ("ci", 48, "int32"), ("cf", 24, "float32"), ("bo0", 8, "float32"), ("lm0", 128, "bfloat16"), ("i16", 16, "float32"),
+        ("ci", 48, "int32"), ("cf", 24, "float32"), ("i16", 16, "float32"),
         ("onef", 256, "float32"), ("one", 128, "bfloat16"), ("idf", 256, "float32"), ("idb", 128, "bfloat16"),
-        ("idq", 128, "float16"), ("idn", 128, "bfloat16"), ("i15", 128, "bfloat16"),
-        ("idk", 128, "bfloat16"),
+        ("idq", 128, "float16"), ("idn", 128, "bfloat16"), ("idc", 128, "bfloat16"), ("idk", 128, "bfloat16"),
         ("bo2", 16, "float32"), ("lm", 128, "bfloat16"), ("hsel", 512, "bfloat16"), ("sel0", 1024, "bfloat16"),
         ("sell", 768, "bfloat16"), ("selp", 768, "bfloat16"),
         ("ua", 128, "bfloat16"), ("ub", 128, "bfloat16"), ("uc", 128, "bfloat16"), ("ud", 128, "bfloat16"),
         ("rm0", 128, "bfloat16"), ("rm", 128, "bfloat16"), ("ca", 128, "bfloat16"),
         ("lu", 32, "uint16"), ("z16", 256, "float32"), ("z8", 128, "float32"),
-        ("mo", 12 * 64, "uint16"), ("mi", 10 * 64, "uint16"), ("ro", 12 * 256, "bfloat16"), ("ri", 10 * 256, "bfloat16"),
-        ("smo", 12 * 1024, "float32"), ("smi", 10 * 512, "float32"), ("yo", 1024, "float32")]:
+        ("mo", 12 * 64, "uint16"), ("mi", 12 * 64, "uint16"), ("ro", 12 * 128, "bfloat16"), ("ri", 12 * 128, "bfloat16"),
+        ("smo", 12 * 1024, "float32"), ("smi", 8 * 512, "float32"), ("yo", 1024, "float32")]:
     _sb(_n, _w, _d)
 for _h in "01":
     for _n, _w, _d in [
             ("mcg", 1024, "bfloat16"), ("c0s", 256, "bfloat16"), ("m1", 256, "bfloat16"), ("m2", 256, "bfloat16"),
             ("m3", 256, "bfloat16"), ("rr", 256, "float32"), ("ff", 256, "bfloat16"), ("ft", 256, "bfloat16"),
             ("msk", 256, "bfloat16"), ("gm", 1024, "float32"), ("cst", 128, "bfloat16"), ("zh", 144, "bfloat16"),
-            ("ofl", 64, "float32"), ("of2", 64, "uint16"), ("ds", 128, "float32"), ("eq", 384, "bfloat16"),
-            ("so", 512, "int32" if CFG["i32"] else "float32"), ("fl", 64, "int32"), ("sall", (4, 16), "int32"), ("zl", 528, "float16"),
-            ("xx", 112, "bfloat16"), ("af", 128, "float32"), ("loc", 512, "float32"), ("wt", 768, "float32")]:
+            ("ofl", 64, "float32"), ("of2", 64, "uint16"), ("ds", 128, "float32"), ("eq", 128, "bfloat16"),
+            ("so", 512, "int32"), ("sall", (4, 16), "int32"), ("zl", 528, "float16"),
+            ("xx", 256, "bfloat16"), ("af", 128, "float32"), ("loc", 512, "float32"), ("wt", 768, "float32")]:
         _sb(_n + _h, _w, _d)
 for _n in ["pa0", "pb0", "pc0", "pa1", "pb1", "pc1", "py0", "py1"]:
     _sb(_n, 512, "float32", "psum")
 
-SEMAPHORES = (["cV", "cS", "cP", "cG", "sent", "stored"] + ["ld%d" % i for i in range(10)] + ["sw%d" % i for i in range(10)]
-              + ["%s%d" % (n, i) for n in ("ar", "br", "er", "fr", "sm") for i in range(10)])
+SEMAPHORES = (["cV", "cS", "cP", "cG", "sent", "stored"] + ["ld%d" % i for i in range(12)] + ["sw%d" % i for i in range(10)]
+              + ["%s%d" % (n, i) for n in ("ar", "br", "sm") for i in range(12)] + ["pp%d" % i for i in range(HOME)])
 
-GUESS = [dict(cy=0.86, ga=1.5, tti=0, v=20, s=60, m=12, g=300, hop=190, hs=100, net=1300, row=40, rate=350, dl=1500, di=180),
-         dict(cy=0.83, ga=1.2, tti=0, v=50, s=40, m=5, g=200, hop=260, hs=40, net=1000, row=20, rate=350, dl=1300, di=170),
-         dict(cy=0.86, ga=1.6, tti=2, v=0, s=20, m=5, g=470, hop=150, hs=60, net=3000, row=40, rate=500, dl=1000, di=230),
-         dict(cy=1.05, ga=1.8, tti=0, v=20, s=80, m=10, g=400, hop=150, hs=150, net=1400, row=60, rate=250, dl=2000, di=100)]
+GUESS = [dict(cy=0.86, ga=1.5, tti=0, v=20, s=150, m=12, g=400, hop=170, hs=100, net=1300, row=60, rate=350, dl=1500, di=180),
+         dict(cy=0.83, ga=1.2, tti=0, v=50, s=200, m=5, g=200, hop=200, hs=40, net=1000, row=30, rate=350, dl=1300, di=170),
+         dict(cy=0.86, ga=1.6, tti=2, v=0, s=60, m=5, g=600, hop=150, hs=60, net=2300, row=80, rate=500, dl=1000, di=230),
+         dict(cy=1.0, ga=2.05, tti=0, v=20, s=150, m=10, g=450, hop=150, hs=150, net=1400, row=60, rate=250, dl=2000, di=100)]
+ONCE = 3000.0
 
 
 def ap(b, c0=0, c1=None, st=1, p0=0, p1=128):
@@ -83,7 +84,7 @@ def ncol(a):
 
 def build(g, T, topo, rank):
     C = CFG
-    ops, cur = [], [None]
+    ops, cur, nth = [], [None], {}
     q = {"V": g.vector, "S": g.scalar, "P": g.tensor, "G": g, "Y": g.sync}
 
     def R(a):
@@ -99,40 +100,42 @@ def build(g, T, topo, rank):
         for a in rd:
             if isinstance(a, tuple):
                 flat += [a[1], a[2]] if a[0] == "ind" else [a]
-        ops.append(dict(half=cur[0], eng=eng, fn=fn, rd=flat, wr=wr, cost=cost, **kw))
+        key = (cur[0], eng, wr[0][0] if wr else None)
+        nth[key] = nth.get(key, 0) + 1
+        ops.append(dict(half=cur[0], kind=key + (nth[key],), eng=eng, fn=fn, rd=flat, wr=wr, cost=cost, **kw))
 
-    def vdur(out, ins, tt=False):
+    def vcost(out, ins, tt=False):
         n = ncol(out)
         if ins and ins[0][0] == "ind":
             return (0, n, 1, 30, tt)
         c = 0.5 if all(SCRATCH[a[0]][2] in ("bfloat16", "uint16", "float16") for a in [out] + ins) else 1.0
         if tt and not any(SCRATCH[a[0]][0] == "psum" for a in ins):
             c *= 2
-        return (max(64, n * c), 0, 1, 0)
+        return (max(64, n * c), 0, 1, 0, False)
 
     def tt(out, i0, i1, o):
-        op("V", lambda: g.vector.tensor_tensor(R(out), R(i0), R(i1), o), [i0, i1], [out], vdur(out, [i0, i1], True))
+        op("V", lambda: g.vector.tensor_tensor(R(out), R(i0), R(i1), o), [i0, i1], [out], vcost(out, [i0, i1], True))
 
     def ts(out, i0, s1, o0, s2=None, o1=None):
         if o1 is None:
             fn = lambda: g.vector.tensor_scalar(R(out), R(i0), R(s1), None, o0)
         else:
             fn = lambda: g.vector.tensor_scalar(R(out), R(i0), R(s1), R(s2), o0, o1)
-        op("V", fn, [i0, s1, s2], [out], vdur(out, [i0]))
+        op("V", fn, [i0, s1, s2], [out], vcost(out, [i0]))
 
     def cp(out, i0):
-        op("V", lambda: g.vector.tensor_copy(R(out), R(i0)), [i0], [out], vdur(out, [i0]))
+        op("V", lambda: g.vector.tensor_copy(R(out), R(i0)), [i0], [out], vcost(out, [i0]))
 
     def ms(out, v):
-        op("V", lambda: g.vector.memset(R(out), v), [], [out], vdur(out, []))
+        op("V", lambda: g.vector.memset(R(out), v), [], [out], vcost(out, []))
 
     def scan(out, d0, d1, o0, o1, first=0.0):
-        op("V", lambda: g.vector.tensor_tensor_scan(R(out), R(d0), R(d1), first, o0, o1), [d0, d1], [out], vdur(out, [d0, d1]))
+        op("V", lambda: g.vector.tensor_tensor_scan(R(out), R(d0), R(d1), first, o0, o1), [d0, d1], [out], vcost(out, [d0, d1]))
 
-    def act(out, i0, f=F.Identity, bias=0.0, scale=1.0):
+    def act(out, i0, f=F.Identity, bias=0.0, scale=1.0, more=0):
         n = ncol(out)
         op("S", lambda: g.scalar.activation(R(out), R(i0), f, bias=R(bias), scale=R(scale)), [i0, bias, scale], [out],
-           (0, n, 1, 0) if i0[0] == "ind" else (n, 0, 1, 0))
+           (0, n, 0, 75, False) if i0[0] == "ind" else (n, 0, 1, more, False))
 
     def mm(lst):
         def fn():
@@ -141,149 +144,140 @@ def build(g, T, topo, rank):
                 h = g.tensor.matmul(R(o), R(l), R(r), s0, s1)
             return h
         d = sum(max(min(64, ncol(l)), ncol(r)) * (2 if SCRATCH[l[0]][2] == "float32" else 0.5) for (o, l, r, s0, s1) in lst)
-        op("P", fn, [x[1] for x in lst] + [x[2] for x in lst], [x[0] for x in lst], (d, 0, len(lst), 30))
+        op("P", fn, [x[1] for x in lst] + [x[2] for x in lst], [x[0] for x in lst], (d, 0, len(lst), 30, False))
 
     def iota(out, pat, base, cmul):
         if SCRATCH[out[0]][2] == "int32":
             fn = lambda: g.iota(R(out), pat, base, cmul)
         else:
             fn = lambda: g.iota(R(out), pat, base, cmul, allow_small_or_imprecise_dtypes=True)
-        op("G", fn, [], [out], (2 * ncol(out), 0, 0, 130))
+        op("G", fn, [], [out], (3.2 * ncol(out), 0, 0, 210, False))
 
     def asel(out, i0, pat, o, base, cmul, fill=0.0):
-        op("G", lambda: g.affine_select(R(out), R(i0), pat, o, fill, base, cmul), [i0], [out], (2 * ncol(out), 0, 0, 170))
+        op("G", lambda: g.affine_select(R(out), R(i0), pat, o, fill, base, cmul), [i0], [out], (3.2 * ncol(out), 0, 0, 270, False))
 
     def paint(x, pat, base, v):
         asel(x, x, pat, A.not_equal, base, -1, v)
 
-    def load(sem, pairs, wr, lat, rd=(), e="Y", by=0):
+    def load(sem, pairs, wr, by, rd=()):
         def fn():
             for (o, i) in pairs:
-                q[e].dma_start(o, i).then_inc(T.sem[sem], 16)
-        op(e, fn, list(rd), wr, (0, 0, 0, 80 * len(pairs)), dma=(sem, 16 * len(pairs)), lat=lat, by=by, nd=len(pairs))
+                g.sync.dma_start(o, i).then_inc(T.sem[sem], 16)
+        op("Y", fn, list(rd), wr, None, dma=(sem, 16 * len(pairs)), by=by / (C["hbm"] if sem[0] == "l" else 1), nd=len(pairs))
+
+    def turned(sem, c0, c1):
+        load(sem, [(T.payr[16:128, c0:c1], T.pay[0:112, c0:c1]), (T.payr[0:16, c0:c1], T.pay[112:128, c0:c1])], [ap("payr", c0, c1)],
+             256 * (c1 - c0))
 
     ind = lambda w, o: ("ind", w, o)
     col = lambda j: ap("cf", j, j + 1)
     blk = lambda n, j, w=128, p0=0, p1=128: ap(n, w * j, w * j + w, p0=p0, p1=p1)
     every = slice(None)
+    CH, PW = C["ch"], 4096 // HOME
 
     for i in range(len(CH) - 1):
-        load("ld%d" % i, [(T.arc[:, CH[i]:CH[i + 1]], T.arcs[:, CH[i]:CH[i + 1]])], [ap("arc", CH[i], CH[i + 1])], 2200 + 2.2 * CH[i + 1],
-             by=512 * (CH[i + 1] - CH[i]))
-    load("ld7", [(T.sti[:], T.st0[:])] + [(T.rsi[8 * j:8 * j + 8, :], T.rs0[:, 256 * j:256 * j + 256]) for j in range(8)],
-         [apx("sti", every, every), ap("rsi")], 2500, by=1 << 17, e=C["q7"])
-    load("ld6", [(T.acs[:], T.ac[:])], [ap("acs")], 12500, by=1 << 18)
+        load("ld%d" % i, [(T.arc[:, CH[i]:CH[i + 1]], T.arcs[:, CH[i]:CH[i + 1]])], [ap("arc", CH[i], CH[i + 1])], 512 * (CH[i + 1] - CH[i]))
+    load("ld8", [(T.sti[:], T.st0[:])] + [(T.rsi[8 * j:8 * j + 8, :], T.rs0[:, 256 * j:256 * j + 256]) for j in range(8)],
+         [apx("sti", every, every), ap("rsi")], 1 << 17)
+    load("ld9", [(T.acs[:], T.ac[:])], [ap("acs")], 1 << 18)
+    turned("ld10", 0, PW)
 
     start = len(ops)
     ms(ap("onef"), 1.0)
     idf, idb = ap("idf", 0, 128), ap("idb")
     iota(ap("ci", 0, 2), [[16, 2]], 0, 1)
-    iota(ap("ci", 8, 16), [[2, 8]], 0, 0)
-    iota(ap("ci", 16, 19), [[0, 3]], 7, 0)
-    iota(ap("ci", 19, 22), [[128, 3]], 7, 0)
-    iota(ap("i16"), [[1, 16]], 0, 0)
+    iota(ap("ci", 2, 3), [[0, 1]], 1, 1)
     asel(idf, ap("onef", 0, 128), [[-1, 128]], A.is_equal, 0, 1)
     iota(ap("lm"), [[1, 8], [0, 16]], 0, 0)
     iota(ap("ua"), [[0, 16], [1, 8]], 0, 0)
     iota(ap("ub"), [[1, 16], [0, 2], [16, 4]], 0, 0)
-    for n in ("uc", "sel0", "hsel", "zl0", "zl1"):
+    iota(ap("i16"), [[1, 16]], 0, 0)
+    iota(ap("ci", 8, 16), [[2, 8]], 0, 0)
+    iota(ap("ci", 32, 40), [[0, 8]], 7, 0)
+    iota(ap("ci", 40, 48), [[0, 2], [128, 4]], 7, 0)
+    for n in ("uc", "sel0", "hsel"):
         ms(ap(n), 0.0)
     ms(ap("r0", p0=64), 1.0)
-    for n in ("ff0", "ff1", "zh0", "zh1", "xx0", "xx1"):
-        act(ap(n), ap("onef", 0, SCRATCH[n][1][1]), scale=0.0)
+    for n, w in (("ff0", 1), ("ff1", 1), ("zh0", 144), ("zh1", 144)):
+        ms(ap(n, 0, w), 0.0)
     act(ap("one"), ap("onef", 0, 128))
     act(ap("idf", 128, 256), idf)
-    for n, v in (("idb", 1.0), ("i15", -17.0), ("idn", -1.0), ("idk", -U * U)):
+    for n, v in (("idb", 1.0), ("idc", -1.0 - STEP), ("idn", -1.0)):
         act(ap(n), idf, scale=v)
     cp(ap("idq"), idf)
     sh, an = A.logical_shift_right, A.bitwise_and
-    ts(ap("ci", 2, 3), ap("ci", 1, 2), 3, sh, 15, an)
-    ts(ap("ci", 3, 4), ap("ci", 0, 1), 3, sh, 1, an)
-    ts(ap("ci", 4, 5), ap("ci", 0, 1), 4, sh)
-    ts(ap("ci", 5, 6), ap("ci", 0, 1), 15, an)
-    ts(ap("ci", 6, 7), ap("ci", 0, 1), 4, sh, 3, an)
-    ts(ap("ci", 7, 8), ap("ci", 0, 1), 6, sh)
-    cp(ap("cf", 0, 8), ap("ci", 0, 8))
-    PN, NEXT, Q8 = col(0), col(2), col(3)
+    P0, P16 = ap("ci", 0, 1), ap("ci", 1, 2)
+    for j, (src, s, m) in enumerate([(P0, 0, 15), (P16, 3, 15), (P0, 3, 1), (P0, 4, 7), (P0, 4, 3), (P0, 6, 1), (P0, 0, 7), (P0, 0, 56),
+                                     (ap("ci", 2, 3), 0, 7)]):
+        ts(ap("ci", 16 + j, 17 + j), src, s, sh, m, an)
+    cp(ap("cf", 0, 8), ap("ci", 16, 24))
+    LABEL, NEXT, UPPER, GROUP, SLOT, SECOND, LOW3 = [col(j) for j in range(7)]
+    ROW = col(21)
+    ts(ROW, ap("ci", 24, 25), col(7), A.add)
+    act(col(11), LABEL, F.Exp, scale=0.8, more=1300)
     ts(ap("bo2"), ap("i16"), NEXT, A.is_equal)
-    ts(ap("lu", 0, 8), ap("ci", 8, 16), Q8, A.add)
-    act(col(9), col(5), scale=8.0)
-    ts(ap("lu", 8, 14), ap("ci", 16, 22), col(9), A.add)
-    L1, LX = ap("lu", 0, 8), ap("lu", 8, 14)
-    act(ap("ca", p1=1), ap("onef", 0, 128, p1=1), scale=160 * U)
+    ts(ap("lu", 0, 8), ap("ci", 8, 16), UPPER, A.add)
+    act(col(9), LABEL, scale=8.0)
+    ts(ap("lu", 8, 24), ap("ci", 32, 48), col(9), A.add, 383.0, A.min)
+    L1, LX = ap("lu", 0, 8), ap("lu", 8, 24)
+    act(ap("ca", p1=1), ap("onef", 0, 128, p1=1), scale=LIFT * U)
     act(ap("z16"), ap("onef"), scale=0.0)
     act(ap("z16", 0, 256, 16), ap("onef", 0, 16), scale=1000.0)
     act(ap("z8"), ap("onef", 0, 128), scale=2 * TOP * U)
     act(ap("z8", 0, 128, 8), ap("onef", 0, 16), scale=NONE)
-    ts(ap("lm"), ap("lm"), col(4), A.is_equal, -1.0, A.mult)
-    ts(ap("ci", 22, 23), ap("ci", 1, 2), 4, sh, 7, an)
-    ts(ap("ci", 23, 24), ap("ci", 0, 1), 7, an)
-    ts(ap("ci", 24, 25), ap("ci", 0, 1), 63, an)
-    cp(ap("cf", 16, 19), ap("ci", 22, 25))
-    act(col(11), col(5), F.Exp, scale=0.8)
-    ops[-1]["cost"] = (1, 0, 1, 1300)
-    if C["nat"]:
-        asel(ap("lm0"), ap("lm"), [[1, 128]], A.not_equal, 0, -1, 1.0)
-        act(ap("lm0"), ap("lm0"), scale=col(11))
-        ts(ap("bo0"), ap("i16", 0, 8), col(16), A.is_equal)
-    ts(ap("ua"), ap("ua"), col(17), A.not_equal, 0.5, A.subtract)
+    ts(ap("lm"), ap("lm"), GROUP, A.is_equal, -1.0, A.mult)
+    ts(ap("ua"), ap("ua"), LOW3, A.not_equal, 0.5, A.subtract)
     tt(ap("lm"), ap("lm"), ap("ua"), A.mult)
     act(ap("lm"), ap("lm"), scale=col(11))
-    ts(col(12), col(5), 0.0, A.is_equal)
+    ts(col(12), LABEL, 0.0, A.is_equal)
     act(col(8), col(12), scale=-1.0, bias=1.0)
-    ts(col(13), col(6), 0.0, A.is_gt)
-    act(col(14), col(7), scale=-1.0, bias=GONE - 1)
+    ts(col(13), SLOT, 0.0, A.is_gt)
+    act(col(14), SECOND, scale=-1.0, bias=GONE - 1)
     act(col(15), col(13), scale=col(14), bias=1.0)
     RB = col(15)
-    ms(ap("uc", p0=64, p1=66), (TOP + 2560) * U)
-    iota(ap("ud"), [[0, 16], [-2 * int(U), 8]], 0, 0)
+    ms(ap("uc", p0=64, p1=66), (TOP + STEP * LIFT) * U)
+    iota(ap("ud"), [[0, 16], [-int(U), 8]], 0, 0)
     act(ap("uc", p0=64, p1=65), ap("ud", p0=64, p1=65))
     paint(ap("sel0"), [[1, 64], [0, 16]], 0, 1.0)
-    paint(ap("hsel"), [[1, 8], [0, 4], [8, 16]], 0, 4096.0)
-    act(col(19), col(7), scale=16 * U, bias=-16 * U)
-    act(col(20), col(7), scale=16 * U * 83, bias=-16 * U * 41)
-    ts(ap("ua"), ap("ub"), col(18), A.is_equal, col(19), A.mult)
-    ts(ap("ub"), ap("ub"), col(18), A.is_equal, col(20), A.mult)
-    act(ap("ub", p1=1), ap("onef", 0, 128, p1=1), scale=-16 * U * 64)
+    paint(ap("hsel"), [[1, 8], [0, 4], [8, 16]], 0, U)
+    act(col(19), SECOND, scale=STEP * U, bias=-STEP * U)
+    act(col(20), SECOND, scale=STEP * U * 83, bias=-STEP * U * 41)
+    ts(ap("rm0"), ap("ub"), ROW, A.is_equal, col(19), A.mult)
+    ts(ap("ub"), ap("ub"), ROW, A.is_equal, col(20), A.mult)
+    act(ap("ub", p1=1), ap("onef", 0, 128, p1=1), scale=-STEP * U * 64)
     act(ap("ub", 0, 128, 4), ap("onef", 0, 32), scale=0.0)
-    tt(ap("ub"), ap("ub"), ap("uc"), A.add)
-    for (n, u) in (("rm0", "ua"), ("rm", "ub")):
-        for b in range(2):
-            act(ap(n, 64 * b + 8, 64 * b + 64), ap(u, 64 * b, 64 * b + 56))
-            act(ap(n, 64 * b, 64 * b + 8), ap(u, 64 * b + 56, 64 * b + 64))
+    tt(ap("rm"), ap("ub"), ap("uc"), A.add)
     for i in range(start, len(ops)):
         ops[i]["soon"] = True
+    for n in ("zl0", "zl1"):
+        iota(ap(n), [[0, 528]], 0, 0)
     act(ap("sell"), ap("sel0", 256, 1024), scale=-1.0)
     act(ap("selp"), ap("sel0", 256, 1024), scale=41.0)
     paint(ap("selp"), [[1, 48], [0, 16]], 80, -42.0)
     for n, v in (("sell", GONE), ("selp", 64.0)):
         paint(ap(n), [[0, 768]], 0, v)
-    banks, turn_no = ["pa0", "pa1", "pb0", "pb1", "pc0", "pc1"], [0]
+    banks, used, start = ["pa0", "pa1", "pb0", "pb1", "pc0", "pc1"], 0, len(ops)
     for i in range(len(CH) - 1):
         c = (CH[i], CH[i + 1])
         ts(ap("xt", *c), ap("arc", *c), 32767, an)
         ts(ap("arc", *c), ap("arc", *c), 15, sh)
-        if C["si32"]:
-            for c0 in range(c[0], c[1], 512):
-                c1 = min(c0 + 512, c[1])
-                b = ap(banks[turn_no[0] % 6], 0, c1 - c0)
-                turn_no[0] += 1
-                act(b, ap("arc", c0, c1))
-                tt(ap("mn", c0, c1), b, ap("xt", c0, c1), A.min)
+        for c0 in range(c[0], c[1], 512):
+            c1 = min(c0 + 512, c[1])
+            b = ap(banks[used % len(banks)], 0, c1 - c0)
+            used += 1
+            act(b, ap("arc", c0, c1))
+            tt(ap("mn", c0, c1), b, ap("xt", c0, c1), A.min)
+        if i in C["mcv"]:
+            ts(ap("mc", *c), ap("mn", *c), 1 / U, A.mult, 159.5 + 0.5 / U, A.add)
         else:
-            tt(ap("mn", *c), ap("xt", *c), ap("arc", *c), A.min)
-        act(ap("mc", *c), ap("mn", *c), bias=159.5 + 2.0 ** -13, scale=2.0 ** -12)
+            act(ap("mc", *c), ap("mn", *c), bias=159.5 + 0.5 / U, scale=1 / U)
     for i, (c0, c1) in enumerate(C["sw"]):
         lo = lambda n, k, o: T[n][16 * k:16 * k + 8, o + c0:o + c1]
         hi = lambda n, k, o: T[n][16 * k + 8:16 * k + 16, o + c0:o + c1]
         load("sw%d" % (2 * i), [(lo("xt", k, 4096), hi("xt", k, 0)) for k in range(8)] + [(hi("xt", k, 4096), hi("arc", k, 0)) for k in range(8)],
-             [ap("xt", 4096 + c0, 4096 + c1)], 2200 + 2.2 * (c1 - c0), [ap("xt", c0, c1), ap("arc", c0, c1)], by=512 * (c1 - c0))
-        last_move = [(hi("xt", k, 0), lo("arc", k, 0)) for k in range(8)]
-        if not C["nat"]:
-            load("sw%d" % (2 * i + 1), last_move, [ap("xt", c0, c1)], 2200 + 1.1 * (c1 - c0), [ap("arc", c0, c1)], by=256 * (c1 - c0))
-    c0, c1 = 0, 4096
-    last_move = [(hi("xt", k, 0), lo("arc", k, 0)) for k in range(8)]
-    load("ld8", [(T.payr[16:128, :], T.pay[0:112, :]), (T.payr[0:16, :], T.pay[112:128, :])], [ap("payr")], 9000, by=1 << 20)
+             [ap("xt", 4096 + c0, 4096 + c1)], 512 * (c1 - c0), [ap("xt", c0, c1), ap("arc", c0, c1)])
+        load("sw%d" % (2 * i + 1), [(hi("xt", k, 0), lo("arc", k, 0)) for k in range(8)], [ap("xt", c0, c1)], 256 * (c1 - c0), [ap("arc", c0, c1)])
+    turned("ld11", PW, 4096)
     ops[-1]["soft"] = [len(ops) - 2]
     act(ap("r0", p1=64), ap("rsi", p1=64))
     for h in range(2):
@@ -291,11 +285,12 @@ def build(g, T, topo, rank):
         bank = "py%d" % h
         for b in range(2):
             o, i = blk(bank, b), ap("acs", 256 * h + b, 256 * h + 256, 2)
-            op("P", lambda o=o, i=i: g.tensor.transpose(R(o), R(i), R(idf)), [i, idf], [o], (256, 0, 1, 30))
+            op("P", lambda o=o, i=i: g.tensor.transpose(R(o), R(i), R(idf)), [i, idf], [o], (256, 0, 1, 30, False))
         act(blk("act", h, 256), ap(bank, 0, 256))
 
     nr = len(T.cores)
     me, nxt = T.cores[rank], T.cores[(rank + 1) % nr]
+    last = T.cores[(rank - (NV - 1)) % nr]
 
     def dst(c):
         a = topo.addr(c)
@@ -306,31 +301,36 @@ def build(g, T, topo, rank):
         k = len(e) // of
         return int(sum(1 << x for x in e[part * k:part * k + k])), k
 
-    sent, first = [0], [0]
+    sent = [0]
 
-    def write(core, src, to, sem):
+    def write(core, src, to, sem, after=()):
         def fn():
             a = topo.addr(core)
             g.remote_dma(R(to), R(src), T.sem[sem], T.sem.sent, a[1], a[0], emask(core, 0, 1)[0])
         n = emask(core, 0, 1)[1]
-        op("G", fn, [src], [to], (0, 0, 1, 0), dma=(sem, n), rows=(8, 128 * ncol(src) * (4 if SCRATCH[src[0]][2] == "float32" else 2)))
+        op("G", fn, [src] + list(after), [to], (0, 0, 1, 0, False), dma=(sem, n), rows=(8, 256 * ncol(src)))
         sent[0] += n
 
-    def payload(t, h, late, steps=((1, 2), (3,)), early=False):
+    def features(j, after=()):
+        write(last, blk("payr", j, PW), blk("payo", j, PW), "pp%d" % j, after)
+
+    def payload(t, h, late):
         H, s = str(h), 2 * t + h
         cur[0] = h
         PA, PC = "pa" + H, "pc" + H
-        rows = blk("ro", 2 * s + (0 if early else 1))
-        folded = t > 0 and (t < NV - 1 or C["fold"][h])
-        fuse = folded and C["pay"][h] == "fuse"
+        home = t == NV - 1
+        pet = home and H in C["pet"]
+        rows = blk("ri" if home else "ro", s)
         xs = [blk("smo", 4 * s + k, 256) for k in range(4)]
-        lst = [ind(ap("payr"), ap("mo", 64 * s + 16 * k, 64 * s + 16 * k + 16)) for k in range(4)]
+        lst = [ind(ap("payo" if home else "payr"), blk("mi" if home else "mo", 4 * s + k, 16)) for k in range(4)]
         wb = [None, ap(PC, 0, 256), ap(PC, 256, 512), ap(PC, 0, 256) if late else ap(PA, 256, 512)]
         loc = [blk("loc" + H, j, 256) for j in range(2)]
-        for ks in steps:
-            for k in ((0,) if ks[0] == 1 else ()) + (() if fuse else ks):
-                act(xs[k], lst[k])
+        act(xs[0], lst[0])
+        for ks in ((1, 2), (3,)):
+            fuse = not home and str(ks[0]) in C["fuse"][h]
             for k in ks:
+                if not fuse:
+                    act(xs[k], lst[k])
                 c = wb[k]
                 mm([(ap(c[0], c[1][0].start + b, c[1][0].stop, 2), blk("selp", 2 * k - 2 + b), rows, True, True) for b in range(2)])
             w = ap(PC) if ks[0] == 1 else wb[3]
@@ -339,213 +339,178 @@ def build(g, T, topo, rank):
                 if fuse:
                     tt(xs[k], lst[k], blk("wt" + H, k - 1, 256), A.mult)
                 else:
-                    tt(xs[k] if folded else wb[k], wb[k], xs[k], A.mult)
-            if not folded:
+                    tt(wb[k] if home and not pet else xs[k], wb[k], xs[k], A.mult)
+            if pet:
+                for k in range(3 if ks[0] == 1 else 0):
+                    mm([(ap("py" + H, 0, 256), idf, xs[k], False, k == 2)])
                 for k in ks:
-                    for j, o in enumerate((A.add, A.max)):
-                        tt(loc[j], wb[k], xs[0] if k == 1 else loc[j], o)
-        if early:
+                    tt(loc[1] if k == 3 else wb[1], xs[0] if k == 1 else wb[1], xs[k], A.max)
+            for k in ks if home and not pet else ():
+                if H in C["pre"]:
+                    if k == 1:
+                        tt(loc[0], ap("py" + H, 0, 256), xs[0], A.add)
+                    tt(loc[0] if k < 3 else blk("yo", 2 * h, 256), wb[k], loc[0], A.add)
+                else:
+                    tt(loc[0], wb[k], xs[0] if k == 1 else loc[0], A.add)
+                tt(loc[1], wb[k], xs[0] if k == 1 else loc[1], A.max)
+        if home:
             return
         r = 16 * (t - (NV - 1)) % 128
         turn = ap("idf", r, r + 128)
-        own = T.cores[(rank - t) % nr]
-        land = blk("smi", s - 2, 512)
         if t == 0:
-            mm([(ap("py" + H), turn, ap("loc" + H), True, False)])
+            for k in range(4):
+                mm([(ap("py" + H, 0, 256), turn, xs[k], k == 0, False)])
+            for k in range(1, 4):
+                tt(loc[1], xs[k], xs[0] if k == 1 else loc[1], A.max)
+            mm([(ap("py" + H, 256, 512), turn, loc[1], False, False)])
             return
-        if folded:
-            def home():
-                g.remote_dma_fused([
-                    RemoteDMATransfer(dst_ids=[dst(own)], dma_engine_mask=emask(own, k, 2)[0], remote_sem=T.sem["sm%d" % (s - 2)],
-                                      srcs=[R(x) for x in xs], dst=R(blk("smi", 2 * (s - 2) + k, 256)), alu_op=1 + k)
-                    for k in range(2)], local_sem=T.sem.sent)
-            n = 2 * emask(own, 0, 2)[1]
-            op("G", home, xs, [land], (0, 0, 1.5, 0), dma=("sm%d" % (s - 2), n), rows=(24, 400000))
-            sent[0] += n
-        else:
-            write(own, ap("loc" + H), land, "sm%d" % (s - 2))
-        if t < NV - 1:
-            for k in range(2):
-                mm([(blk("py" + H, k, 256), turn, blk("smi", 2 * (s - 2) + k, 256), False, t == NV - 2 and k == 1)])
+        own = T.cores[(rank - t) % nr]
 
+        def fold():
+            g.remote_dma_fused([
+                RemoteDMATransfer(dst_ids=[dst(own)], dma_engine_mask=emask(own, k, 2)[0], remote_sem=T.sem["sm%d" % s],
+                                  srcs=[R(x) for x in xs], dst=R(blk("smi", 2 * (s - 2) + k, 256)), alu_op=1 + k)
+                for k in range(2)], local_sem=T.sem.sent)
+        n = 2 * emask(own, 0, 2)[1]
+        op("G", fold, xs, [blk("smi", s - 2, 512)], (0, 0, 1.5, 0, False), dma=("sm%d" % s, n), rows=(24, 400000))
+        sent[0] += n
+        for k in range(2):
+            mm([(blk("py" + H, k, 256), turn, blk("smi", 2 * (s - 2) + k, 256), False, t == NV - 2 and k == 1 and H not in C["pet"])])
+
+    features(0)
     for t in range(NV):
         for h in range(2):
             H = str(h)
             cur[0] = h
             PA, PB, PC = "pa" + H, "pb" + H, "pc" + H
             s = 2 * t + h
+            nth.clear()
             lb, l0 = ("off0", 64 * h) if t == 0 else ("mi", 64 * (s - 2))
+            rin = blk("ri", s - 2) if t else None
+            if h == 1 and 0 < t < HOME:
+                features(t, [rin])
             SC = ap(PB, 256, 512)
             mm([(SC, idf, blk("act", h, 256), True, False)])
             for k in range(4):
                 i0 = ind(ap("mc"), ap(lb, l0 + 16 * k, l0 + 16 * k + 16))
-                if C["mce"][k] == "S":
+                if C["mce"][h][k] == "S":
                     act(blk("mcg" + H, k, 256), i0, bias=-160.0)
                 else:
                     ts(blk("mcg" + H, k, 256), i0, -160.0, A.add)
             cbank = [ap("py" + H, 0, 256), ap(PA, 0, 256), ap(PC, 0, 256), ap(PA, 256, 512)]
-            last = blk("mcg" + H, 0, 256)
+            low = blk("mcg" + H, 0, 256)
             for k in range(1 if t else 0, 4):
                 c = cbank[k]
                 lst = [(c, idb, blk("mcg" + H, k, 256), True, False)]
                 if t == 0:
                     lst.append((c, blk("sel0", 2 * k + h, p1=64), ap("r0", p1=64), False, True))
                 else:
-                    x = blk("ri", 2 * (s - 2) + (0 if C["parts"] == 2 and k < 3 else 1), p1=64)
                     for b in range(2):
-                        lst.append((ap(c[0], c[1][0].start + b, c[1][0].stop, 2), blk("sell", 2 * k - 2 + b, p1=64), x, False, b == 1))
+                        lst.append((ap(c[0], c[1][0].start + b, c[1][0].stop, 2), blk("sell", 2 * k - 2 + b, p1=64), blk("ri", s - 2, p1=64),
+                                    False, b == 1))
                 mm(lst)
                 if k == 0:
-                    last = ap("c0s" + H)
-                    act(last, c)
+                    low = ap("c0s" + H)
+                    cp(low, c)
                 else:
-                    tt(ap("m%d" % k + H), c, last, A.min)
-                    last = ap("m%d" % k + H)
+                    tt(ap("m%d" % k + H), c, low, A.min)
+                    low = ap("m%d" % k + H)
             HI = ap(PC, 256, 320)
-            nat = C["nat"] and t == 0
-            if not nat:
-                (act if "l" in C["sx"] else cp)(ap("ofl" + H), ap(lb, l0, l0 + 64))
-                mm([(HI, idf, ap("ofl" + H), True, False)])
+            (act if "l" in C["sx"] else cp)(ap("ofl" + H), ap(lb, l0, l0 + 64))
+            mm([(HI, idf, ap("ofl" + H), True, False)])
             mm([(blk(PB, 2 + b), ap("m3" + H, b, 256, 2), idb, False, b == 1) for b in range(2)])
             scan(ap("rr" + H), ap("z16"), SC, A.add, A.min)
             tt(ap("ff" + H, 1, 256), ap("rr" + H, 0, 255), ap(PB, 257, 512), A.is_gt)
-            for b in range(0 if nat else 2):
+            for b in range(2):
                 tt(ap("zh" + H, 16 + b, 144, 16), ap("rr" + H, 128 * b + 7, 128 * b + 128, 16), ap("rr" + H, 128 * b + 15, 128 * b + 128, 16), A.is_gt)
             mm([(ap(PA, b, 256, 2), blk("ff" + H, b), idb, True, True) for b in range(2)])
             act(ap("ft" + H), ap(PA, 0, 256), scale=col(8), bias=col(12))
-            if not nat:
-                mm([(HI, ap("zh" + H, 16 - 2 * x, 144 - 2 * x), blk("hsel", x, 64), False, x == 7) for x in range(8)])
-                (act if "2" in C["sx"] else cp)(ap("of2" + H), HI)
-            mm([(ap(PA, 256, 512), ap("lm0" if nat else "lm"), ap("ft" + H), True, True)])
-            act(ap("msk" + H), ap(PA, 256, 512), F.Relu, scale=65536.0)
-            if t and C["late"][h]:
+            mm([(HI, ap("zh" + H, 16 - 2 * x, 144 - 2 * x), blk("hsel", x, 64), False, x == 7) for x in range(8)])
+            (act if "2" in C["sx"] else cp)(ap("of2" + H), HI)
+            mm([(ap(PA, 256, 512), ap("lm"), ap("ft" + H), True, True)])
+            um = C["um"][h]
+            if len(um) < 4:
+                act(ap("msk" + H), ap(PA, 256, 512), F.Relu, scale=65536.0)
+            if um:
+                act(ap(PA, 256, 512), ap(PA, 256, 512), F.Relu, scale=65536.0)
+            for k in um:
+                act(blk("gm" + H, int(k), 256), ind(ap("xt"), blk("of2" + H, int(k), 16)))
+            for k in um:
+                tt(blk("gm" + H, int(k), 256), ap(PA, 256, 512), blk("gm" + H, int(k), 256), A.min)
+            if t and C["late"][h][t - 1] == "1":
                 payload(t - 1, h, True)
-            AA = ap(PB, 256, 384)
+            K, AA = ap(PA, 0, 128), ap(PB, 256, 384)
             mm([(AA, ap("one", p1=1), ap("ca", p1=1), True, False)])
-
-            def keys(bank, part):
-                K = ap(bank, 0, 128)
-                if part == 0 and t == 0:
-                    return ([(K, ap("r0", 0, 128), ap("uc"), True, False)]
-                            + [(ap(bank, 64 * b, 64 * b + 64), ap("r0", b, 256, 2), blk("rm0", h, 64), False, False) for b in range(2)])
-                if part == 0:
-                    return [(K, blk("ri", 2 * (s - 2) + 1), ap("rm"), True, False)]
-                if part == 1:
-                    return [(K, ap("i15"), ap("cst" + H), False, False)]
-                return [(K, idf, ap("af" + H), False, False)]
-
-            def closed(lst):
-                return lst[:-1] + [lst[-1][:4] + (True,)]
-
-            mm(keys(PA, 0))
-            for k in range(4 if nat else 0):
-                for u, table in enumerate((ap("xt", 0, 4096), ap("arc"))):
-                    n, o = (("gm" + H, 256 * k), ("smo", 1024 * (2 + h) + 256 * k))[u]
-                    tt(ap(n, o, o + 256), ind(table, ap(lb, l0 + 16 * k, l0 + 16 * k + 16)), ap("msk" + H), A.min)
-                    mm([(ap(PB, 256 + 64 * b + 4 * u + k, 320 + 64 * b, 8), ap(n, o + b, o + 256, 2), ap("bo0"), False, (k, u, b) == (3, 1, 1))
-                        for b in range(2)])
-            if nat and h == 1:
-                load("sw9", last_move, [ap("xt", 0, 4096)], 0, [ap("arc")], by=1 << 20)
-            for k in range(0 if nat else 4):
-                tt(blk("gm" + H, k, 256), ind(ap("xt"), blk("of2" + H, k, 16)), ap("msk" + H), A.min)
+            if t == 0:
+                mm([(K, ap("r0", 0, 128), ap("uc"), True, False)]
+                   + [(ap(PA, 64 * b, 64 * b + 64), ap("r0", b, 256, 2), blk("rm0", h, 64), False, False) for b in range(2)])
+            else:
+                mm([(K, rin, ap("rm"), True, False)])
+            for k in range(4):
+                if str(k) not in um:
+                    tt(blk("gm" + H, k, 256), ind(ap("xt"), blk("of2" + H, k, 16)), ap("msk" + H), A.min)
                 mm([(ap(PB, 256 + 64 * b + k, 320 + 64 * b, 4), ap("gm" + H, 256 * k + b, 256 * k + 256, 2), ap("bo2"), False, k == 3 and b == 1)
                     for b in range(2)])
-            act(ap("cst" + H), AA, bias=0.5 - U / 2)
             act(ap("af" + H), AA)
-            mm(keys(PA, 1))
-            mm(closed(keys(PA, 2)))
+            act(ap("cst" + H), AA, bias=0.5 - U / 2)
+            mm([(K, idf, ap("af" + H), False, False)])
+            mm([(K, ap("idc"), ap("cst" + H), False, True)])
             tt(ap("ds" + H), AA, ap("cst" + H), A.subtract)
             xx = "xx" + H
-            cost = dict(scale=-1.0 / (16 * U), bias=130 + TOP / 16 - 0.4)
-
-            def lists(k):
-                mm([(ap(PB, 16 * k, 16 * k + 16), ap("zl" + H, 16 + 128 * k - 2 * x, 144 + 128 * k - 2 * x), ap("idq", x, 128, 8), x == 0, x == 7)
-                    for x in range(8)])
-
-            def states(k0, k1, sem):
-                c = (64 * s + 16 * k0, 64 * s + 16 * k1)
-                if "m" in C["sx"]:
-                    act(ap("mo", *c), ap(PB, 16 * k0, 16 * k1), bias=2048.0)
-                else:
-                    ts(ap("mo", *c), ap(PB, 16 * k0, 16 * k1), 2048.0, A.add)
-                if t < NV - 1:
-                    write(nxt, ap("mo", *c), ap("mi", *c), sem)
-                    first[0] = len(ops) - 1
-
-            def residuals(bank, j, sem):
-                for p in (0, 64):
-                    o = ap(bank, 128, 256, p0=p, p1=p + 64)
-                    mm([(o, ap(xx, 48, 112), idb, True, False), (o, ap(xx, 0, 64), ap("idn"), False, True)])
-                act(blk("ro", j), ap(bank, 128, 256), F.Relu, scale=-1.0, bias=RB)
-                if t < NV - 1:
-                    write(nxt, blk("ro", j), blk("ri", j), sem)
-                    ops[-1]["soft"] = [first[0]]
-
-            kb = PA
-            two = C["tail"] if t == NV - 1 else C["parts"] == 2
-            strikes = 0 if t == NV - 1 and two else C["strikes"]
+            cost = dict(scale=-1.0 / (STEP * U), bias=130 + TOP / STEP - 0.25)
             for k in range(4):
-                K = ap(kb, 0, 128)
-                onpe = k < strikes
-                nb = PC if kb == PA else PA
-                if onpe and k == 0:
-                    mm(keys(nb, 0) + keys(nb, 1) + keys(nb, 2))
-                win, fl = ap("so" + H, 128 * k + 7, 128 * k + 128, 8), blk("fl" + H, k, 16)
-                scan(blk("so" + H, k), ap("z8"), K, A.min, A.max, 2 * TOP * U)
-                if k + 1 < strikes:
-                    mm(keys(kb, 0) + keys(kb, 1) + keys(kb, 2)
-                       + [(K, ap("idk"), blk("eq" + H, j), False, False) for j in range(k)])
-                if not C["i32"]:
-                    cp(fl, win)
                 d = apx("sall" + H, k, every)
-                ts(d, win if C["i32"] else fl, int(U) - 1, an)
-                if k < 3:
-                    tt(blk("eq" + H, k), ind(d, L1), ap("ds" + H), A.is_equal if onpe else A.not_equal)
-                    if onpe:
-                        mm([(ap(nb, 0, 128), ap("idk"), blk("eq" + H, k), False, True)])
-                        if k + 1 < strikes:
-                            mm([(K, ap("idk"), blk("eq" + H, k), False, False)])
-                        kb = nb
-                    else:
-                        tt(K, K, blk("eq" + H, k), A.mult)
+                scan(blk("so" + H, k), ap("z8"), K, A.min, A.max, 2 * TOP * U)
+                ts(d, ap("so" + H, 128 * k + 7, 128 * k + 128, 8), int(U) - 1, an)
+                if str(k) in C["pes"][h]:
+                    tt(ap("eq" + H), ind(d, L1), ap("ds" + H), A.is_equal)
+                    mm([(K, ap("idk"), ap("eq" + H), False, True)])
+                elif k < 3:
+                    tt(ap("eq" + H), ind(d, L1), ap("ds" + H), A.not_equal)
+                    tt(K, K, ap("eq" + H), A.mult)
                 for k0, k1 in C["conv"]:
-                    if k1 == k + 1:
-                        for b in range(2):
-                            o, i0 = ap("zl" + H, 16 + 128 * k0 + b, 16 + 128 * k1, 16), apx("sall" + H, slice(k0, k1), slice(8 * b, 8 * b + 8))
-                            if ("y" if k == 3 else "z") in C["sx"]:
-                                act(o, i0, bias=-U / 2)
-                            else:
-                                ts(o, i0, -U / 2, A.add)
-                        for j in range(k0, min(k1, 3)):
-                            lists(j)
+                    if k1 != k + 1:
+                        continue
+                    for b in range(2):
+                        o, i0 = ap("zl" + H, 16 + 128 * k0 + b, 16 + 128 * k1, 16), apx("sall" + H, slice(k0, k1), slice(8 * b, 8 * b + 8))
+                        if k < 3 or C["z3"][b] == "S":
+                            act(o, i0, bias=-U / 2)
+                        else:
+                            ts(o, i0, -U / 2, A.add)
+                    for j in range(k0, k1):
+                        mm([(ap(PB, 16 * j, 16 * j + 16), ap("zl" + H, 16 + 128 * j - 2 * x, 144 + 128 * j - 2 * x), ap("idq", x, 128, 8),
+                             x == 0, x == 7) for x in range(8)])
                 if k == 2:
-                    act(ap(xx, 0, 96), ind(ap("so" + H, 0, 384), LX), **cost)
-                    if two:
-                        states(0, 3, "er%d" % s)
-                        residuals(PB, 2 * s, "fr%d" % s)
-                        if t == NV - 1:
-                            payload(t, h, False, ((1, 2),), True)
-            act(ap(xx, 96, 112), ap("so" + H, 384 + 7, 512, 8), **cost)
-            lists(3)
-            states(3 if two else 0, 4, "ar%d" % s)
-            if t == NV - 1 and two:
-                residuals(PB, 2 * s + 1, None)
-                payload(t, h, False, ((3,),))
-                continue
-            residuals(PC if kb == PA else PA, 2 * s + 1, "br%d" % s)
-            if t == NV - 1 or not C["late"][h]:
+                    act(ap(xx), ind(ap("so" + H, 0, 384), LX), **cost)
+            for c0 in (176, 240):
+                act(ap(xx, c0, c0 + 16), ap("so" + H, 384 + 7, 512, 8), **cost)
+            to = nxt if t < NV - 1 else last
+            if "m" in C["sx"]:
+                act(blk("mo", s, 64), ap(PB, 0, 64), bias=U / 2)
+            else:
+                ts(blk("mo", s, 64), ap(PB, 0, 64), U / 2, A.add)
+            write(to, blk("mo", s, 64), blk("mi", s, 64), "ar%d" % s)
+            first = len(ops) - 1
+            o = ap(PA if C["rb"] == "A" else PC, 128, 256)
+            mm([(o, ap(xx, 128, 256), idb, True, False), (o, ap(xx, 0, 128), ap("idn"), False, True)])
+            act(blk("ro", s), o, F.Relu, scale=-1.0, bias=RB)
+            write(to, blk("ro", s), blk("ri", s), "br%d" % s)
+            ops[-1]["soft"] = [first]
+            if t == NV - 1 or C["late"][h][t] == "0":
                 payload(t, h, False)
     r = 16 * NV % 128
     for h in range(2):
         cur[0] = h
         for k, o in enumerate((T.ys, T.ym)):
             a = blk("yo", 2 * h + k, 256)
-            tt(a, blk("py%d" % h, k, 256), blk("smi", 2 * (2 * NV - 4 + h) + k, 256), A.add)
+            b = blk("smo", 4 * (2 * NV - 2 + h) + 3, 256) if k == 0 and str(h) in C["pet"] else blk("loc%d" % h, k, 256)
+            if k or str(h) not in C["pre"]:
+                tt(a, blk("py%d" % h, k, 256), b, A.add)
 
             def store(o=o, j=2 * h + k, h=h):
                 g.sync.dma_start(o[128 - r:128, 256 * h:256 * h + 256], R(blk("yo", j, 256, p1=r))).then_inc(T.sem.stored, 16)
                 g.sync.dma_start(o[0:128 - r, 256 * h:256 * h + 256], R(blk("yo", j, 256, p0=r))).then_inc(T.sem.stored, 16)
-            op("Y", store, [a], [], (0, 0, 0, 120), dma=("stored", 128), lat=2500, by=1 << 17, nd=2)
+            op("Y", store, [a], [], None, dma=("stored", 128), by=1 << 17, nd=2)
     return ops, q, sent[0]
 
 
@@ -572,7 +537,10 @@ def link(ops):
         for a in o["wr"]:
             wr[a[0]][cols(a)] = i
         d.discard(i)
-        o["deps"] = sorted(d)
+        o["far"] = sorted(j for j in d if not (o["eng"] == "P" and ops[j]["eng"] == "P"))
+        o["own"] = [j for j in o["far"] if ops[j]["eng"] == o["eng"] and "dma" not in ops[j]]
+        o["other"] = [j for j in o["far"] if j not in o["own"]]
+        o["deps"] = sorted(d | set(o.get("soft", [])))
 
 
 KEPT = {}
@@ -581,37 +549,40 @@ KEPT = {}
 def times(ops, m):
     dur, pre, wire, post = [], [], [], []
     for o in ops:
-        c, ga, n, ns = o["cost"][:4]
         if "by" in o:
             x = (m["di"] * o["nd"], m["di"] + 0.6 * m["dl"], o["by"] / m["rate"], 0.4 * m["dl"])
         elif "rows" in o:
+            n = o["cost"][2]
             x = (n * m["g"], n * m["g"] + 0.6 * m["net"], o["rows"][0] * m["row"] + o["rows"][1] / m["rate"], 0.4 * m["net"])
         else:
-            if len(o["cost"]) > 4 and o["cost"][4]:
-                ga *= max(m["ga"], m["tti"]) / m["ga"]
-            if o["eng"] == "G":
-                c, ns = 1.6 * c, 1.6 * ns
-            x = ((c + ga * m["ga"]) * m["cy"] + n * m[{"V": "v", "S": "s", "P": "m", "G": "g"}[o["eng"]]] + ns, 0.0, 0.0, m["hop"])
+            c, ga, n, ns, two = o["cost"]
+            c += ga * max(m["ga"], m["tti"] if two else 0)
+            x = (c * m["cy"] + n * m[{"V": "v", "S": "s", "P": "m", "G": "g"}[o["eng"]]] + ns, 0.0, 0.0, m["hop"])
         for lst, v in zip((dur, pre, wire, post), x):
             lst.append(v)
     return dur, pre, wire, post, m["hop"] - m["hs"]
 
 
-def replay(ops, seq, tm, at=None):
+def replay(ops, seq, tm, at=None, why=None):
     dur, pre, wire, post, near = tm
-    free, done, line, end = {e: 0.0 for e in "VSPGY"}, [0.0] * len(ops), 0.0, 0.0
+    free, done, line, end, once = {e: 0.0 for e in "VSPGY"}, [0.0] * len(ops), 0.0, 0.0, ONCE
+    before = {e: None for e in free}
     for i in seq:
         o = ops[i]
         e = o["eng"]
-        a = free[e]
+        a, w = free[e], before[e]
         for j in o["other"]:
             if done[j] > a:
-                a = done[j]
+                a, w = done[j], j
         for j in o["own"]:
             if done[j] - near > a:
-                a = done[j] - near
+                a, w = done[j] - near, j
         if at is not None:
-            at[i] = a
+            at[i], before[e] = a, i
+            if why is not None:
+                why[i] = w
+        if once and "rows" in o:
+            a, once = a + once, 0.0
         free[e] = b = a + dur[i]
         if wire[i]:
             line = max(a + pre[i], line) + wire[i]
@@ -626,10 +597,6 @@ def order(ops, tries=TRIES):
     n = len(ops)
     kids = [[] for _ in ops]
     for i, o in enumerate(ops):
-        o["far"] = [j for j in o["deps"] if not (o["eng"] == "P" and ops[j]["eng"] == "P")]
-        o["own"] = [j for j in o["far"] if ops[j]["eng"] == o["eng"] and "dma" not in ops[j]]
-        o["other"] = [j for j in o["far"] if j not in o["own"]]
-        o["deps"] = sorted(set(o["deps"]) | set(o.get("soft", [])))
         for j in o["deps"]:
             kids[j].append(i)
     eng = [o["eng"] for o in ops]
@@ -647,7 +614,7 @@ def order(ops, tries=TRIES):
         for i in range(n):
             if not left[i]:
                 ready[eng[i]].append(i)
-        free, seq, at, line = {e: 0.0 for e in ready}, [], [0.0] * n, 0.0
+        free, seq, at, line, once = {e: 0.0 for e in ready}, [], [0.0] * n, 0.0, ONCE
         for _ in range(n):
             t0, e = min((max(free[e], min([rdy[i] for i in r])), e) for e, r in ready.items() if r)
             r = ready[e]
@@ -659,6 +626,8 @@ def order(ops, tries=TRIES):
             r.remove(i)
             seq.append(i)
             a = at[i] = max(t0, rdy[i])
+            if once and "rows" in ops[i]:
+                a, once = a + once, 0.0
             free[e] = done = a + dur[i]
             if wire[i]:
                 line = max(a + pre[i], line) + wire[i]
@@ -672,15 +641,13 @@ def order(ops, tries=TRIES):
         ends = [replay(ops, seq, tm) for tm in tms]
         return sum(ends) / len(ends), seq, at, ends
 
-    if "best" not in KEPT:
-        rng = np.random.default_rng(7)
+    def shake(lag):
         best = None
-        for lag in (0.0, 2000.0, 4000.0, 8000.0):
-            for slack in (0.0, 130.0, 300.0, 600.0):
-                pri = {i: tail[i] + fixed[i] - (lag if ops[i]["half"] == 1 else 0.0) for i in range(n)}
-                got = run(pri, slack)
-                if best is None or got[0] < best[0][0]:
-                    best = (got, pri, slack)
+        for slack in (0.0, 130.0, 300.0, 600.0):
+            pri = {i: tail[i] + fixed[i] - (lag if ops[i]["half"] == 1 else 0.0) for i in range(n)}
+            got = run(pri, slack)
+            if best is None or got[0] < best[0][0]:
+                best = (got, pri, slack)
         for trial in range(tries):
             got, pri, slack = best
             t = rng.random() * got[3][0]
@@ -693,8 +660,44 @@ def order(ops, tries=TRIES):
             tried = run(new, slack)
             if tried[0] <= got[0]:
                 best = (tried, new, slack)
-        KEPT["best"] = best[0]
-    end, seq, at, ends = KEPT["best"]
+        return best[0][1]
+
+    def swap(seq, count):
+        for trial in range(count):
+            if trial % 8 == 0:
+                tm, at, why = tms[rng.integers(len(tms))], [0.0] * n, [None] * n
+                replay(ops, seq, tm, at, why)
+                if trial % 64 == 0:
+                    seq = sorted(seq, key=lambda j: at[j])
+                    total = sum(replay(ops, seq, m) for m in tms)
+                i, pairs = int(np.argmax(at)), []
+                while why[i] is not None:
+                    if why[i] not in ops[i]["deps"]:
+                        pairs.append((why[i], i))
+                    i = why[i]
+            p, i = pairs[rng.integers(len(pairs))]
+            a, b = seq.index(p), seq.index(i)
+            if a > b:
+                continue
+            between = set(seq[a:b + 1])
+            if between.isdisjoint(ops[i]["deps"]) and rng.random() < 0.7:
+                new = seq[:a] + [i] + seq[a:b] + seq[b + 1:]
+            elif between.isdisjoint(kids[p]):
+                new = seq[:a] + seq[a + 1:b + 1] + [p] + seq[b + 1:]
+            else:
+                continue
+            tried = sum(replay(ops, new, m) for m in tms)
+            if tried <= total:
+                seq, total = new, tried
+        return sum(replay(ops, seq, m) for m in tms), seq
+
+    if "best" not in KEPT:
+        rng = np.random.default_rng(7)
+        seq = swap(min(swap(shake(lag), 4 * tries) for lag in CFG["lags"])[1], 8 * tries)[1]
+        at = [0.0] * n
+        replay(ops, seq, tms[0], at)
+        KEPT["best"] = (seq, at, [replay(ops, seq, m) for m in tms])
+    seq, at, ends = KEPT["best"]
     for i in range(n):
         ops[i]["at"] = at[i]
     return seq, ends

@@ -5,22 +5,24 @@ from concourse.mybir import ActivationFunctionType as F
 
 NV = 6
 CFG = dict(
-    mce=("VSSS", "VSSS"),
+    mce=("VVSS", "VSSS"),
     conv=[(0, 2), (2, 3), (3, 4)],
-    late=("11110", "11111"),
-    fuse=("13", "13"), rb="C", pet="", hbm=1.0,
+    late=("11110", "11110"),
+    fuse=("1", "1"), cut=(2, 1), m0=0, hv=("12", "1"), mc0=("VSSS", "VSSS"), c0="VV", rf=1, p0=2, rb="C", pet="01", hbm=1.0,
     mcv=(2, 3, 4),
-    ch=[0, 512, 1536, 2816, 3840, 4096],
+    ch=[0, 256, 768, 1792, 2816, 3840, 4096],
     sw=[(0, 1536), (1536, 2816), (2816, 4096)],
-    lags=(1700.0, 2000.0, 2300.0, 2000.0), z3="VV", um=("", ""), pre="0", sx="l2", pes=("", ""),
+    lags=(1700.0, 2000.0, 2300.0, 2000.0), swaps=(4000, 14000), heat=0.0005, z3="SSSV", zh="VV", on=("2", "2"), fold=(32, 700000),
+    um=("", ""), pre="", sx="l2",
 )
 HOME = 4
-TRIES = 240
+TRIES = 20
 SCRATCH = {}
 GONE = 106.0
 U = 4096.0
 STEP, TOP = 12.0, 2176.0
 NONE = U * (TOP - STEP * 176) + 4095
+WHOLE = 2.0 ** 23
 LIFT = 136.0
 
 
@@ -29,28 +31,28 @@ def _sb(n, w, d, where="sbuf"):
 
 
 for _n, _w, _d in [
-        ("arc", 4096, "int32"), ("xt", 8192, "int32"), ("mn", 4096, "float32"), ("mc", 4096, "bfloat16"),
+        ("xt", 8192, "int32"), ("mn", 4096, "int32"), ("p16", 256, "bfloat16"), ("cm", 256, "bfloat16"), ("bo3", 32, "float32"),
         ("payr", 4096, "bfloat16"), ("payo", 4096, "bfloat16"), ("acs", 512, "float32"), ("act", 512, "float32"),
         ("sti", (4, 32), "int32"), ("off0", 128, "uint16"), ("rsi", 256, "int32"), ("r0", 256, "bfloat16"),
         ("ci", 48, "int32"), ("cf", 24, "float32"), ("i16", 16, "float32"),
         ("onef", 256, "float32"), ("one", 128, "bfloat16"), ("idf", 256, "float32"), ("idb", 128, "bfloat16"),
-        ("idq", 128, "float16"), ("idn", 128, "bfloat16"), ("idc", 128, "bfloat16"), ("idk", 128, "bfloat16"),
-        ("bo2", 16, "float32"), ("lm", 128, "bfloat16"), ("hsel", 512, "bfloat16"), ("sel0", 1024, "bfloat16"),
+        ("idq", 128, "float16"), ("idn", 128, "bfloat16"), ("idc", 128, "bfloat16"),
+        ("bo2", 36, "float32"), ("lm", 128, "bfloat16"), ("hsel", 512, "bfloat16"), ("sel0", (2, 4, 128), "bfloat16"),
         ("sell", 768, "bfloat16"), ("selp", 768, "bfloat16"),
         ("ua", 128, "bfloat16"), ("ub", 128, "bfloat16"), ("uc", 128, "bfloat16"), ("ud", 128, "bfloat16"),
-        ("rm0", 128, "bfloat16"), ("rm", 128, "bfloat16"), ("ca", 128, "bfloat16"),
+        ("rm0", 280, "bfloat16"), ("rm", 128, "bfloat16"), ("ca", 128, "bfloat16"),
         ("lu", 32, "uint16"), ("z16", 256, "float32"), ("z8", 128, "float32"),
         ("mo", 12 * 64, "uint16"), ("mi", 12 * 64, "uint16"), ("ro", 12 * 128, "bfloat16"), ("ri", 12 * 128, "bfloat16"),
         ("smo", 12 * 1024, "float32"), ("smi", 8 * 512, "float32"), ("yo", 1024, "float32")]:
     _sb(_n, _w, _d)
 for _h in "01":
     for _n, _w, _d in [
-            ("mcg", 1024, "bfloat16"), ("c0s", 256, "bfloat16"), ("m1", 256, "bfloat16"), ("m2", 256, "bfloat16"),
-            ("m3", 256, "bfloat16"), ("rr", 256, "float32"), ("ff", 256, "bfloat16"), ("ft", 256, "bfloat16"),
+            ("mcg", 1024, "bfloat16"), ("c0s", 256, "int32"), ("tp", 256, "bfloat16"), ("m1", 256, "bfloat16"), ("m2", 256, "bfloat16"),
+            ("m3", 256, "bfloat16"), ("rr", 260, "float32"), ("ff", 256, "bfloat16"), ("ft", 256, "bfloat16"),
             ("msk", 256, "bfloat16"), ("gm", 1024, "float32"), ("cst", 128, "bfloat16"), ("zh", 144, "bfloat16"),
-            ("ofl", 64, "float32"), ("of2", 64, "uint16"), ("ds", 128, "float32"), ("eq", 128, "bfloat16"),
-            ("so", 512, "int32"), ("sall", (4, 16), "int32"), ("zl", 528, "float16"),
-            ("xx", 256, "bfloat16"), ("af", 128, "float32"), ("loc", 512, "float32"), ("wt", 768, "float32")]:
+            ("ofl", 64, "float32"), ("of2", 64, "uint16"), ("ds", 128, "int32"), ("eq", 128, "bfloat16"),
+            ("so", 512, "int32"), ("sall", (4, 16), "int32"), ("zl", (264, 2), "float16"),
+            ("xx", 128, "bfloat16"), ("af", 128, "float32"), ("loc", 512, "float32"), ("wt", 768, "float32")]:
         _sb(_n + _h, _w, _d)
 for _n in ["pa0", "pb0", "pc0", "pa1", "pb1", "pc1", "py0", "py1"]:
     _sb(_n, 512, "float32", "psum")
@@ -58,19 +60,25 @@ for _n in ["pa0", "pb0", "pc0", "pa1", "pb1", "pc1", "py0", "py1"]:
 SEMAPHORES = (["cV", "cS", "cP", "cG", "sent", "stored"] + ["ld%d" % i for i in range(12)] + ["sw%d" % i for i in range(10)]
               + ["%s%d" % (n, i) for n in ("ar", "br", "sm") for i in range(12)] + ["pp%d" % i for i in range(HOME)])
 
-GUESS = [dict(cy=0.86, ga=1.5, tti=0, v=20, s=150, m=12, g=400, hop=170, hs=100, net=1300, row=60, rate=350, dl=1500, di=180),
-         dict(cy=0.83, ga=1.2, tti=0, v=50, s=200, m=5, g=200, hop=200, hs=40, net=1000, row=30, rate=350, dl=1300, di=170),
-         dict(cy=0.86, ga=1.6, tti=2, v=0, s=60, m=5, g=600, hop=150, hs=60, net=2300, row=80, rate=500, dl=1000, di=230),
+GUESS = [dict(cy=0.86, ga=1.5, tti=0, v=20, s=150, m=12, g=400, hop=170, hs=150, net=1300, row=60, rate=350, dl=1500, di=180),
+         dict(cy=0.83, ga=1.2, tti=0, v=50, s=200, m=5, g=200, hop=200, hs=100, net=1000, row=30, rate=350, dl=1300, di=170),
+         dict(cy=0.86, ga=1.6, tti=2, v=0, s=60, m=5, g=600, hop=150, hs=80, net=2300, row=80, rate=500, dl=1000, di=230),
          dict(cy=1.0, ga=2.05, tti=0, v=20, s=150, m=10, g=450, hop=150, hs=150, net=1400, row=60, rate=250, dl=2000, di=100)]
 ONCE = 3000.0
 
 
 def ap(b, c0=0, c1=None, st=1, p0=0, p1=128):
-    return (b, (slice(c0, SCRATCH[b][1][1] if c1 is None else c1, st),), p0, p1)
+    s = SCRATCH[b][1][1:]
+    w = int(np.prod(s[1:]))
+    return (b, (slice(c0 // w, s[0] if c1 is None else c1 // w, st),) + (slice(None),) * (len(s) - 1), p0, p1)
 
 
 def apx(b, *idx):
     return (b, idx, 0, 128)
+
+
+def bit(a, b):
+    return (a[0], (slice(a[1][0].start + b, a[1][0].stop, 2),), a[2], a[3])
 
 
 def cols(a):
@@ -84,7 +92,7 @@ def ncol(a):
 
 def build(g, T, topo, rank):
     C = CFG
-    ops, cur, nth = [], [None], {}
+    ops, cur, nth = [], [None, -1, "walk"], {}
     q = {"V": g.vector, "S": g.scalar, "P": g.tensor, "G": g, "Y": g.sync}
 
     def R(a):
@@ -100,9 +108,9 @@ def build(g, T, topo, rank):
         for a in rd:
             if isinstance(a, tuple):
                 flat += [a[1], a[2]] if a[0] == "ind" else [a]
-        key = (cur[0], eng, wr[0][0] if wr else None)
+        key = (cur[0], cur[2], eng, wr[0][0] if wr else None)
         nth[key] = nth.get(key, 0) + 1
-        ops.append(dict(half=cur[0], kind=key + (nth[key],), eng=eng, fn=fn, rd=flat, wr=wr, cost=cost, **kw))
+        ops.append(dict(half=cur[0], visit=cur[1], kind=key + (nth[key],), eng=eng, fn=fn, rd=flat, wr=wr, cost=cost, **kw))
 
     def vcost(out, ins, tt=False):
         n = ncol(out)
@@ -176,115 +184,132 @@ def build(g, T, topo, rank):
     CH, PW = C["ch"], 4096 // HOME
 
     for i in range(len(CH) - 1):
-        load("ld%d" % i, [(T.arc[:, CH[i]:CH[i + 1]], T.arcs[:, CH[i]:CH[i + 1]])], [ap("arc", CH[i], CH[i + 1])], 512 * (CH[i + 1] - CH[i]))
-    load("ld8", [(T.sti[:], T.st0[:])] + [(T.rsi[8 * j:8 * j + 8, :], T.rs0[:, 256 * j:256 * j + 256]) for j in range(8)],
+        load("ld%d" % i, [(T.xt[:, 4096 + CH[i]:4096 + CH[i + 1]], T.arcs[:, CH[i]:CH[i + 1]])], [ap("xt", 4096 + CH[i], 4096 + CH[i + 1])],
+             512 * (CH[i + 1] - CH[i]))
+    load("ld8", [(T.sti[:], T.st0[:])] + [(T.rsi[16 * k:16 * k + 16, :], T.rs0[:, 512 * k:512 * k + 512]) for k in range(4)],
          [apx("sti", every, every), ap("rsi")], 1 << 17)
     load("ld9", [(T.acs[:], T.ac[:])], [ap("acs")], 1 << 18)
-    turned("ld10", 0, PW)
+    if not C["p0"]:
+        turned("ld10", 0, PW)
 
     start = len(ops)
-    ms(ap("onef"), 1.0)
     idf, idb = ap("idf", 0, 128), ap("idb")
-    iota(ap("ci", 0, 2), [[16, 2]], 0, 1)
-    iota(ap("ci", 2, 3), [[0, 1]], 1, 1)
+    sh, an = A.logical_shift_right, A.bitwise_and
+    P0, P16, P2 = ap("ci", 0, 1), ap("ci", 1, 2), ap("ci", 2, 3)
+    LABEL, GROUP, PAIR, NEXT, UPPER, SLOT, SECOND = [col(j) for j in range(7)]
+    fields = [(P0, 0, 15), (P0, 4, 7), (P0, 1, 7), (P16, 3, 14), (P0, 3, 1), (P0, 4, 3), (P0, 6, 1), (P0, 0, 49), (P2, 0, 14), (P0, 0, 1)]
+
+    def field(j):
+        ts(ap("ci", 16 + j, 17 + j), fields[j][0], fields[j][1], sh, fields[j][2], an)
+
+    ms(ap("onef", 0, 128), 1.0)
+    iota(ap("ci", 0, 4), [[2, 2], [16, 2]], 0, 1)
+    ms(ap("sel0"), 0.0)
+    field(0)
+    act(col(11), ap("ci", 16, 17), F.Exp, scale=0.8, more=1300)
     asel(idf, ap("onef", 0, 128), [[-1, 128]], A.is_equal, 0, 1)
     iota(ap("lm"), [[1, 8], [0, 16]], 0, 0)
-    iota(ap("ua"), [[0, 16], [1, 8]], 0, 0)
-    iota(ap("ub"), [[1, 16], [0, 2], [16, 4]], 0, 0)
-    iota(ap("i16"), [[1, 16]], 0, 0)
-    iota(ap("ci", 8, 16), [[2, 8]], 0, 0)
-    iota(ap("ci", 32, 40), [[0, 8]], 7, 0)
-    iota(ap("ci", 40, 48), [[0, 2], [128, 4]], 7, 0)
-    for n in ("uc", "sel0", "hsel"):
-        ms(ap(n), 0.0)
+    iota(ap("ua"), [[0, 8], [1, 8], [0, 2]], 0, 0)
+    paint(ap("sel0"), [[1, 2], [2, 32], [0, 16]], 0, 1.0)
+    field(1)
+    field(2)
+    cp(ap("cf", 0, 3), ap("ci", 16, 19))
+    ms(ap("hsel"), 0.0)
+    paint(ap("hsel"), [[1, 8], [0, 4], [8, 16]], 0, U)
     ms(ap("r0", p0=64), 1.0)
-    for n, w in (("ff0", 1), ("ff1", 1), ("zh0", 144), ("zh1", 144)):
-        ms(ap(n, 0, w), 0.0)
-    act(ap("one"), ap("onef", 0, 128))
-    act(ap("idf", 128, 256), idf)
-    for n, v in (("idb", 1.0), ("idc", -1.0 - STEP), ("idn", -1.0)):
-        act(ap(n), idf, scale=v)
-    cp(ap("idq"), idf)
-    sh, an = A.logical_shift_right, A.bitwise_and
-    P0, P16 = ap("ci", 0, 1), ap("ci", 1, 2)
-    for j, (src, s, m) in enumerate([(P0, 0, 15), (P16, 3, 15), (P0, 3, 1), (P0, 4, 7), (P0, 4, 3), (P0, 6, 1), (P0, 0, 7), (P0, 0, 56),
-                                     (ap("ci", 2, 3), 0, 7)]):
-        ts(ap("ci", 16 + j, 17 + j), src, s, sh, m, an)
-    cp(ap("cf", 0, 8), ap("ci", 16, 24))
-    LABEL, NEXT, UPPER, GROUP, SLOT, SECOND, LOW3 = [col(j) for j in range(7)]
-    ROW = col(21)
-    ts(ROW, ap("ci", 24, 25), col(7), A.add)
-    act(col(11), LABEL, F.Exp, scale=0.8, more=1300)
-    ts(ap("bo2"), ap("i16"), NEXT, A.is_equal)
-    ts(ap("lu", 0, 8), ap("ci", 8, 16), UPPER, A.add)
-    act(col(9), LABEL, scale=8.0)
-    ts(ap("lu", 8, 24), ap("ci", 32, 48), col(9), A.add, 383.0, A.min)
-    L1, LX = ap("lu", 0, 8), ap("lu", 8, 24)
-    act(ap("ca", p1=1), ap("onef", 0, 128, p1=1), scale=LIFT * U)
-    act(ap("z16"), ap("onef"), scale=0.0)
-    act(ap("z16", 0, 256, 16), ap("onef", 0, 16), scale=1000.0)
-    act(ap("z8"), ap("onef", 0, 128), scale=2 * TOP * U)
-    act(ap("z8", 0, 128, 8), ap("onef", 0, 16), scale=NONE)
+    for n, w, v in (("rr0", 1, 0.0), ("rr1", 1, 0.0), ("zh0", 144, 0.0), ("zh1", 144, 0.0), ("z16", 256, 0.0), ("p16", 256, 1.0), ("one", 128, 1.0)):
+        ms(ap(n, 0, w), v)
+    ms(ap("z16", 0, 256, 16), 1000.0)
+    ms(ap("p16", 0, 256, 16), 2.0)
+    ms(ap("cm", p1=1), -160.0)
+    act(idb, idf)
     ts(ap("lm"), ap("lm"), GROUP, A.is_equal, -1.0, A.mult)
-    ts(ap("ua"), ap("ua"), LOW3, A.not_equal, 0.5, A.subtract)
+    ts(ap("ua"), ap("ua"), PAIR, A.not_equal, 0.5, A.subtract)
     tt(ap("lm"), ap("lm"), ap("ua"), A.mult)
     act(ap("lm"), ap("lm"), scale=col(11))
     ts(col(12), LABEL, 0.0, A.is_equal)
-    act(col(8), col(12), scale=-1.0, bias=1.0)
+    ts(col(8), LABEL, 0.0, A.not_equal)
+    for i in range(start, len(ops)):
+        ops[i]["soon"] = True
+    iota(ap("ub"), [[1, 16], [0, 2], [16, 4]], 0, 0)
+    iota(ap("i16"), [[1, 16]], 0, 0)
+    iota(ap("ci", 8, 16), [[2, 8]], 0, 0)
+    ms(ap("uc"), 0.0)
+    act(ap("idf", 128, 256), idf)
+    for n, v in (("idc", -1.0 - STEP), ("idn", -1.0), ("idq", 1.0)):
+        act(ap(n), idf, scale=v)
+    for j in range(3, len(fields)):
+        field(j)
+    cp(ap("cf", 3, 8), ap("ci", 19, 24))
+    ROW = col(21)
+    ts(ROW, ap("ci", 24, 25), col(7), A.add)
+    act(col(16), ap("ci", 25, 26), scale=-1.0, bias=1.0)
+    act(col(17), ap("ci", 25, 26), scale=2.0 ** -14, bias=-2.0 ** -15)
+    act(col(18), NEXT, bias=1.0)
+    ms(ap("bo2"), 0.0)
+    ts(ap("bo3", 0, 16), ap("i16"), NEXT, A.is_equal, col(16), A.mult)
+    ts(ap("bo3", 16, 32), ap("i16"), col(18), A.is_equal, col(17), A.mult)
+    for u in range(2):
+        tt(ap("bo2", 2 + u, 34, 4), ap("bo3", u, 16, 2), ap("bo3", 16 + u, 32, 2), A.add)
+    ts(ap("lu", 0, 8), ap("ci", 8, 16), UPPER, A.add)
+    act(col(9), LABEL, scale=8.0, bias=7.0)
+    ts(ap("lu", 8, 12), ap("onef", 0, 4), col(9), A.mult)
+    L1, LX = ap("lu", 0, 8), ap("lu", 8, 12)
+    act(ap("ca", p1=1), ap("onef", 0, 128, p1=1), scale=LIFT * U)
+    act(ap("z8"), ap("onef", 0, 128), scale=2 * TOP * U)
+    act(ap("z8", 0, 128, 8), ap("onef", 0, 16), scale=NONE)
     ts(col(13), SLOT, 0.0, A.is_gt)
     act(col(14), SECOND, scale=-1.0, bias=GONE - 1)
     act(col(15), col(13), scale=col(14), bias=1.0)
     RB = col(15)
-    ms(ap("uc", p0=64, p1=66), (TOP + STEP * LIFT) * U)
+    ms(ap("uc", p0=64, p1=66), (TOP + (STEP + 1) * LIFT) * U - WHOLE)
     iota(ap("ud"), [[0, 16], [-int(U), 8]], 0, 0)
     act(ap("uc", p0=64, p1=65), ap("ud", p0=64, p1=65))
-    paint(ap("sel0"), [[1, 64], [0, 16]], 0, 1.0)
-    paint(ap("hsel"), [[1, 8], [0, 4], [8, 16]], 0, U)
     act(col(19), SECOND, scale=STEP * U, bias=-STEP * U)
     act(col(20), SECOND, scale=STEP * U * 83, bias=-STEP * U * 41)
-    ts(ap("rm0"), ap("ub"), ROW, A.is_equal, col(19), A.mult)
+    ms(ap("rm0"), 0.0)
+    act(col(22), col(19), scale=col(16))
+    act(col(23), col(22), scale=-1.0, bias=col(19))
+    for h in range(2):
+        ts(ap("rm0", 8 + 136 * h, 136 + 136 * h), ap("ub"), ROW, A.is_equal, col(22 + h), A.mult)
     ts(ap("ub"), ap("ub"), ROW, A.is_equal, col(20), A.mult)
     act(ap("ub", p1=1), ap("onef", 0, 128, p1=1), scale=-STEP * U * 64)
     act(ap("ub", 0, 128, 4), ap("onef", 0, 32), scale=0.0)
     tt(ap("rm"), ap("ub"), ap("uc"), A.add)
-    for i in range(start, len(ops)):
-        ops[i]["soon"] = True
     for n in ("zl0", "zl1"):
         iota(ap(n), [[0, 528]], 0, 0)
-    act(ap("sell"), ap("sel0", 256, 1024), scale=-1.0)
-    act(ap("selp"), ap("sel0", 256, 1024), scale=41.0)
-    paint(ap("selp"), [[1, 48], [0, 16]], 80, -42.0)
-    for n, v in (("sell", GONE), ("selp", 64.0)):
+    for b in range(2):
+        act(blk("sell", b, 384), apx("sel0", b, slice(1, 4), every), scale=-1.0)
+        act(blk("selp", b, 384), apx("sel0", b, slice(1, 4), every), scale=41.0)
+    paint(ap("selp"), [[1, 2], [2, 24], [0, 16]], 80, -42.0)
+    for n, v in (("sell", GONE - 160), ("selp", 64.0)):
         paint(ap(n), [[0, 768]], 0, v)
     banks, used, start = ["pa0", "pa1", "pb0", "pb1", "pc0", "pc1"], 0, len(ops)
     for i in range(len(CH) - 1):
         c = (CH[i], CH[i + 1])
-        ts(ap("xt", *c), ap("arc", *c), 32767, an)
-        ts(ap("arc", *c), ap("arc", *c), 15, sh)
         for c0 in range(c[0], c[1], 512):
             c1 = min(c0 + 512, c[1])
             b = ap(banks[used % len(banks)], 0, c1 - c0)
             used += 1
-            act(b, ap("arc", c0, c1))
+            act(b, ap("xt", 4096 + c0, 4096 + c1), F.Relu, scale=2.0 ** -15, bias=-0.5625)
+            if c0 == c[0]:
+                ts(ap("xt", *c), ap("xt", 4096 + c[0], 4096 + c[1]), 32767, an)
             tt(ap("mn", c0, c1), b, ap("xt", c0, c1), A.min)
-        if i in C["mcv"]:
-            ts(ap("mc", *c), ap("mn", *c), 1 / U, A.mult, 159.5 + 0.5 / U, A.add)
-        else:
-            act(ap("mc", *c), ap("mn", *c), bias=159.5 + 0.5 / U, scale=1 / U)
     for i, (c0, c1) in enumerate(C["sw"]):
-        lo = lambda n, k, o: T[n][16 * k:16 * k + 8, o + c0:o + c1]
-        hi = lambda n, k, o: T[n][16 * k + 8:16 * k + 16, o + c0:o + c1]
-        load("sw%d" % (2 * i), [(lo("xt", k, 4096), hi("xt", k, 0)) for k in range(8)] + [(hi("xt", k, 4096), hi("arc", k, 0)) for k in range(8)],
-             [ap("xt", 4096 + c0, 4096 + c1)], 512 * (c1 - c0), [ap("xt", c0, c1), ap("arc", c0, c1)])
-        load("sw%d" % (2 * i + 1), [(hi("xt", k, 0), lo("arc", k, 0)) for k in range(8)], [ap("xt", c0, c1)], 256 * (c1 - c0), [ap("arc", c0, c1)])
+        load("sw%d" % (2 * i), [(T.xt[0:128:2, 4096 + c0:4096 + c1], T.xt[1:128:2, c0:c1])],
+             [ap("xt", 4096 + c0, 4096 + c1)], 256 * (c1 - c0), [ap("xt", c0, c1)])
+        load("sw%d" % (2 * i + 1), [(T.xt[1:128:2, c0:c1], T.arcs[0:128:2, c0:c1])], [ap("xt", c0, c1)], 256 * (c1 - c0))
+    if C["p0"]:
+        turned("ld10", 0, PW)
+        ops[-1]["soft"] = [len(ops) - 1 - C["p0"]]
     turned("ld11", PW, 4096)
-    ops[-1]["soft"] = [len(ops) - 2]
+    ops[-1]["soft"] = [len(ops) - 2, len(ops) - 3]
     act(ap("r0", p1=64), ap("rsi", p1=64))
     for h in range(2):
         cp(blk("off0", h, 64), apx("sti", every, slice(16 * h, 16 * h + 16)))
         bank = "py%d" % h
         for b in range(2):
-            o, i = blk(bank, b), ap("acs", 256 * h + b, 256 * h + 256, 2)
+            o, i = blk(bank, b), bit(blk("acs", h, 256), b)
             op("P", lambda o=o, i=i: g.tensor.transpose(R(o), R(i), R(idf)), [i, idf], [o], (256, 0, 1, 30, False))
         act(blk("act", h, 256), ap(bank, 0, 256))
 
@@ -316,9 +341,9 @@ def build(g, T, topo, rank):
 
     def payload(t, h, late):
         H, s = str(h), 2 * t + h
-        cur[0] = h
         PA, PC = "pa" + H, "pc" + H
         home = t == NV - 1
+        cur[2] = "home" if home else "first" if t == 0 else "late" if late else "now"
         pet = home and H in C["pet"]
         rows = blk("ri" if home else "ro", s)
         xs = [blk("smo", 4 * s + k, 256) for k in range(4)]
@@ -330,9 +355,8 @@ def build(g, T, topo, rank):
             fuse = not home and str(ks[0]) in C["fuse"][h]
             for k in ks:
                 if not fuse:
-                    act(xs[k], lst[k])
-                c = wb[k]
-                mm([(ap(c[0], c[1][0].start + b, c[1][0].stop, 2), blk("selp", 2 * k - 2 + b), rows, True, True) for b in range(2)])
+                    (cp if home and str(k) in C["hv"][h] else act)(xs[k], lst[k])
+                mm([(bit(wb[k], b), blk("selp", 3 * b + k - 1), rows, True, True) for b in range(2)])
             w = ap(PC) if ks[0] == 1 else wb[3]
             act(ap("wt" + H, 256 * ks[0] - 256, 256 * ks[-1]) if fuse else w, w, F.Exp, scale=-0.125)
             for k in ks:
@@ -361,7 +385,8 @@ def build(g, T, topo, rank):
             for k in range(4):
                 mm([(ap("py" + H, 0, 256), turn, xs[k], k == 0, False)])
             for k in range(1, 4):
-                tt(loc[1], xs[k], xs[0] if k == 1 else loc[1], A.max)
+                w = wb[2] if C["m0"] else loc[1]
+                tt(w if k < 3 else loc[1], xs[0] if k == 1 else w, xs[k], A.max)
             mm([(ap("py" + H, 256, 512), turn, loc[1], False, False)])
             return
         own = T.cores[(rank - t) % nr]
@@ -372,16 +397,18 @@ def build(g, T, topo, rank):
                                   srcs=[R(x) for x in xs], dst=R(blk("smi", 2 * (s - 2) + k, 256)), alu_op=1 + k)
                 for k in range(2)], local_sem=T.sem.sent)
         n = 2 * emask(own, 0, 2)[1]
-        op("G", fold, xs, [blk("smi", s - 2, 512)], (0, 0, 1.5, 0, False), dma=("sm%d" % s, n), rows=(24, 400000))
+        op("G", fold, xs, [blk("smi", s - 2, 512)], (0, 0, 1.5, 0, False), dma=("sm%d" % s, n), rows=C["fold"])
         sent[0] += n
-        for k in range(2):
-            mm([(blk("py" + H, k, 256), turn, blk("smi", 2 * (s - 2) + k, 256), False, t == NV - 2 and k == 1 and H not in C["pet"])])
+        n = C["cut"][0]
+        for k in range(n):
+            mm([(blk("py" + H, k, 512 // n), turn, blk("smi", n * (s - 2) + k, 512 // n), False,
+                 t == NV - 2 and k == n - 1 and H not in C["pet"])])
 
     features(0)
     for t in range(NV):
         for h in range(2):
             H = str(h)
-            cur[0] = h
+            cur[:] = [h, t, "walk"]
             PA, PB, PC = "pa" + H, "pb" + H, "pc" + H
             s = 2 * t + h
             nth.clear()
@@ -390,69 +417,83 @@ def build(g, T, topo, rank):
             if h == 1 and 0 < t < HOME:
                 features(t, [rin])
             SC = ap(PB, 256, 512)
-            mm([(SC, idf, blk("act", h, 256), True, False)])
+            n = C["cut"][1]
+            for k in range(n):
+                mm([(blk(PB, n + k, 256 // n), idf, blk("act", n * h + k, 256 // n), k == 0, False)])
             for k in range(4):
-                i0 = ind(ap("mc"), ap(lb, l0 + 16 * k, l0 + 16 * k + 16))
-                if C["mce"][h][k] == "S":
-                    act(blk("mcg" + H, k, 256), i0, bias=-160.0)
+                i0 = ind(ap("mn"), ap(lb, l0 + 16 * k, l0 + 16 * k + 16))
+                o, v = (ap("c0s" + H), -0.5 + 0.5 / U) if k == 0 and t else (blk("mcg" + H, k, 256), 159.5 + 0.5 / U)
+                if C["mce" if t else "mc0"][h][k] == "S":
+                    act(o, i0, scale=1 / U, bias=v)
                 else:
-                    ts(blk("mcg" + H, k, 256), i0, -160.0, A.add)
+                    ts(o, i0, 1 / U, A.mult, v, A.add)
             cbank = [ap("py" + H, 0, 256), ap(PA, 0, 256), ap(PC, 0, 256), ap(PA, 256, 512)]
-            low = blk("mcg" + H, 0, 256)
+            low = ap("c0s" + H)
             for k in range(1 if t else 0, 4):
                 c = cbank[k]
                 lst = [(c, idb, blk("mcg" + H, k, 256), True, False)]
                 if t == 0:
-                    lst.append((c, blk("sel0", 2 * k + h, p1=64), ap("r0", p1=64), False, True))
+                    lst.append((c, ap("one", p1=1), ap("cm", p1=1), False, False))
+                    lst.append((c, ("sel0", (h, k, every), 0, 64), ap("r0", p1=64), False, True))
                 else:
                     for b in range(2):
-                        lst.append((ap(c[0], c[1][0].start + b, c[1][0].stop, 2), blk("sell", 2 * k - 2 + b, p1=64), blk("ri", s - 2, p1=64),
-                                    False, b == 1))
+                        lst.append((bit(c, b), blk("sell", 3 * b + k - 1, p1=64), blk("ri", s - 2, p1=64), False, b == 1))
                 mm(lst)
                 if k == 0:
                     low = ap("c0s" + H)
-                    cp(low, c)
+                    (act if C["c0"][h] == "S" else cp)(low, c)
                 else:
                     tt(ap("m%d" % k + H), c, low, A.min)
                     low = ap("m%d" % k + H)
             HI = ap(PC, 256, 320)
             (act if "l" in C["sx"] else cp)(ap("ofl" + H), ap(lb, l0, l0 + 64))
             mm([(HI, idf, ap("ofl" + H), True, False)])
-            mm([(blk(PB, 2 + b), ap("m3" + H, b, 256, 2), idb, False, b == 1) for b in range(2)])
-            scan(ap("rr" + H), ap("z16"), SC, A.add, A.min)
-            tt(ap("ff" + H, 1, 256), ap("rr" + H, 0, 255), ap(PB, 257, 512), A.is_gt)
+            mm([(blk(PB, 2 + b), bit(ap("m3" + H), b), idb, False, b == 1) for b in range(2)])
+            scan(ap("rr" + H, 1, 257), ap("z16"), SC, A.add, A.min)
+            tt(ap("ff" + H), ap("rr" + H, 0, 256), SC, A.is_gt)
+            scan(ap("tp" + H), ap("p16"), ap("ff" + H), A.subtract, A.max)
             for b in range(2):
-                tt(ap("zh" + H, 16 + b, 144, 16), ap("rr" + H, 128 * b + 7, 128 * b + 128, 16), ap("rr" + H, 128 * b + 15, 128 * b + 128, 16), A.is_gt)
-            mm([(ap(PA, b, 256, 2), blk("ff" + H, b), idb, True, True) for b in range(2)])
-            act(ap("ft" + H), ap(PA, 0, 256), scale=col(8), bias=col(12))
+                (act if C["zh"][b] == "S" else cp)(ap("zh" + H, 16 + b, 144, 16), ap("tp" + H, 128 * b + 15, 128 * b + 128, 16))
+            mm([(bit(ap(PA, 0, 256), b), blk("ff" + H, b), idb, True, True) for b in range(2)])
+            on = C["on"][h]
+            if "f" in on:
+                ts(ap("ft" + H), ap(PA, 0, 256), col(8), A.mult, col(12), A.add)
+            else:
+                act(ap("ft" + H), ap(PA, 0, 256), scale=col(8), bias=col(12))
             mm([(HI, ap("zh" + H, 16 - 2 * x, 144 - 2 * x), blk("hsel", x, 64), False, x == 7) for x in range(8)])
-            (act if "2" in C["sx"] else cp)(ap("of2" + H), HI)
+            (cp if "2" in on else act)(ap("of2" + H), HI)
             mm([(ap(PA, 256, 512), ap("lm"), ap("ft" + H), True, True)])
             um = C["um"][h]
-            if len(um) < 4:
-                act(ap("msk" + H), ap(PA, 256, 512), F.Relu, scale=65536.0)
+            if "k" in on:
+                ts(ap("msk" + H), ap(PA, 256, 512), 0.0, A.max, 2.0 ** 33, A.mult)
+            else:
+                act(ap("msk" + H), ap(PA, 256, 512), F.Relu, scale=2.0 ** 33)
             if um:
-                act(ap(PA, 256, 512), ap(PA, 256, 512), F.Relu, scale=65536.0)
+                act(ap(PA, 256, 512), ap(PA, 256, 512), F.Relu, scale=2.0 ** 33)
             for k in um:
                 act(blk("gm" + H, int(k), 256), ind(ap("xt"), blk("of2" + H, int(k), 16)))
             for k in um:
                 tt(blk("gm" + H, int(k), 256), ap(PA, 256, 512), blk("gm" + H, int(k), 256), A.min)
             if t and C["late"][h][t - 1] == "1":
                 payload(t - 1, h, True)
+                cur[2] = "walk"
             K, AA = ap(PA, 0, 128), ap(PB, 256, 384)
             mm([(AA, ap("one", p1=1), ap("ca", p1=1), True, False)])
             if t == 0:
                 mm([(K, ap("r0", 0, 128), ap("uc"), True, False)]
-                   + [(ap(PA, 64 * b, 64 * b + 64), ap("r0", b, 256, 2), blk("rm0", h, 64), False, False) for b in range(2)])
+                   + [(K, bit(ap("r0"), b), ap("rm0", 8 + 144 * h - 8 * b, 136 + 144 * h - 8 * b), False, False) for b in range(2)])
             else:
                 mm([(K, rin, ap("rm"), True, False)])
             for k in range(4):
                 if str(k) not in um:
                     tt(blk("gm" + H, k, 256), ind(ap("xt"), blk("of2" + H, k, 16)), ap("msk" + H), A.min)
-                mm([(ap(PB, 256 + 64 * b + k, 320 + 64 * b, 4), ap("gm" + H, 256 * k + b, 256 * k + 256, 2), ap("bo2"), False, k == 3 and b == 1)
+                mm([(ap(PB, 256 + k, 384, 4), bit(blk("gm" + H, k, 256), b), ap("bo2", 2 - 2 * b, 34 - 2 * b), False, k == 3 and b == 1)
                     for b in range(2)])
-            act(ap("af" + H), AA)
-            act(ap("cst" + H), AA, bias=0.5 - U / 2)
+            for n, v in (("af", WHOLE - LIFT * U), ("cst", 0.5 - U / 2)):
+                if n[0] in on:
+                    ts(ap(n + H), AA, v, A.add)
+                else:
+                    act(ap(n + H), AA, bias=v)
             mm([(K, idf, ap("af" + H), False, False)])
             mm([(K, ap("idc"), ap("cst" + H), False, True)])
             tt(ap("ds" + H), AA, ap("cst" + H), A.subtract)
@@ -462,45 +503,50 @@ def build(g, T, topo, rank):
                 d = apx("sall" + H, k, every)
                 scan(blk("so" + H, k), ap("z8"), K, A.min, A.max, 2 * TOP * U)
                 ts(d, ap("so" + H, 128 * k + 7, 128 * k + 128, 8), int(U) - 1, an)
-                if str(k) in C["pes"][h]:
-                    tt(ap("eq" + H), ind(d, L1), ap("ds" + H), A.is_equal)
-                    mm([(K, ap("idk"), ap("eq" + H), False, True)])
-                elif k < 3:
+                if k < 3:
                     tt(ap("eq" + H), ind(d, L1), ap("ds" + H), A.not_equal)
                     tt(K, K, ap("eq" + H), A.mult)
                 for k0, k1 in C["conv"]:
                     if k1 != k + 1:
                         continue
-                    for b in range(2):
-                        o, i0 = ap("zl" + H, 16 + 128 * k0 + b, 16 + 128 * k1, 16), apx("sall" + H, slice(k0, k1), slice(8 * b, 8 * b + 8))
-                        if k < 3 or C["z3"][b] == "S":
-                            act(o, i0, bias=-U / 2)
-                        else:
-                            ts(o, i0, -U / 2, A.add)
+                    o, i0 = ap("zl" + H, 16 + 128 * k0, 16 + 128 * k1, 8), apx("sall" + H, slice(k0, k1), every)
+                    if C["z3"][k] == "S":
+                        act(o, i0, bias=-U / 2)
+                    else:
+                        ts(o, i0, -U / 2, A.add)
                     for j in range(k0, k1):
                         mm([(ap(PB, 16 * j, 16 * j + 16), ap("zl" + H, 16 + 128 * j - 2 * x, 144 + 128 * j - 2 * x), ap("idq", x, 128, 8),
                              x == 0, x == 7) for x in range(8)])
-                if k == 2:
-                    act(ap(xx), ind(ap("so" + H, 0, 384), LX), **cost)
-            for c0 in (176, 240):
-                act(ap(xx, c0, c0 + 16), ap("so" + H, 384 + 7, 512, 8), **cost)
+                if k == 0:
+                    act(ap(xx, 0, 64), ind(ap("so" + H, 0, 128), LX), **cost)
+            if "x" in on:
+                ts(ap(xx, 64, 128), ap("so" + H, 7, 512, 8), cost["scale"], A.mult, cost["bias"], A.add)
+            else:
+                act(ap(xx, 64, 128), ap("so" + H, 7, 512, 8), **cost)
             to = nxt if t < NV - 1 else last
             if "m" in C["sx"]:
                 act(blk("mo", s, 64), ap(PB, 0, 64), bias=U / 2)
             else:
                 ts(blk("mo", s, 64), ap(PB, 0, 64), U / 2, A.add)
-            write(to, blk("mo", s, 64), blk("mi", s, 64), "ar%d" % s)
+            if t < NV - 1 or not C["rf"]:
+                write(to, blk("mo", s, 64), blk("mi", s, 64), "ar%d" % s)
             first = len(ops) - 1
             o = ap(PA if C["rb"] == "A" else PC, 128, 256)
-            mm([(o, ap(xx, 128, 256), idb, True, False), (o, ap(xx, 0, 128), ap("idn"), False, True)])
-            act(blk("ro", s), o, F.Relu, scale=-1.0, bias=RB)
+            mm([(o[:2] + (p, p + 64), ap(xx, c0, c0 + 64), m, c0 == 0, c0 == 64) for p in (0, 64) for c0, m in ((0, idb), (64, ap("idn")))])
+            if "r" in on:
+                ts(blk("ro", s), o, RB, A.add, 0.0, A.max)
+            else:
+                act(blk("ro", s), o, F.Relu, bias=RB)
             write(to, blk("ro", s), blk("ri", s), "br%d" % s)
-            ops[-1]["soft"] = [first]
+            if t < NV - 1 or not C["rf"]:
+                ops[-1]["soft"] = [first]
+            else:
+                write(to, blk("mo", s, 64), blk("mi", s, 64), "ar%d" % s)
             if t == NV - 1 or C["late"][h][t] == "0":
                 payload(t, h, False)
     r = 16 * NV % 128
     for h in range(2):
-        cur[0] = h
+        cur[:] = [h, NV - 1, "end"]
         for k, o in enumerate((T.ys, T.ym)):
             a = blk("yo", 2 * h + k, 256)
             b = blk("smo", 4 * (2 * NV - 2 + h) + 3, 256) if k == 0 and str(h) in C["pet"] else blk("loc%d" % h, k, 256)
@@ -600,6 +646,7 @@ def order(ops, tries=TRIES):
         for j in o["deps"]:
             kids[j].append(i)
     eng = [o["eng"] for o in ops]
+    waits = [len(o["deps"]) for o in ops]
     tms = [times(ops, m) for m in GUESS]
     dur, pre, wire, post, near = tms[0]
     tail = [0.0] * n
@@ -662,38 +709,99 @@ def order(ops, tries=TRIES):
                 best = (tried, new, slack)
         return best[0][1]
 
+    queue = ["VSPGY".index(e) for e in eng]
+    other, own, far = [o["other"] for o in ops], [o["own"] for o in ops], ["rows" in o for o in ops]
+    deps = [o["deps"] for o in ops]
+
+    def play(seq, tm, s0, marks, done):
+        dur, pre, wire, post, near = tm
+        free, line, end, once = marks[s0]
+        free, marks, done = list(free), marks[:s0 + 1], list(done)
+        for c in range(s0 * 48, n, 48):
+            if c > s0 * 48:
+                marks.append((tuple(free), line, end, once))
+            for i in seq[c:c + 48]:
+                e = queue[i]
+                a = free[e]
+                for j in other[i]:
+                    if done[j] > a:
+                        a = done[j]
+                for j in own[i]:
+                    if done[j] - near > a:
+                        a = done[j] - near
+                if wire[i]:
+                    if once and far[i]:
+                        a, once = a + once, 0.0
+                    free[e] = b = a + dur[i]
+                    line = max(a + pre[i], line) + wire[i]
+                    b = max(b, line)
+                else:
+                    free[e] = b = a + dur[i]
+                done[i] = b = b + post[i]
+                if b > end:
+                    end = b
+        return end, marks, done
+
+    def along(first, near, inside, other_end):
+        move, todo = [first], [first]
+        while todo and len(move) < 6:
+            for j in near[todo.pop()]:
+                if inside(j) and j not in move:
+                    move.append(j)
+                    todo.append(j)
+        return None if todo or other_end in move else move
+
     def swap(seq, count):
+        zero = [((0.0,) * 5, 0.0, 0.0, ONCE)]
+        keep = None
         for trial in range(count):
             if trial % 8 == 0:
                 tm, at, why = tms[rng.integers(len(tms))], [0.0] * n, [None] * n
                 replay(ops, seq, tm, at, why)
-                if trial % 64 == 0:
-                    seq = sorted(seq, key=lambda j: at[j])
-                    total = sum(replay(ops, seq, m) for m in tms)
                 i, pairs = int(np.argmax(at)), []
                 while why[i] is not None:
-                    if why[i] not in ops[i]["deps"]:
+                    if why[i] not in deps[i]:
                         pairs.append((why[i], i))
                     i = why[i]
+                if trial % 80 == 0:
+                    seq = sorted(seq, key=lambda j: at[j])
+                    state = [play(seq, tm, 0, zero, [0.0] * n) for tm in tms]
+                    total = sum(s[0] / z for s, z in zip(state, size))
+                    if keep is None or total < keep[0]:
+                        keep = (total, seq)
+                pos = [0] * n
+                for j, x in enumerate(seq):
+                    pos[x] = j
             p, i = pairs[rng.integers(len(pairs))]
-            a, b = seq.index(p), seq.index(i)
+            a, b = pos[p], pos[i]
             if a > b:
                 continue
-            between = set(seq[a:b + 1])
-            if between.isdisjoint(ops[i]["deps"]) and rng.random() < 0.7:
-                new = seq[:a] + [i] + seq[a:b] + seq[b + 1:]
-            elif between.isdisjoint(kids[p]):
-                new = seq[:a] + seq[a + 1:b + 1] + [p] + seq[b + 1:]
+            more = int(rng.random() * 12) if rng.random() < 0.3 else 0
+            if rng.random() < 0.6:
+                a = min(a, max([a - more, 0] + [pos[j] + 1 for j in deps[i]]))
+                move = along(i, deps, lambda j: pos[j] >= a, p)
+                if not move:
+                    continue
+                new = seq[:a] + sorted(move, key=lambda x: pos[x]) + [x for x in seq[a:b + 1] if x not in move] + seq[b + 1:]
             else:
-                continue
-            tried = sum(replay(ops, new, m) for m in tms)
-            if tried <= total:
-                seq, total = new, tried
-        return sum(replay(ops, seq, m) for m in tms), seq
+                b = max(b, min([b + more, n - 1] + [pos[k] - 1 for k in kids[p]]))
+                move = along(p, kids, lambda j: pos[j] <= b, i)
+                if not move:
+                    continue
+                new = seq[:a] + [x for x in seq[a:b + 1] if x not in move] + sorted(move, key=lambda x: pos[x]) + seq[b + 1:]
+            got = [play(new, tm, a // 48, s[1], s[2]) for tm, s in zip(tms, state)]
+            tried = sum(s[0] / z for s, z in zip(got, size))
+            if tried <= total + CFG["heat"] * (1 - trial / count) * rng.random():
+                seq, total, state = new, tried, got
+                for j in range(a, b + 1):
+                    pos[seq[j]] = j
+        return keep
 
     if "best" not in KEPT:
         rng = np.random.default_rng(7)
-        seq = swap(min(swap(shake(lag), 4 * tries) for lag in CFG["lags"])[1], 8 * tries)[1]
+        first = [shake(lag) for lag in CFG["lags"]]
+        size = [replay(ops, first[0], m) for m in tms]
+        seq = swap(min(swap(x, CFG["swaps"][0]) for x in first)[1], CFG["swaps"][1])[1]
         at = [0.0] * n
         replay(ops, seq, tms[0], at)
         KEPT["best"] = (seq, at, [replay(ops, seq, m) for m in tms])

@@ -5,15 +5,15 @@ from concourse.mybir import ActivationFunctionType as F
 
 NV = 6
 CFG = dict(
-    mce=("VVSS", "VSSS"),
+    mce=("SSSV", "SSSS"),
     conv=[(0, 2), (2, 3), (3, 4)],
-    late=("11110", "11110"),
-    fuse=("1", "1"), cut=(2, 1), m0=0, hv=("12", "1"), mc0=("VSSS", "VSSS"), c0="VV", rf=1, p0=2, rb="C", pet="01", hbm=1.0,
+    late=("00000", "11110"),
+    fuse=("13", "13"), cut=(2, 1), m0=1, two=0, take=(1, 2, 3, 4, 5), pair=("3", ""), c1b="01", y0=0, bits=("", "12"), res=("0123", "3"), hv=("3", "3"), mc0=("VSSS", "VSSS"), c0="SS", rf=("01", "01"), early=(3, 3), ahead="", eng="SS", pe3="", x0p="", p0=2, rb="C", pet="01", hbm=1.0,
     mcv=(2, 3, 4),
     ch=[0, 256, 768, 1792, 2816, 3840, 4096],
     sw=[(0, 1536), (1536, 2816), (2816, 4096)],
-    lags=(1700.0, 2000.0, 2300.0, 2000.0), swaps=(4000, 14000), heat=0.0005, z3="SSSV", zh="VV", on=("2", "2"), fold=(32, 700000),
-    um=("", ""), pre="", sx="l2",
+    lags=(1350.0, 1400.0, 1450.0, 1450.0, 1500.0, 1500.0, 1550.0, 1600.0), swaps=(2500, 16000), heat=0.0005, fit=(0.0, 0.5, 0.3), side=(0.6, 0.3), z3=("SSSV", "SSSV"), zh="GG", fill="VVVGGGGGGGG", st="YYYS", on=("2xr", "2xr"), fold=(32, 700000),
+    um=("", ""), pre="", sx="0",
 )
 HOME = 4
 TRIES = 20
@@ -36,13 +36,14 @@ for _n, _w, _d in [
         ("sti", (4, 32), "int32"), ("off0", 128, "uint16"), ("rsi", 256, "int32"), ("r0", 256, "bfloat16"),
         ("ci", 48, "int32"), ("cf", 24, "float32"), ("i16", 16, "float32"),
         ("onef", 256, "float32"), ("one", 128, "bfloat16"), ("idf", 256, "float32"), ("idb", 128, "bfloat16"),
-        ("idq", 128, "float16"), ("idn", 128, "bfloat16"), ("idc", 128, "bfloat16"),
+        ("idq", 128, "float16"), ("id2", 64, "float16"), ("idc", 128, "bfloat16"),
         ("bo2", 36, "float32"), ("lm", 128, "bfloat16"), ("hsel", 512, "bfloat16"), ("sel0", (2, 4, 128), "bfloat16"),
         ("sell", 768, "bfloat16"), ("selp", 768, "bfloat16"),
         ("ua", 128, "bfloat16"), ("ub", 128, "bfloat16"), ("uc", 128, "bfloat16"), ("ud", 128, "bfloat16"),
         ("rm0", 280, "bfloat16"), ("rm", 128, "bfloat16"), ("ca", 128, "bfloat16"),
         ("lu", 32, "uint16"), ("z16", 256, "float32"), ("z8", 128, "float32"),
         ("mo", 12 * 64, "uint16"), ("mi", 12 * 64, "uint16"), ("ro", 12 * 128, "bfloat16"), ("ri", 12 * 128, "bfloat16"),
+        ("eo", (12, 48), "bfloat16"), ("ei", 12 * 48, "bfloat16"), ("re0", 128, "bfloat16"), ("re1", 128, "bfloat16"),
         ("smo", 12 * 1024, "float32"), ("smi", 8 * 512, "float32"), ("yo", 1024, "float32")]:
     _sb(_n, _w, _d)
 for _h in "01":
@@ -50,7 +51,7 @@ for _h in "01":
             ("mcg", 1024, "bfloat16"), ("c0s", 256, "int32"), ("tp", 256, "bfloat16"), ("m1", 256, "bfloat16"), ("m2", 256, "bfloat16"),
             ("m3", 256, "bfloat16"), ("rr", 260, "float32"), ("ff", 256, "bfloat16"), ("ft", 256, "bfloat16"),
             ("msk", 256, "bfloat16"), ("gm", 1024, "float32"), ("cst", 128, "bfloat16"), ("zh", 144, "bfloat16"),
-            ("ofl", 64, "float32"), ("of2", 64, "uint16"), ("ds", 128, "int32"), ("eq", 128, "bfloat16"),
+            ("ofl", 64, "float16"), ("of2", 64, "uint16"), ("ds", 128, "int32"), ("eq", 128, "bfloat16"),
             ("so", 512, "int32"), ("sall", (4, 16), "int32"), ("zl", (264, 2), "float16"),
             ("xx", 128, "bfloat16"), ("af", 128, "float32"), ("loc", 512, "float32"), ("wt", 768, "float32")]:
         _sb(_n + _h, _w, _d)
@@ -58,13 +59,15 @@ for _n in ["pa0", "pb0", "pc0", "pa1", "pb1", "pc1", "py0", "py1"]:
     _sb(_n, 512, "float32", "psum")
 
 SEMAPHORES = (["cV", "cS", "cP", "cG", "sent", "stored"] + ["ld%d" % i for i in range(12)] + ["sw%d" % i for i in range(10)]
-              + ["%s%d" % (n, i) for n in ("ar", "br", "sm") for i in range(12)] + ["pp%d" % i for i in range(HOME)])
+              + ["%s%d" % (n, i) for n in ("ar", "br", "er", "sm") for i in range(12)] + ["pp%d" % i for i in range(HOME)])
 
 GUESS = [dict(cy=0.86, ga=1.5, tti=0, v=20, s=150, m=12, g=400, hop=170, hs=150, net=1300, row=60, rate=350, dl=1500, di=180),
          dict(cy=0.83, ga=1.2, tti=0, v=50, s=200, m=5, g=200, hop=200, hs=100, net=1000, row=30, rate=350, dl=1300, di=170),
          dict(cy=0.86, ga=1.6, tti=2, v=0, s=60, m=5, g=600, hop=150, hs=80, net=2300, row=80, rate=500, dl=1000, di=230),
          dict(cy=1.0, ga=2.05, tti=0, v=20, s=150, m=10, g=450, hop=150, hs=150, net=1400, row=60, rate=250, dl=2000, di=100)]
-ONCE = 3000.0
+for _m, _v in zip(GUESS, (3000, 4000, 6000, 5000)):
+    _m["once"] = _v
+ONCE = 0.0
 
 
 def ap(b, c0=0, c1=None, st=1, p0=0, p1=128):
@@ -159,10 +162,13 @@ def build(g, T, topo, rank):
             fn = lambda: g.iota(R(out), pat, base, cmul)
         else:
             fn = lambda: g.iota(R(out), pat, base, cmul, allow_small_or_imprecise_dtypes=True)
-        op("G", fn, [], [out], (3.2 * ncol(out), 0, 0, 210, False))
+        op("G", fn, [], [out], (2.4 * ncol(out), 0, 0, 170, False))
 
     def asel(out, i0, pat, o, base, cmul, fill=0.0):
-        op("G", lambda: g.affine_select(R(out), R(i0), pat, o, fill, base, cmul), [i0], [out], (3.2 * ncol(out), 0, 0, 270, False))
+        op("G", lambda: g.affine_select(R(out), R(i0), pat, o, fill, base, cmul), [i0], [out], (2.4 * ncol(out), 0, 0, 220, False))
+
+    def gcp(out, i0):
+        asel(out, i0, [[0, ncol(out)]], A.is_ge, 0, 0)
 
     def paint(x, pat, base, v):
         asel(x, x, pat, A.not_equal, base, -1, v)
@@ -215,13 +221,14 @@ def build(g, T, topo, rank):
     field(2)
     cp(ap("cf", 0, 3), ap("ci", 16, 19))
     ms(ap("hsel"), 0.0)
+    fills = [(ap("r0"), 1), (ap("one"), 1), (ap("cm"), -160), (ap("z16"), 0), (ap("z16", 0, 256, 16), 1000), (ap("rr0", 0, 1), 0),
+             (ap("rr1", 0, 1), 0), (ap("p16"), 1), (ap("p16", 0, 256, 16), 2), (ap("zh0"), 0), (ap("zh1"), 0)]
+    for j, (x, v) in enumerate(fills):
+        if C["fill"][j] == "V":
+            ms(x, float(v))
+        else:
+            iota(x, [[0, ncol(x)]], v, 0)
     paint(ap("hsel"), [[1, 8], [0, 4], [8, 16]], 0, U)
-    ms(ap("r0", p0=64), 1.0)
-    for n, w, v in (("rr0", 1, 0.0), ("rr1", 1, 0.0), ("zh0", 144, 0.0), ("zh1", 144, 0.0), ("z16", 256, 0.0), ("p16", 256, 1.0), ("one", 128, 1.0)):
-        ms(ap(n, 0, w), v)
-    ms(ap("z16", 0, 256, 16), 1000.0)
-    ms(ap("p16", 0, 256, 16), 2.0)
-    ms(ap("cm", p1=1), -160.0)
     act(idb, idf)
     ts(ap("lm"), ap("lm"), GROUP, A.is_equal, -1.0, A.mult)
     ts(ap("ua"), ap("ua"), PAIR, A.not_equal, 0.5, A.subtract)
@@ -232,58 +239,57 @@ def build(g, T, topo, rank):
     for i in range(start, len(ops)):
         ops[i]["soon"] = True
     iota(ap("ub"), [[1, 16], [0, 2], [16, 4]], 0, 0)
-    iota(ap("i16"), [[1, 16]], 0, 0)
     iota(ap("ci", 8, 16), [[2, 8]], 0, 0)
     ms(ap("uc"), 0.0)
     act(ap("idf", 128, 256), idf)
-    for n, v in (("idc", -1.0 - STEP), ("idn", -1.0), ("idq", 1.0)):
+    for n, v in (("idc", -1.0 - STEP), ("idq", 1.0)):
         act(ap(n), idf, scale=v)
     for j in range(3, len(fields)):
         field(j)
     cp(ap("cf", 3, 8), ap("ci", 19, 24))
     ROW = col(21)
     ts(ROW, ap("ci", 24, 25), col(7), A.add)
-    act(col(16), ap("ci", 25, 26), scale=-1.0, bias=1.0)
-    act(col(17), ap("ci", 25, 26), scale=2.0 ** -14, bias=-2.0 ** -15)
-    act(col(18), NEXT, bias=1.0)
-    ms(ap("bo2"), 0.0)
-    ts(ap("bo3", 0, 16), ap("i16"), NEXT, A.is_equal, col(16), A.mult)
-    ts(ap("bo3", 16, 32), ap("i16"), col(18), A.is_equal, col(17), A.mult)
+    ODD = ap("ci", 25, 26)
+    ts(col(16), ODD, -1.0, A.mult, 1.0, A.add)
+    ts(col(17), ODD, 2.0 ** -14, A.mult, -2.0 ** -15, A.add)
+    cp(col(18), ODD)
+    ts(col(10), col(16), -U / 2, A.mult)
+    ts(col(19), ODD, -U / 2, A.mult)
+    tt(ap("id2"), ap("idf", 0, 128, 2), ap("idf", 1, 128, 2), A.add)
+    iota(ap("bo2"), [[0, 36]], 0, 0)
     for u in range(2):
-        tt(ap("bo2", 2 + u, 34, 4), ap("bo3", u, 16, 2), ap("bo3", 16 + u, 32, 2), A.add)
+        ts(ap("bo2", 2 + u, 34, 4), ap("ci", 8, 16), NEXT, A.is_equal, col(16 + u), A.mult)
     ts(ap("lu", 0, 8), ap("ci", 8, 16), UPPER, A.add)
-    act(col(9), LABEL, scale=8.0, bias=7.0)
+    ts(col(9), LABEL, 8.0, A.mult, 7.0, A.add)
     ts(ap("lu", 8, 12), ap("onef", 0, 4), col(9), A.mult)
     L1, LX = ap("lu", 0, 8), ap("lu", 8, 12)
-    act(ap("ca", p1=1), ap("onef", 0, 128, p1=1), scale=LIFT * U)
-    act(ap("z8"), ap("onef", 0, 128), scale=2 * TOP * U)
-    act(ap("z8", 0, 128, 8), ap("onef", 0, 16), scale=NONE)
+    iota(ap("ca"), [[0, 128]], int(LIFT * U), 0)
+    iota(ap("z8"), [[0, 128]], int(2 * WHOLE) - 1, 0)
+    iota(ap("z8", 0, 128, 8), [[0, 16]], int(NONE), 0)
     ts(col(13), SLOT, 0.0, A.is_gt)
-    act(col(14), SECOND, scale=-1.0, bias=GONE - 1)
-    act(col(15), col(13), scale=col(14), bias=1.0)
+    ts(col(14), SECOND, -1.0, A.mult, GONE - 1, A.add)
+    ts(col(15), col(13), col(14), A.mult, 1.0, A.add)
     RB = col(15)
     ms(ap("uc", p0=64, p1=66), (TOP + (STEP + 1) * LIFT) * U - WHOLE)
     iota(ap("ud"), [[0, 16], [-int(U), 8]], 0, 0)
     act(ap("uc", p0=64, p1=65), ap("ud", p0=64, p1=65))
-    act(col(19), SECOND, scale=STEP * U, bias=-STEP * U)
-    act(col(20), SECOND, scale=STEP * U * 83, bias=-STEP * U * 41)
-    ms(ap("rm0"), 0.0)
-    act(col(22), col(19), scale=col(16))
-    act(col(23), col(22), scale=-1.0, bias=col(19))
+    ts(col(20), SECOND, STEP * U * 83, A.mult, -STEP * U * 41, A.add)
+    iota(ap("rm0"), [[0, 280]], 0, 0)
+    ts(col(22), ODD, STEP * U, A.mult, -STEP * U, A.add)
+    ts(col(23), ODD, -STEP * U, A.mult)
     for h in range(2):
         ts(ap("rm0", 8 + 136 * h, 136 + 136 * h), ap("ub"), ROW, A.is_equal, col(22 + h), A.mult)
     ts(ap("ub"), ap("ub"), ROW, A.is_equal, col(20), A.mult)
     act(ap("ub", p1=1), ap("onef", 0, 128, p1=1), scale=-STEP * U * 64)
-    act(ap("ub", 0, 128, 4), ap("onef", 0, 32), scale=0.0)
+    iota(ap("ub", 0, 128, 4), [[0, 32]], 0, 0)
     tt(ap("rm"), ap("ub"), ap("uc"), A.add)
     for n in ("zl0", "zl1"):
-        iota(ap(n), [[0, 528]], 0, 0)
+        for c0 in (0, 264):
+            act(ap(n, c0, c0 + 264), ap("hsel", 0, 264), scale=0.0)
     for b in range(2):
-        act(blk("sell", b, 384), apx("sel0", b, slice(1, 4), every), scale=-1.0)
         act(blk("selp", b, 384), apx("sel0", b, slice(1, 4), every), scale=41.0)
     paint(ap("selp"), [[1, 2], [2, 24], [0, 16]], 80, -42.0)
-    for n, v in (("sell", GONE - 160), ("selp", 64.0)):
-        paint(ap(n), [[0, 768]], 0, v)
+    act(ap("selp", p1=1), ap("selp", p1=1), scale=0.0, bias=64.0 - 160)
     banks, used, start = ["pa0", "pa1", "pb0", "pb1", "pc0", "pc1"], 0, len(ops)
     for i in range(len(CH) - 1):
         c = (CH[i], CH[i + 1])
@@ -326,7 +332,7 @@ def build(g, T, topo, rank):
         k = len(e) // of
         return int(sum(1 << x for x in e[part * k:part * k + k])), k
 
-    sent = [0]
+    sent, sums = [0], []
 
     def write(core, src, to, sem, after=()):
         def fn():
@@ -334,6 +340,14 @@ def build(g, T, topo, rank):
             g.remote_dma(R(to), R(src), T.sem[sem], T.sem.sent, a[1], a[0], emask(core, 0, 1)[0])
         n = emask(core, 0, 1)[1]
         op("G", fn, [src] + list(after), [to], (0, 0, 1, 0, False), dma=(sem, n), rows=(8, 256 * ncol(src)))
+        sent[0] += n
+
+    def two(core, pairs, sem):
+        def fn():
+            g.remote_dma_fused([RemoteDMATransfer(dst_ids=[dst(core)], dma_engine_mask=emask(core, k, 2)[0], remote_sem=T.sem[sem],
+                                                  src=R(x[0]), dst=R(x[1])) for k, x in enumerate(pairs)], local_sem=T.sem.sent)
+        n = 2 * emask(core, 0, 2)[1]
+        op("G", fn, [x[0] for x in pairs], [x[1] for x in pairs], (0, 0, 1.3, 0, False), dma=(sem, n), rows=(16, 512 * ncol(pairs[0][0])))
         sent[0] += n
 
     def features(j, after=()):
@@ -350,7 +364,7 @@ def build(g, T, topo, rank):
         lst = [ind(ap("payo" if home else "payr"), blk("mi" if home else "mo", 4 * s + k, 16)) for k in range(4)]
         wb = [None, ap(PC, 0, 256), ap(PC, 256, 512), ap(PC, 0, 256) if late else ap(PA, 256, 512)]
         loc = [blk("loc" + H, j, 256) for j in range(2)]
-        act(xs[0], lst[0])
+        (cp if home and "0" in C["hv"][h] else act)(xs[0], lst[0])
         for ks in ((1, 2), (3,)):
             fuse = not home and str(ks[0]) in C["fuse"][h]
             for k in ks:
@@ -358,17 +372,30 @@ def build(g, T, topo, rank):
                     (cp if home and str(k) in C["hv"][h] else act)(xs[k], lst[k])
                 mm([(bit(wb[k], b), blk("selp", 3 * b + k - 1), rows, True, True) for b in range(2)])
             w = ap(PC) if ks[0] == 1 else wb[3]
-            act(ap("wt" + H, 256 * ks[0] - 256, 256 * ks[-1]) if fuse else w, w, F.Exp, scale=-0.125)
+            act(ap("wt" + H, 256 * ks[0] - 256, 256 * ks[-1]) if fuse else w, w, F.Exp, scale=-0.125, bias=-20.0)
             for k in ks:
-                if fuse:
+                if fuse and ks[0] == 1 and C["two"]:
+                    if k == 1:
+                        tt(ap("smo", 1024 * s + 256, 1024 * s + 768), ind(ap("payr"), ap("mo", 64 * s + 16, 64 * s + 48)), ap("wt" + H, 0, 512),
+                           A.mult)
+                elif fuse and str(k) in C["bits"][h]:
+                    for j in (2 * k, 2 * k + 1):
+                        tt(blk("smo", 8 * s + j), ind(ap("payr"), blk("mo", 8 * s + j, 8)), blk("wt" + H, j - 2), A.mult)
+                elif fuse:
                     tt(xs[k], lst[k], blk("wt" + H, k - 1, 256), A.mult)
                 else:
                     tt(wb[k] if home and not pet else xs[k], wb[k], xs[k], A.mult)
             if pet:
-                for k in range(3 if ks[0] == 1 else 0):
-                    mm([(ap("py" + H, 0, 256), idf, xs[k], False, k == 2)])
+                whole = H in C["pe3"]
+                top = ap("pb" + H, 0, 256) if H in C["x0p"] else wb[1]
+                if ks[0] == 1 and H in C["x0p"]:
+                    mm([(top, idf, xs[0], True, True)])
+                for k in range(3) if ks[0] == 1 else (3,) if whole else ():
+                    mm([(ap("py" + H, 0, 256), idf, xs[k], False, k == 2 and not whole)])
                 for k in ks:
-                    tt(loc[1] if k == 3 else wb[1], xs[0] if k == 1 else wb[1], xs[k], A.max)
+                    tt(loc[1] if k == 3 else top, xs[0] if k == 1 and H not in C["x0p"] else top, xs[k], A.max)
+                if whole and ks[0] == 3:
+                    mm([(ap("py" + H, 256, 512), idf, loc[1], False, True)])
             for k in ks if home and not pet else ():
                 if H in C["pre"]:
                     if k == 1:
@@ -382,12 +409,12 @@ def build(g, T, topo, rank):
         r = 16 * (t - (NV - 1)) % 128
         turn = ap("idf", r, r + 128)
         if t == 0:
-            for k in range(4):
-                mm([(ap("py" + H, 0, 256), turn, xs[k], k == 0, False)])
             for k in range(1, 4):
-                w = wb[2] if C["m0"] else loc[1]
+                w = ap("py" + H, 256, 512) if C["m0"] else loc[1]
                 tt(w if k < 3 else loc[1], xs[0] if k == 1 else w, xs[k], A.max)
-            mm([(ap("py" + H, 256, 512), turn, loc[1], False, False)])
+            for k in range(4):
+                sums.append((C["take"][0] + k // 2, h, (ap("py" + H, 0, 256), turn, xs[k], k == 0, False)))
+            sums.append((C["take"][0] + 1, h, (ap("py" + H, 256, 512), turn, loc[1], False, False)))
             return
         own = T.cores[(rank - t) % nr]
 
@@ -401,8 +428,17 @@ def build(g, T, topo, rank):
         sent[0] += n
         n = C["cut"][0]
         for k in range(n):
-            mm([(blk("py" + H, k, 512 // n), turn, blk("smi", n * (s - 2) + k, 512 // n), False,
-                 t == NV - 2 and k == n - 1 and H not in C["pet"])])
+            sums.append((C["take"][t], h, (blk("py" + H, k, 512 // n), turn, blk("smi", n * (s - 2) + k, 512 // n), False,
+                                           t == NV - 2 and k == n - 1 and H not in C["pet"])))
+
+    def take_up(t):
+        after, was = len(ops) - 1, list(cur)
+        for x in [x for x in sums if x[0] <= t]:
+            cur[:] = [x[1], min(t, NV - 1), "sum"]
+            mm([x[2]])
+            ops[-1]["soft"] = [after]
+            sums.remove(x)
+        cur[:] = was
 
     features(0)
     for t in range(NV):
@@ -418,42 +454,72 @@ def build(g, T, topo, rank):
                 features(t, [rin])
             SC = ap(PB, 256, 512)
             n = C["cut"][1]
-            for k in range(n):
-                mm([(blk(PB, n + k, 256 // n), idf, blk("act", n * h + k, 256 // n), k == 0, False)])
+            costs = [(blk(PB, n + k, 256 // n), idf, blk("act", n * h + k, 256 // n), k == 0, False) for k in range(n)]
+            for x in costs if H not in C["c1b"] or t == 0 and C["y0"] else ():
+                mm([x])
             for k in range(4):
                 i0 = ind(ap("mn"), ap(lb, l0 + 16 * k, l0 + 16 * k + 16))
                 o, v = (ap("c0s" + H), -0.5 + 0.5 / U) if k == 0 and t else (blk("mcg" + H, k, 256), 159.5 + 0.5 / U)
                 if C["mce" if t else "mc0"][h][k] == "S":
                     act(o, i0, scale=1 / U, bias=v)
+                elif C["mce" if t else "mc0"][h][k] == "B":
+                    act(blk("mcg" + H, 2 * k), ind(ap("mn"), ap(lb, l0 + 16 * k, l0 + 16 * k + 8)), scale=1 / U, bias=v)
+                    ts(blk("mcg" + H, 2 * k + 1), ind(ap("mn"), ap(lb, l0 + 16 * k + 8, l0 + 16 * k + 16)), 1 / U, A.mult, v, A.add)
                 else:
                     ts(o, i0, 1 / U, A.mult, v, A.add)
-            cbank = [ap("py" + H, 0, 256), ap(PA, 0, 256), ap(PC, 0, 256), ap(PA, 256, 512)]
+            cbank = [ap("py" + H, 0, 256), ap(PB if H in C["c1b"] else PA, 0, 256), ap(PC, 0, 256), ap(PA, 256, 512)]
             low = ap("c0s" + H)
-            for k in range(1 if t else 0, 4):
+            if t == 0 and C["y0"]:
+                for k in range(2):
+                    c = blk("py" + H, k, 256)
+                    mm([(c, ap("one", p1=1), ap("cm", p1=1), k == 0, False), (c, ("sel0", (h, k, every), 0, 64), ap("r0", p1=64), False, False)])
+                for k in range(2):
+                    mm([(blk("py" + H, k, 256), idb, blk("mcg" + H, k, 256), False, k == 1)])
+                (act if C["c0"][h] == "S" else cp)(low, blk("py" + H, 0, 256))
+                tt(ap("m1" + H), blk("py" + H, 1, 256), low, A.min)
+                low = ap("m1" + H)
+            for k in range(1 if t else 2 if C["y0"] else 0, 4):
                 c = cbank[k]
-                lst = [(c, idb, blk("mcg" + H, k, 256), True, False)]
                 if t == 0:
-                    lst.append((c, ap("one", p1=1), ap("cm", p1=1), False, False))
-                    lst.append((c, ("sel0", (h, k, every), 0, 64), ap("r0", p1=64), False, True))
+                    lst = [(c, ap("one", p1=1), ap("cm", p1=1)), (c, ("sel0", (h, k, every), 0, 64), ap("r0", p1=64))]
+                elif k < 3 and C["ahead"]:
+                    if k == 1:
+                        mm([(ap(PB, 256, 384, p1=48), blk("ei", s - 2, 48), idb, True, True)])
+                        if C["ahead"][h] == "S":
+                            act(ap("re" + H, p1=48), ap(PB, 256, 384, p1=48), scale=-1.0)
+                        else:
+                            ts(ap("re" + H, p1=48), ap(PB, 256, 384, p1=48), -1.0, A.mult)
+                    lst = [(bit(c, b), ("sel0", (b, k, every), 0, 48), ap("re" + H, p1=48)) for b in range(2)]
                 else:
-                    for b in range(2):
-                        lst.append((bit(c, b), blk("sell", 3 * b + k - 1, p1=64), blk("ri", s - 2, p1=64), False, b == 1))
-                mm(lst)
+                    lst = [(bit(c, b), blk("selp", 3 * b + k - 1), rin) for b in range(2)]
+                if str(k) in C["res"][t > 0]:
+                    mm([x + (j == 0, False) for j, x in enumerate(lst)])
+                    mm([(c, idb, blk("mcg" + H, k, 256), False, True)])
+                elif t and (k < C["early"][h] or C["ahead"]):
+                    mm([(c, idb, blk("mcg" + H, k, 256), True, False)])
+                    mm([x + (False, j == 1) for j, x in enumerate(lst)])
+                else:
+                    mm([(c, idb, blk("mcg" + H, k, 256), True, False)] + [x + (False, j == 1) for j, x in enumerate(lst)])
                 if k == 0:
                     low = ap("c0s" + H)
                     (act if C["c0"][h] == "S" else cp)(low, c)
                 else:
                     tt(ap("m%d" % k + H), c, low, A.min)
                     low = ap("m%d" % k + H)
+                for x in costs if k == 1 and H in C["c1b"] else ():
+                    mm([x])
+            if C["ahead"] and s == 1:
+                for b in range(2):
+                    paint(apx("sel0", b, slice(1, 3), every), [[0, 256]], 0, -160.0)
             HI = ap(PC, 256, 320)
-            (act if "l" in C["sx"] else cp)(ap("ofl" + H), ap(lb, l0, l0 + 64))
-            mm([(HI, idf, ap("ofl" + H), True, False)])
+            act(ap("ofl" + H), ap(lb, l0, l0 + 64), bias=-U / 2)
+            mm([(HI, ap("idq"), ap("ofl" + H), True, False)])
             mm([(blk(PB, 2 + b), bit(ap("m3" + H), b), idb, False, b == 1) for b in range(2)])
             scan(ap("rr" + H, 1, 257), ap("z16"), SC, A.add, A.min)
             tt(ap("ff" + H), ap("rr" + H, 0, 256), SC, A.is_gt)
             scan(ap("tp" + H), ap("p16"), ap("ff" + H), A.subtract, A.max)
             for b in range(2):
-                (act if C["zh"][b] == "S" else cp)(ap("zh" + H, 16 + b, 144, 16), ap("tp" + H, 128 * b + 15, 128 * b + 128, 16))
+                {"S": act, "V": cp, "G": gcp}[C["zh"][b] if t else "V"](ap("zh" + H, 16 + b, 144, 16), ap("tp" + H, 128 * b + 15, 128 * b + 128, 16))
             mm([(bit(ap(PA, 0, 256), b), blk("ff" + H, b), idb, True, True) for b in range(2)])
             on = C["on"][h]
             if "f" in on:
@@ -461,7 +527,10 @@ def build(g, T, topo, rank):
             else:
                 act(ap("ft" + H), ap(PA, 0, 256), scale=col(8), bias=col(12))
             mm([(HI, ap("zh" + H, 16 - 2 * x, 144 - 2 * x), blk("hsel", x, 64), False, x == 7) for x in range(8)])
-            (cp if "2" in on else act)(ap("of2" + H), HI)
+            if "2" in on:
+                ts(ap("of2" + H), HI, U / 2, A.add)
+            else:
+                act(ap("of2" + H), HI, bias=U / 2)
             mm([(ap(PA, 256, 512), ap("lm"), ap("ft" + H), True, True)])
             um = C["um"][h]
             if "k" in on:
@@ -481,7 +550,7 @@ def build(g, T, topo, rank):
             mm([(AA, ap("one", p1=1), ap("ca", p1=1), True, False)])
             if t == 0:
                 mm([(K, ap("r0", 0, 128), ap("uc"), True, False)]
-                   + [(K, bit(ap("r0"), b), ap("rm0", 8 + 144 * h - 8 * b, 136 + 144 * h - 8 * b), False, False) for b in range(2)])
+                   + [(K, bit(ap("r0", p1=64), b), ap("rm0", 8 + 144 * h - 8 * b, 136 + 144 * h - 8 * b, p1=64), False, False) for b in range(2)])
             else:
                 mm([(K, rin, ap("rm"), True, False)])
             for k in range(4):
@@ -496,8 +565,21 @@ def build(g, T, topo, rank):
                     act(ap(n + H), AA, bias=v)
             mm([(K, idf, ap("af" + H), False, False)])
             mm([(K, ap("idc"), ap("cst" + H), False, True)])
+            if h == 1:
+                take_up(t)
             tt(ap("ds" + H), AA, ap("cst" + H), A.subtract)
             xx = "xx" + H
+            to, early = nxt if t < NV - 1 else last, C["early"][h]
+
+            def send(k0, k1, e, sem):
+                x = ap("mo", 64 * s + 16 * k0, 64 * s + 16 * k1)
+                if e == "S":
+                    act(x, ap(PB, 16 * k0, 16 * k1), bias=U / 2)
+                elif e:
+                    ts(x, ap(PB, 16 * k0, 16 * k1), U / 2, A.add)
+                if sem:
+                    write(to, x, ap("mi", 64 * s + 16 * k0, 64 * s + 16 * k1), sem)
+
             cost = dict(scale=-1.0 / (STEP * U), bias=130 + TOP / STEP - 0.25)
             for k in range(4):
                 d = apx("sall" + H, k, every)
@@ -509,54 +591,69 @@ def build(g, T, topo, rank):
                 for k0, k1 in C["conv"]:
                     if k1 != k + 1:
                         continue
-                    o, i0 = ap("zl" + H, 16 + 128 * k0, 16 + 128 * k1, 8), apx("sall" + H, slice(k0, k1), every)
-                    if C["z3"][k] == "S":
-                        act(o, i0, bias=-U / 2)
-                    else:
-                        ts(o, i0, -U / 2, A.add)
+                    pair = str(k) in C["pair"][h]
+                    for e in range(2 if pair else 1):
+                        o, i0 = ap("zl" + H, 16 + 2 * e + 128 * k0, 16 + 128 * k1, 8), apx("sall" + H, slice(k0, k1), every)
+                        if C["z3"][h][k] == "S":
+                            act(o, i0, **(dict(scale=col(16 + 2 * e), bias=col(10 + 9 * e)) if pair else dict(bias=-U / 2)))
+                        elif pair:
+                            ts(o, i0, -U / 2, A.add, col(16 + 2 * e), A.mult)
+                        else:
+                            ts(o, i0, -U / 2, A.add)
                     for j in range(k0, k1):
-                        mm([(ap(PB, 16 * j, 16 * j + 16), ap("zl" + H, 16 + 128 * j - 2 * x, 144 + 128 * j - 2 * x), ap("idq", x, 128, 8),
-                             x == 0, x == 7) for x in range(8)])
+                        n, pick = (4, "id2") if pair else (8, "idq")
+                        mm([(ap(PB, 16 * j, 16 * j + 16), ap("zl" + H, 16 + 128 * j - 16 // n * x, 144 + 128 * j - 16 // n * x),
+                             ap(pick, x, 16 * n, n), x == 0, x == n - 1) for x in range(n)])
+                if k == early - 1:
+                    both = C["ahead"] and t < NV - 1
+                    send(0, early, C["eng"][h], None if both else "er%d" % s)
+                    if C["ahead"]:
+                        act(ap(xx, 64, 112), ap("so" + H, 7, 384, 8), scale=-cost["scale"], bias=-cost["bias"])
+                    if both:
+                        tt(apx("eo", s, slice(16, 48)), ap(xx, 80, 112), ap(xx, 0, 32), A.add)
+                        two(to, [(ap("mo", 64 * s, 64 * s + 48), ap("mi", 64 * s, 64 * s + 48)), (apx("eo", s, every), blk("ei", s, 48))], "er%d" % s)
                 if k == 0:
                     act(ap(xx, 0, 64), ind(ap("so" + H, 0, 128), LX), **cost)
+            k = 3 if C["ahead"] else 0
             if "x" in on:
-                ts(ap(xx, 64, 128), ap("so" + H, 7, 512, 8), cost["scale"], A.mult, cost["bias"], A.add)
+                ts(ap(xx, 64 + 16 * k, 128), ap("so" + H, 128 * k + 7, 512, 8), -cost["scale"], A.mult, -cost["bias"], A.add)
             else:
-                act(ap(xx, 64, 128), ap("so" + H, 7, 512, 8), **cost)
-            to = nxt if t < NV - 1 else last
-            if "m" in C["sx"]:
-                act(blk("mo", s, 64), ap(PB, 0, 64), bias=U / 2)
-            else:
-                ts(blk("mo", s, 64), ap(PB, 0, 64), U / 2, A.add)
-            if t < NV - 1 or not C["rf"]:
-                write(to, blk("mo", s, 64), blk("mi", s, 64), "ar%d" % s)
+                act(ap(xx, 64 + 16 * k, 128), ap("so" + H, 128 * k + 7, 512, 8), scale=-cost["scale"], bias=-cost["bias"])
+            rows_first = H in C["rf"][t == NV - 1]
+            send(early, 4, "S" if H in C["sx"] else "V", None if rows_first else "ar%d" % s)
             first = len(ops) - 1
             o = ap(PA if C["rb"] == "A" else PC, 128, 256)
-            mm([(o[:2] + (p, p + 64), ap(xx, c0, c0 + 64), m, c0 == 0, c0 == 64) for p in (0, 64) for c0, m in ((0, idb), (64, ap("idn")))])
+            mm([(o[:2] + (p, p + 64), ap(xx, c0, c0 + 64), idb, c0 == 0, c0 == 64) for p in (0, 64) for c0 in (0, 64)])
             if "r" in on:
                 ts(blk("ro", s), o, RB, A.add, 0.0, A.max)
             else:
                 act(blk("ro", s), o, F.Relu, bias=RB)
             write(to, blk("ro", s), blk("ri", s), "br%d" % s)
-            if t < NV - 1 or not C["rf"]:
+            if not rows_first:
                 ops[-1]["soft"] = [first]
             else:
-                write(to, blk("mo", s, 64), blk("mi", s, 64), "ar%d" % s)
-            if t == NV - 1 or C["late"][h][t] == "0":
+                send(early, 4, None, "ar%d" % s)
+            if t < NV - 1 and C["late"][h][t] == "0":
                 payload(t, h, False)
+    take_up(NV)
+    for h in range(2):
+        cur[:] = [h, NV - 1, "home"]
+        payload(NV - 1, h, False)
     r = 16 * NV % 128
     for h in range(2):
         cur[:] = [h, NV - 1, "end"]
         for k, o in enumerate((T.ys, T.ym)):
             a = blk("yo", 2 * h + k, 256)
             b = blk("smo", 4 * (2 * NV - 2 + h) + 3, 256) if k == 0 and str(h) in C["pet"] else blk("loc%d" % h, k, 256)
-            if k or str(h) not in C["pre"]:
+            if str(h) in C["pe3"]:
+                act(a, blk("py%d" % h, k, 256))
+            elif k or str(h) not in C["pre"]:
                 tt(a, blk("py%d" % h, k, 256), b, A.add)
 
             def store(o=o, j=2 * h + k, h=h):
-                g.sync.dma_start(o[128 - r:128, 256 * h:256 * h + 256], R(blk("yo", j, 256, p1=r))).then_inc(T.sem.stored, 16)
-                g.sync.dma_start(o[0:128 - r, 256 * h:256 * h + 256], R(blk("yo", j, 256, p0=r))).then_inc(T.sem.stored, 16)
-            op("Y", store, [a], [], None, dma=("stored", 128), by=1 << 17, nd=2)
+                q[C["st"][j]].dma_start(o[128 - r:128, 256 * h:256 * h + 256], R(blk("yo", j, 256, p1=r))).then_inc(T.sem.stored, 16)
+                q[C["st"][j]].dma_start(o[0:128 - r, 256 * h:256 * h + 256], R(blk("yo", j, 256, p0=r))).then_inc(T.sem.stored, 16)
+            op(C["st"][2 * h + k], store, [a], [], None, dma=("stored", 128), by=1 << 17, nd=2)
     return ops, q, sent[0]
 
 
@@ -599,7 +696,8 @@ def times(ops, m):
             x = (m["di"] * o["nd"], m["di"] + 0.6 * m["dl"], o["by"] / m["rate"], 0.4 * m["dl"])
         elif "rows" in o:
             n = o["cost"][2]
-            x = (n * m["g"], n * m["g"] + 0.6 * m["net"], o["rows"][0] * m["row"] + o["rows"][1] / m["rate"], 0.4 * m["net"])
+            n = n * m["g"] + (m["once"] if o["visit"] < 0 else 0)
+            x = (n, n + 0.6 * m["net"], o["rows"][0] * m["row"] + o["rows"][1] / m["rate"], 0.4 * m["net"])
         else:
             c, ga, n, ns, two = o["cost"]
             c += ga * max(m["ga"], m["tti"] if two else 0)
@@ -652,6 +750,13 @@ def order(ops, tries=TRIES):
     tail = [0.0] * n
     for i in range(n - 1, -1, -1):
         tail[i] = max(dur[i], pre[i] + wire[i]) + post[i] + max([tail[k] for k in kids[i]], default=0.0)
+    ref = [i for i, o in enumerate(ops) if o["kind"][1:] in (("walk", "V", "rr0", 1), ("walk", "V", "rr1", 1)) and o["visit"] == 2]
+    for i, o in enumerate(ops):
+        tail[i] += tail[ref[0]] - tail[ref[1]] if o["half"] == 1 else 0.0
+    aside = [o["kind"][1] == "sum" or o["kind"][1] in ("first", "late", "now") and o["eng"] in "VG" for o in ops]
+    loose = [i for i, o in enumerate(ops) if o["kind"][1] in ("first", "late", "now", "sum")]
+    for i in range(n):
+        tail[i] -= CFG["fit"][0] if aside[i] else 0.0
     fixed = [1e9 - 1e6 * i if "soon" in o or "by" in o and not o["deps"] else 0.0 for i, o in enumerate(ops)]
 
     def run(pri, slack):
@@ -666,7 +771,7 @@ def order(ops, tries=TRIES):
             t0, e = min((max(free[e], min([rdy[i] for i in r])), e) for e, r in ready.items() if r)
             r = ready[e]
             i = max([j for j in r if rdy[j] <= t0], key=pri.get)
-            lim = t0 + (1.2 * (dur[i] + wire[i]) if e == "G" else min(slack, 0.5 * dur[i]))
+            lim = t0 + (1.2 * (dur[i] + wire[i]) if e == "G" else CFG["fit"][1] * dur[i] if aside[i] else min(slack, 0.5 * dur[i]))
             soon = [j for j in r if t0 < rdy[j] <= lim and pri[j] > pri[i]]
             if soon:
                 i = max(soon, key=pri.get)
@@ -742,9 +847,14 @@ def order(ops, tries=TRIES):
                     end = b
         return end, marks, done
 
+    walk = [i for i, o in enumerate(ops) if o["kind"][1:3] == ("walk", "V") and o["half"] is not None]
+
+    def worth(state):
+        return sum((s[0] + CFG["side"][1] * sum([s[2][i] for i in walk]) / len(walk)) / z for s, z in zip(state, size))
+
     def along(first, near, inside, other_end):
         move, todo = [first], [first]
-        while todo and len(move) < 6:
+        while todo and len(move) < 10:
             for j in near[todo.pop()]:
                 if inside(j) and j not in move:
                     move.append(j)
@@ -758,26 +868,38 @@ def order(ops, tries=TRIES):
             if trial % 8 == 0:
                 tm, at, why = tms[rng.integers(len(tms))], [0.0] * n, [None] * n
                 replay(ops, seq, tm, at, why)
-                i, pairs = int(np.argmax(at)), []
+                i, pairs = int(np.argmax(at)) if rng.random() < CFG["side"][0] else walk[rng.integers(len(walk))], []
                 while why[i] is not None:
                     if why[i] not in deps[i]:
                         pairs.append((why[i], i))
                     i = why[i]
+                pairs = pairs[:30] if i < 0 or rng.random() < 0.3 else pairs
                 if trial % 80 == 0:
                     seq = sorted(seq, key=lambda j: at[j])
                     state = [play(seq, tm, 0, zero, [0.0] * n) for tm in tms]
-                    total = sum(s[0] / z for s, z in zip(state, size))
+                    total = worth(state)
                     if keep is None or total < keep[0]:
                         keep = (total, seq)
                 pos = [0] * n
                 for j, x in enumerate(seq):
                     pos[x] = j
+            if not pairs:
+                continue
             p, i = pairs[rng.integers(len(pairs))]
+            up = rng.random() < 0.6
+            if rng.random() < CFG["fit"][2]:
+                x = loose[rng.integers(len(loose))]
+                waits = [j for j in seq[max(0, pos[x] - 200):pos[x] + 200] if eng[j] == eng[x] and j != x and why[j] in deps[j]]
+                if not waits:
+                    continue
+                j = waits[rng.integers(len(waits))]
+                up = pos[j] < pos[x]
+                p, i = (j, x) if up else (x, seq[pos[j] - 1])
             a, b = pos[p], pos[i]
-            if a > b:
+            if a >= b:
                 continue
             more = int(rng.random() * 12) if rng.random() < 0.3 else 0
-            if rng.random() < 0.6:
+            if up:
                 a = min(a, max([a - more, 0] + [pos[j] + 1 for j in deps[i]]))
                 move = along(i, deps, lambda j: pos[j] >= a, p)
                 if not move:
@@ -790,7 +912,7 @@ def order(ops, tries=TRIES):
                     continue
                 new = seq[:a] + [x for x in seq[a:b + 1] if x not in move] + sorted(move, key=lambda x: pos[x]) + seq[b + 1:]
             got = [play(new, tm, a // 48, s[1], s[2]) for tm, s in zip(tms, state)]
-            tried = sum(s[0] / z for s, z in zip(got, size))
+            tried = worth(got)
             if tried <= total + CFG["heat"] * (1 - trial / count) * rng.random():
                 seq, total, state = new, tried, got
                 for j in range(a, b + 1):

import numpy as np
from concourse.bass import DstId, RemoteDMATransfer
from concourse.mybir import AluOpType as A
from concourse.mybir import ActivationFunctionType as F

NV = 6
CFG = dict(
    mce=("SSSV", "SSSS"),
    conv=[(0, 2), (2, 3), (3, 4)],
    late=("00000", "11110"),
    fuse=("13", "13"), cut=(2, 1), m0=1, two=0, take=(1, 2, 3, 4, 5), pair=("3", ""), c1b="01", y0=0, bits=("", "12"), res=("0123", "3"), hv=("3", "3"), mc0=("VSSS", "VSSS"), c0="SS", rf=("01", "01"), early=(3, 3), ahead="", eng="SS", pe3="", x0p="", p0=2, rb="C", pet="01", hbm=1.0,
    mcv=(2, 3, 4),
    ch=[0, 256, 768, 1792, 2816, 3840, 4096],
    sw=[(0, 1536), (1536, 2816), (2816, 4096)],
    lags=(1350.0, 1400.0, 1450.0, 1450.0, 1500.0, 1500.0, 1550.0, 1600.0), swaps=(2500, 16000), heat=0.0005, fit=(0.0, 0.5, 0.3), side=(0.6, 0.3), z3=("SSSV", "SSSV"), zh="GG", fill="VVVGGGGGGGG", st="YYYS", on=("2xr", "2xr"), fold=(32, 700000),
    um=("", ""), pre="", sx="0",
)
HOME = 4
TRIES = 20
SCRATCH = {}
GONE = 106.0
U = 4096.0
STEP, TOP = 12.0, 2176.0
NONE = U * (TOP - STEP * 176) + 4095
WHOLE = 2.0 ** 23
LIFT = 136.0


def _sb(n, w, d, where="sbuf"):
    SCRATCH[n] = (where, [128] + (list(w) if isinstance(w, tuple) else [w]), d)


for _n, _w, _d in [
        ("xt", 8192, "int32"), ("mn", 4096, "int32"), ("p16", 256, "bfloat16"), ("cm", 256, "bfloat16"), ("bo3", 32, "float32"),
        ("payr", 4096, "bfloat16"), ("payo", 4096, "bfloat16"), ("acs", 512, "float32"), ("act", 512, "float32"),
        ("sti", (4, 32), "int32"), ("off0", 128, "uint16"), ("rsi", 256, "int32"), ("r0", 256, "bfloat16"),
        ("ci", 48, "int32"), ("cf", 24, "float32"), ("i16", 16, "float32"),
        ("onef", 256, "float32"), ("one", 128, "bfloat16"), ("idf", 256, "float32"), ("idb", 128, "bfloat16"),
        ("idq", 128, "float16"), ("id2", 64, "float16"), ("idc", 128, "bfloat16"),
        ("bo2", 36, "float32"), ("lm", 128, "bfloat16"), ("hsel", 512, "bfloat16"), ("sel0", (2, 4, 128), "bfloat16"),
        ("sell", 768, "bfloat16"), ("selp", 768, "bfloat16"),
        ("ua", 128, "bfloat16"), ("ub", 128, "bfloat16"), ("uc", 128, "bfloat16"), ("ud", 128, "bfloat16"),
        ("rm0", 280, "bfloat16"), ("rm", 128, "bfloat16"), ("ca", 128, "bfloat16"),
        ("lu", 32, "uint16"), ("z16", 256, "float32"), ("z8", 128, "float32"),
        ("mo", 12 * 64, "uint16"), ("mi", 12 * 64, "uint16"), ("ro", 12 * 128, "bfloat16"), ("ri", 12 * 128, "bfloat16"),
        ("eo", (12, 48), "bfloat16"), ("ei", 12 * 48, "bfloat16"), ("re0", 128, "bfloat16"), ("re1", 128, "bfloat16"),
        ("smo", 12 * 1024, "float32"), ("smi", 8 * 512, "float32"), ("yo", 1024, "float32")]:
    _sb(_n, _w, _d)
for _h in "01":
    for _n, _w, _d in [
            ("mcg", 1024, "bfloat16"), ("c0s", 256, "int32"), ("tp", 256, "bfloat16"), ("m1", 256, "bfloat16"), ("m2", 256, "bfloat16"),
            ("m3", 256, "bfloat16"), ("rr", 260, "float32"), ("ff", 256, "bfloat16"), ("ft", 256, "bfloat16"),
            ("msk", 256, "bfloat16"), ("gm", 1024, "float32"), ("cst", 128, "bfloat16"), ("zh", 144, "bfloat16"),
            ("ofl", 64, "float16"), ("of2", 64, "uint16"), ("ds", 128, "int32"), ("eq", 128, "bfloat16"),
            ("so", 512, "int32"), ("sall", (4, 16), "int32"), ("zl", (264, 2), "float16"),
            ("xx", 128, "bfloat16"), ("af", 128, "float32"), ("loc", 512, "float32"), ("wt", 768, "float32")]:
        _sb(_n + _h, _w, _d)
for _n in ["pa0", "pb0", "pc0", "pa1", "pb1", "pc1", "py0", "py1"]:
    _sb(_n, 512, "float32", "psum")

SEMAPHORES = (["cV", "cS", "cP", "cG", "sent", "stored"] + ["ld%d" % i for i in range(12)] + ["sw%d" % i for i in range(10)]
              + ["%s%d" % (n, i) for n in ("ar", "br", "er", "sm") for i in range(12)] + ["pp%d" % i for i in range(HOME)])

GUESS = [dict(cy=0.86, ga=1.5, tti=0, v=20, s=150, m=12, g=400, hop=170, hs=150, net=1300, row=60, rate=350, dl=1500, di=180),
         dict(cy=0.83, ga=1.2, tti=0, v=50, s=200, m=5, g=200, hop=200, hs=100, net=1000, row=30, rate=350, dl=1300, di=170),
         dict(cy=0.86, ga=1.6, tti=2, v=0, s=60, m=5, g=600, hop=150, hs=80, net=2300, row=80, rate=500, dl=1000, di=230),
         dict(cy=1.0, ga=2.05, tti=0, v=20, s=150, m=10, g=450, hop=150, hs=150, net=1400, row=60, rate=250, dl=2000, di=100)]
for _m, _v in zip(GUESS, (3000, 4000, 6000, 5000)):
    _m["once"] = _v
ONCE = 0.0


def ap(b, c0=0, c1=None, st=1, p0=0, p1=128):
    s = SCRATCH[b][1][1:]
    w = int(np.prod(s[1:]))
    return (b, (slice(c0 // w, s[0] if c1 is None else c1 // w, st),) + (slice(None),) * (len(s) - 1), p0, p1)


def apx(b, *idx):
    return (b, idx, 0, 128)


def bit(a, b):
    return (a[0], (slice(a[1][0].start + b, a[1][0].stop, 2),), a[2], a[3])


def cols(a):
    s = SCRATCH[a[0]][1][1:]
    return np.arange(int(np.prod(s))).reshape(s)[a[1]].reshape(-1)


def ncol(a):
    return len(cols(a))


def build(g, T, topo, rank):
    C = CFG
    ops, cur, nth = [], [None, -1, "walk"], {}
    q = {"V": g.vector, "S": g.scalar, "P": g.tensor, "G": g, "Y": g.sync}

    def R(a):
        if isinstance(a, (int, float)) or a is None:
            return a
        if a[0] == "ind":
            return R(a[1]).indirect(R(a[2]))
        idx = tuple(slice(x.start, x.stop) if isinstance(x, slice) and x.step == 1 else x for x in a[1])
        return T[a[0]][(slice(a[2], a[3]),) + idx]

    def op(eng, fn, rd, wr, cost, **kw):
        flat = []
        for a in rd:
            if isinstance(a, tuple):
                flat += [a[1], a[2]] if a[0] == "ind" else [a]
        key = (cur[0], cur[2], eng, wr[0][0] if wr else None)
        nth[key] = nth.get(key, 0) + 1
        ops.append(dict(half=cur[0], visit=cur[1], kind=key + (nth[key],), eng=eng, fn=fn, rd=flat, wr=wr, cost=cost, **kw))

    def vcost(out, ins, tt=False):
        n = ncol(out)
        if ins and ins[0][0] == "ind":
            return (0, n, 1, 30, tt)
        c = 0.5 if all(SCRATCH[a[0]][2] in ("bfloat16", "uint16", "float16") for a in [out] + ins) else 1.0
        if tt and not any(SCRATCH[a[0]][0] == "psum" for a in ins):
            c *= 2
        return (max(64, n * c), 0, 1, 0, False)

    def tt(out, i0, i1, o):
        op("V", lambda: g.vector.tensor_tensor(R(out), R(i0), R(i1), o), [i0, i1], [out], vcost(out, [i0, i1], True))

    def ts(out, i0, s1, o0, s2=None, o1=None):
        if o1 is None:
            fn = lambda: g.vector.tensor_scalar(R(out), R(i0), R(s1), None, o0)
        else:
            fn = lambda: g.vector.tensor_scalar(R(out), R(i0), R(s1), R(s2), o0, o1)
        op("V", fn, [i0, s1, s2], [out], vcost(out, [i0]))

    def cp(out, i0):
        op("V", lambda: g.vector.tensor_copy(R(out), R(i0)), [i0], [out], vcost(out, [i0]))

    def ms(out, v):
        op("V", lambda: g.vector.memset(R(out), v), [], [out], vcost(out, []))

    def scan(out, d0, d1, o0, o1, first=0.0):
        op("V", lambda: g.vector.tensor_tensor_scan(R(out), R(d0), R(d1), first, o0, o1), [d0, d1], [out], vcost(out, [d0, d1]))

    def act(out, i0, f=F.Identity, bias=0.0, scale=1.0, more=0):
        n = ncol(out)
        op("S", lambda: g.scalar.activation(R(out), R(i0), f, bias=R(bias), scale=R(scale)), [i0, bias, scale], [out],
           (0, n, 0, 75, False) if i0[0] == "ind" else (n, 0, 1, more, False))

    def mm(lst):
        def fn():
            h = None
            for (o, l, r, s0, s1) in lst:
                h = g.tensor.matmul(R(o), R(l), R(r), s0, s1)
            return h
        d = sum(max(min(64, ncol(l)), ncol(r)) * (2 if SCRATCH[l[0]][2] == "float32" else 0.5) for (o, l, r, s0, s1) in lst)
        op("P", fn, [x[1] for x in lst] + [x[2] for x in lst], [x[0] for x in lst], (d, 0, len(lst), 30, False))

    def iota(out, pat, base, cmul):
        if SCRATCH[out[0]][2] == "int32":
            fn = lambda: g.iota(R(out), pat, base, cmul)
        else:
            fn = lambda: g.iota(R(out), pat, base, cmul, allow_small_or_imprecise_dtypes=True)
        op("G", fn, [], [out], (2.4 * ncol(out), 0, 0, 170, False))

    def asel(out, i0, pat, o, base, cmul, fill=0.0):
        op("G", lambda: g.affine_select(R(out), R(i0), pat, o, fill, base, cmul), [i0], [out], (2.4 * ncol(out), 0, 0, 220, False))

    def gcp(out, i0):
        asel(out, i0, [[0, ncol(out)]], A.is_ge, 0, 0)

    def paint(x, pat, base, v):
        asel(x, x, pat, A.not_equal, base, -1, v)

    def load(sem, pairs, wr, by, rd=()):
        def fn():
            for (o, i) in pairs:
                g.sync.dma_start(o, i).then_inc(T.sem[sem], 16)
        op("Y", fn, list(rd), wr, None, dma=(sem, 16 * len(pairs)), by=by / (C["hbm"] if sem[0] == "l" else 1), nd=len(pairs))

    def turned(sem, c0, c1):
        load(sem, [(T.payr[16:128, c0:c1], T.pay[0:112, c0:c1]), (T.payr[0:16, c0:c1], T.pay[112:128, c0:c1])], [ap("payr", c0, c1)],
             256 * (c1 - c0))

    ind = lambda w, o: ("ind", w, o)
    col = lambda j: ap("cf", j, j + 1)
    blk = lambda n, j, w=128, p0=0, p1=128: ap(n, w * j, w * j + w, p0=p0, p1=p1)
    every = slice(None)
    CH, PW = C["ch"], 4096 // HOME

    for i in range(len(CH) - 1):
        load("ld%d" % i, [(T.xt[:, 4096 + CH[i]:4096 + CH[i + 1]], T.arcs[:, CH[i]:CH[i + 1]])], [ap("xt", 4096 + CH[i], 4096 + CH[i + 1])],
             512 * (CH[i + 1] - CH[i]))
    load("ld8", [(T.sti[:], T.st0[:])] + [(T.rsi[16 * k:16 * k + 16, :], T.rs0[:, 512 * k:512 * k + 512]) for k in range(4)],
         [apx("sti", every, every), ap("rsi")], 1 << 17)
    load("ld9", [(T.acs[:], T.ac[:])], [ap("acs")], 1 << 18)
    if not C["p0"]:
        turned("ld10", 0, PW)

    start = len(ops)
    idf, idb = ap("idf", 0, 128), ap("idb")
    sh, an = A.logical_shift_right, A.bitwise_and
    P0, P16, P2 = ap("ci", 0, 1), ap("ci", 1, 2), ap("ci", 2, 3)
    LABEL, GROUP, PAIR, NEXT, UPPER, SLOT, SECOND = [col(j) for j in range(7)]
    fields = [(P0, 0, 15), (P0, 4, 7), (P0, 1, 7), (P16, 3, 14), (P0, 3, 1), (P0, 4, 3), (P0, 6, 1), (P0, 0, 49), (P2, 0, 14), (P0, 0, 1)]

    def field(j):
        ts(ap("ci", 16 + j, 17 + j), fields[j][0], fields[j][1], sh, fields[j][2], an)

    ms(ap("onef", 0, 128), 1.0)
    iota(ap("ci", 0, 4), [[2, 2], [16, 2]], 0, 1)
    ms(ap("sel0"), 0.0)
    field(0)
    act(col(11), ap("ci", 16, 17), F.Exp, scale=0.8, more=1300)
    asel(idf, ap("onef", 0, 128), [[-1, 128]], A.is_equal, 0, 1)
    iota(ap("lm"), [[1, 8], [0, 16]], 0, 0)
    iota(ap("ua"), [[0, 8], [1, 8], [0, 2]], 0, 0)
    paint(ap("sel0"), [[1, 2], [2, 32], [0, 16]], 0, 1.0)
    field(1)
    field(2)
    cp(ap("cf", 0, 3), ap("ci", 16, 19))
    ms(ap("hsel"), 0.0)
    fills = [(ap("r0"), 1), (ap("one"), 1), (ap("cm"), -160), (ap("z16"), 0), (ap("z16", 0, 256, 16), 1000), (ap("rr0", 0, 1), 0),
             (ap("rr1", 0, 1), 0), (ap("p16"), 1), (ap("p16", 0, 256, 16), 2), (ap("zh0"), 0), (ap("zh1"), 0)]
    for j, (x, v) in enumerate(fills):
        if C["fill"][j] == "V":
            ms(x, float(v))
        else:
            iota(x, [[0, ncol(x)]], v, 0)
    paint(ap("hsel"), [[1, 8], [0, 4], [8, 16]], 0, U)
    act(idb, idf)
    ts(ap("lm"), ap("lm"), GROUP, A.is_equal, -1.0, A.mult)
    ts(ap("ua"), ap("ua"), PAIR, A.not_equal, 0.5, A.subtract)
    tt(ap("lm"), ap("lm"), ap("ua"), A.mult)
    act(ap("lm"), ap("lm"), scale=col(11))
    ts(col(12), LABEL, 0.0, A.is_equal)
    ts(col(8), LABEL, 0.0, A.not_equal)
    for i in range(start, len(ops)):
        ops[i]["soon"] = True
    iota(ap("ub"), [[1, 16], [0, 2], [16, 4]], 0, 0)
    iota(ap("ci", 8, 16), [[2, 8]], 0, 0)
    ms(ap("uc"), 0.0)
    act(ap("idf", 128, 256), idf)
    for n, v in (("idc", -1.0 - STEP), ("idq", 1.0)):
        act(ap(n), idf, scale=v)
    for j in range(3, len(fields)):
        field(j)
    cp(ap("cf", 3, 8), ap("ci", 19, 24))
    ROW = col(21)
    ts(ROW, ap("ci", 24, 25), col(7), A.add)
    ODD = ap("ci", 25, 26)
    ts(col(16), ODD, -1.0, A.mult, 1.0, A.add)
    ts(col(17), ODD, 2.0 ** -14, A.mult, -2.0 ** -15, A.add)
    cp(col(18), ODD)
    ts(col(10), col(16), -U / 2, A.mult)
    ts(col(19), ODD, -U / 2, A.mult)
    tt(ap("id2"), ap("idf", 0, 128, 2), ap("idf", 1, 128, 2), A.add)
    iota(ap("bo2"), [[0, 36]], 0, 0)
    for u in range(2):
        ts(ap("bo2", 2 + u, 34, 4), ap("ci", 8, 16), NEXT, A.is_equal, col(16 + u), A.mult)
    ts(ap("lu", 0, 8), ap("ci", 8, 16), UPPER, A.add)
    ts(col(9), LABEL, 8.0, A.mult, 7.0, A.add)
    ts(ap("lu", 8, 12), ap("onef", 0, 4), col(9), A.mult)
    L1, LX = ap("lu", 0, 8), ap("lu", 8, 12)
    iota(ap("ca"), [[0, 128]], int(LIFT * U), 0)
    iota(ap("z8"), [[0, 128]], int(2 * WHOLE) - 1, 0)
    iota(ap("z8", 0, 128, 8), [[0, 16]], int(NONE), 0)
    ts(col(13), SLOT, 0.0, A.is_gt)
    ts(col(14), SECOND, -1.0, A.mult, GONE - 1, A.add)
    ts(col(15), col(13), col(14), A.mult, 1.0, A.add)
    RB = col(15)
    ms(ap("uc", p0=64, p1=66), (TOP + (STEP + 1) * LIFT) * U - WHOLE)
    iota(ap("ud"), [[0, 16], [-int(U), 8]], 0, 0)
    act(ap("uc", p0=64, p1=65), ap("ud", p0=64, p1=65))
    ts(col(20), SECOND, STEP * U * 83, A.mult, -STEP * U * 41, A.add)
    iota(ap("rm0"), [[0, 280]], 0, 0)
    ts(col(22), ODD, STEP * U, A.mult, -STEP * U, A.add)
    ts(col(23), ODD, -STEP * U, A.mult)
    for h in range(2):
        ts(ap("rm0", 8 + 136 * h, 136 + 136 * h), ap("ub"), ROW, A.is_equal, col(22 + h), A.mult)
    ts(ap("ub"), ap("ub"), ROW, A.is_equal, col(20), A.mult)
    act(ap("ub", p1=1), ap("onef", 0, 128, p1=1), scale=-STEP * U * 64)
    iota(ap("ub", 0, 128, 4), [[0, 32]], 0, 0)
    tt(ap("rm"), ap("ub"), ap("uc"), A.add)
    for n in ("zl0", "zl1"):
        for c0 in (0, 264):
            act(ap(n, c0, c0 + 264), ap("hsel", 0, 264), scale=0.0)
    for b in range(2):
        act(blk("selp", b, 384), apx("sel0", b, slice(1, 4), every), scale=41.0)
    paint(ap("selp"), [[1, 2], [2, 24], [0, 16]], 80, -42.0)
    act(ap("selp", p1=1), ap("selp", p1=1), scale=0.0, bias=64.0 - 160)
    banks, used, start = ["pa0", "pa1", "pb0", "pb1", "pc0", "pc1"], 0, len(ops)
    for i in range(len(CH) - 1):
        c = (CH[i], CH[i + 1])
        for c0 in range(c[0], c[1], 512):
            c1 = min(c0 + 512, c[1])
            b = ap(banks[used % len(banks)], 0, c1 - c0)
            used += 1
            act(b, ap("xt", 4096 + c0, 4096 + c1), F.Relu, scale=2.0 ** -15, bias=-0.5625)
            if c0 == c[0]:
                ts(ap("xt", *c), ap("xt", 4096 + c[0], 4096 + c[1]), 32767, an)
            tt(ap("mn", c0, c1), b, ap("xt", c0, c1), A.min)
    for i, (c0, c1) in enumerate(C["sw"]):
        load("sw%d" % (2 * i), [(T.xt[0:128:2, 4096 + c0:4096 + c1], T.xt[1:128:2, c0:c1])],
             [ap("xt", 4096 + c0, 4096 + c1)], 256 * (c1 - c0), [ap("xt", c0, c1)])
        load("sw%d" % (2 * i + 1), [(T.xt[1:128:2, c0:c1], T.arcs[0:128:2, c0:c1])], [ap("xt", c0, c1)], 256 * (c1 - c0))
    if C["p0"]:
        turned("ld10", 0, PW)
        ops[-1]["soft"] = [len(ops) - 1 - C["p0"]]
    turned("ld11", PW, 4096)
    ops[-1]["soft"] = [len(ops) - 2, len(ops) - 3]
    act(ap("r0", p1=64), ap("rsi", p1=64))
    for h in range(2):
        cp(blk("off0", h, 64), apx("sti", every, slice(16 * h, 16 * h + 16)))
        bank = "py%d" % h
        for b in range(2):
            o, i = blk(bank, b), bit(blk("acs", h, 256), b)
            op("P", lambda o=o, i=i: g.tensor.transpose(R(o), R(i), R(idf)), [i, idf], [o], (256, 0, 1, 30, False))
        act(blk("act", h, 256), ap(bank, 0, 256))

    nr = len(T.cores)
    me, nxt = T.cores[rank], T.cores[(rank + 1) % nr]
    last = T.cores[(rank - (NV - 1)) % nr]

    def dst(c):
        a = topo.addr(c)
        return DstId(rid=a[0], pnc=a[1])

    def emask(c, part, of):
        e = topo.engines(me, c)
        k = len(e) // of
        return int(sum(1 << x for x in e[part * k:part * k + k])), k

    sent, sums = [0], []

    def write(core, src, to, sem, after=()):
        def fn():
            a = topo.addr(core)
            g.remote_dma(R(to), R(src), T.sem[sem], T.sem.sent, a[1], a[0], emask(core, 0, 1)[0])
        n = emask(core, 0, 1)[1]
        op("G", fn, [src] + list(after), [to], (0, 0, 1, 0, False), dma=(sem, n), rows=(8, 256 * ncol(src)))
        sent[0] += n

    def two(core, pairs, sem):
        def fn():
            g.remote_dma_fused([RemoteDMATransfer(dst_ids=[dst(core)], dma_engine_mask=emask(core, k, 2)[0], remote_sem=T.sem[sem],
                                                  src=R(x[0]), dst=R(x[1])) for k, x in enumerate(pairs)], local_sem=T.sem.sent)
        n = 2 * emask(core, 0, 2)[1]
        op("G", fn, [x[0] for x in pairs], [x[1] for x in pairs], (0, 0, 1.3, 0, False), dma=(sem, n), rows=(16, 512 * ncol(pairs[0][0])))
        sent[0] += n

    def features(j, after=()):
        write(last, blk("payr", j, PW), blk("payo", j, PW), "pp%d" % j, after)

    def payload(t, h, late):
        H, s = str(h), 2 * t + h
        PA, PC = "pa" + H, "pc" + H
        home = t == NV - 1
        cur[2] = "home" if home else "first" if t == 0 else "late" if late else "now"
        pet = home and H in C["pet"]
        rows = blk("ri" if home else "ro", s)
        xs = [blk("smo", 4 * s + k, 256) for k in range(4)]
        lst = [ind(ap("payo" if home else "payr"), blk("mi" if home else "mo", 4 * s + k, 16)) for k in range(4)]
        wb = [None, ap(PC, 0, 256), ap(PC, 256, 512), ap(PC, 0, 256) if late else ap(PA, 256, 512)]
        loc = [blk("loc" + H, j, 256) for j in range(2)]
        (cp if home and "0" in C["hv"][h] else act)(xs[0], lst[0])
        for ks in ((1, 2), (3,)):
            fuse = not home and str(ks[0]) in C["fuse"][h]
            for k in ks:
                if not fuse:
                    (cp if home and str(k) in C["hv"][h] else act)(xs[k], lst[k])
                mm([(bit(wb[k], b), blk("selp", 3 * b + k - 1), rows, True, True) for b in range(2)])
            w = ap(PC) if ks[0] == 1 else wb[3]
            act(ap("wt" + H, 256 * ks[0] - 256, 256 * ks[-1]) if fuse else w, w, F.Exp, scale=-0.125, bias=-20.0)
            for k in ks:
                if fuse and ks[0] == 1 and C["two"]:
                    if k == 1:
                        tt(ap("smo", 1024 * s + 256, 1024 * s + 768), ind(ap("payr"), ap("mo", 64 * s + 16, 64 * s + 48)), ap("wt" + H, 0, 512),
                           A.mult)
                elif fuse and str(k) in C["bits"][h]:
                    for j in (2 * k, 2 * k + 1):
                        tt(blk("smo", 8 * s + j), ind(ap("payr"), blk("mo", 8 * s + j, 8)), blk("wt" + H, j - 2), A.mult)
                elif fuse:
                    tt(xs[k], lst[k], blk("wt" + H, k - 1, 256), A.mult)
                else:
                    tt(wb[k] if home and not pet else xs[k], wb[k], xs[k], A.mult)
            if pet:
                whole = H in C["pe3"]
                top = ap("pb" + H, 0, 256) if H in C["x0p"] else wb[1]
                if ks[0] == 1 and H in C["x0p"]:
                    mm([(top, idf, xs[0], True, True)])
                for k in range(3) if ks[0] == 1 else (3,) if whole else ():
                    mm([(ap("py" + H, 0, 256), idf, xs[k], False, k == 2 and not whole)])
                for k in ks:
                    tt(loc[1] if k == 3 else top, xs[0] if k == 1 and H not in C["x0p"] else top, xs[k], A.max)
                if whole and ks[0] == 3:
                    mm([(ap("py" + H, 256, 512), idf, loc[1], False, True)])
            for k in ks if home and not pet else ():
                if H in C["pre"]:
                    if k == 1:
                        tt(loc[0], ap("py" + H, 0, 256), xs[0], A.add)
                    tt(loc[0] if k < 3 else blk("yo", 2 * h, 256), wb[k], loc[0], A.add)
                else:
                    tt(loc[0], wb[k], xs[0] if k == 1 else loc[0], A.add)
                tt(loc[1], wb[k], xs[0] if k == 1 else loc[1], A.max)
        if home:
            return
        r = 16 * (t - (NV - 1)) % 128
        turn = ap("idf", r, r + 128)
        if t == 0:
            for k in range(1, 4):
                w = ap("py" + H, 256, 512) if C["m0"] else loc[1]
                tt(w if k < 3 else loc[1], xs[0] if k == 1 else w, xs[k], A.max)
            for k in range(4):
                sums.append((C["take"][0] + k // 2, h, (ap("py" + H, 0, 256), turn, xs[k], k == 0, False)))
            sums.append((C["take"][0] + 1, h, (ap("py" + H, 256, 512), turn, loc[1], False, False)))
            return
        own = T.cores[(rank - t) % nr]

        def fold():
            g.remote_dma_fused([
                RemoteDMATransfer(dst_ids=[dst(own)], dma_engine_mask=emask(own, k, 2)[0], remote_sem=T.sem["sm%d" % s],
                                  srcs=[R(x) for x in xs], dst=R(blk("smi", 2 * (s - 2) + k, 256)), alu_op=1 + k)
                for k in range(2)], local_sem=T.sem.sent)
        n = 2 * emask(own, 0, 2)[1]
        op("G", fold, xs, [blk("smi", s - 2, 512)], (0, 0, 1.5, 0, False), dma=("sm%d" % s, n), rows=C["fold"])
        sent[0] += n
        n = C["cut"][0]
        for k in range(n):
            sums.append((C["take"][t], h, (blk("py" + H, k, 512 // n), turn, blk("smi", n * (s - 2) + k, 512 // n), False,
                                           t == NV - 2 and k == n - 1 and H not in C["pet"])))

    def take_up(t):
        after, was = len(ops) - 1, list(cur)
        for x in [x for x in sums if x[0] <= t]:
            cur[:] = [x[1], min(t, NV - 1), "sum"]
            mm([x[2]])
            ops[-1]["soft"] = [after]
            sums.remove(x)
        cur[:] = was

    features(0)
    for t in range(NV):
        for h in range(2):
            H = str(h)
            cur[:] = [h, t, "walk"]
            PA, PB, PC = "pa" + H, "pb" + H, "pc" + H
            s = 2 * t + h
            nth.clear()
            lb, l0 = ("off0", 64 * h) if t == 0 else ("mi", 64 * (s - 2))
            rin = blk("ri", s - 2) if t else None
            if h == 1 and 0 < t < HOME:
                features(t, [rin])
            SC = ap(PB, 256, 512)
            n = C["cut"][1]
            costs = [(blk(PB, n + k, 256 // n), idf, blk("act", n * h + k, 256 // n), k == 0, False) for k in range(n)]
            for x in costs if H not in C["c1b"] or t == 0 and C["y0"] else ():
                mm([x])
            for k in range(4):
                i0 = ind(ap("mn"), ap(lb, l0 + 16 * k, l0 + 16 * k + 16))
                o, v = (ap("c0s" + H), -0.5 + 0.5 / U) if k == 0 and t else (blk("mcg" + H, k, 256), 159.5 + 0.5 / U)
                if C["mce" if t else "mc0"][h][k] == "S":
                    act(o, i0, scale=1 / U, bias=v)
                elif C["mce" if t else "mc0"][h][k] == "B":
                    act(blk("mcg" + H, 2 * k), ind(ap("mn"), ap(lb, l0 + 16 * k, l0 + 16 * k + 8)), scale=1 / U, bias=v)
                    ts(blk("mcg" + H, 2 * k + 1), ind(ap("mn"), ap(lb, l0 + 16 * k + 8, l0 + 16 * k + 16)), 1 / U, A.mult, v, A.add)
                else:
                    ts(o, i0, 1 / U, A.mult, v, A.add)
            cbank = [ap("py" + H, 0, 256), ap(PB if H in C["c1b"] else PA, 0, 256), ap(PC, 0, 256), ap(PA, 256, 512)]
            low = ap("c0s" + H)
            if t == 0 and C["y0"]:
                for k in range(2):
                    c = blk("py" + H, k, 256)
                    mm([(c, ap("one", p1=1), ap("cm", p1=1), k == 0, False), (c, ("sel0", (h, k, every), 0, 64), ap("r0", p1=64), False, False)])
                for k in range(2):
                    mm([(blk("py" + H, k, 256), idb, blk("mcg" + H, k, 256), False, k == 1)])
                (act if C["c0"][h] == "S" else cp)(low, blk("py" + H, 0, 256))
                tt(ap("m1" + H), blk("py" + H, 1, 256), low, A.min)
                low = ap("m1" + H)
            for k in range(1 if t else 2 if C["y0"] else 0, 4):
                c = cbank[k]
                if t == 0:
                    lst = [(c, ap("one", p1=1), ap("cm", p1=1)), (c, ("sel0", (h, k, every), 0, 64), ap("r0", p1=64))]
                elif k < 3 and C["ahead"]:
                    if k == 1:
                        mm([(ap(PB, 256, 384, p1=48), blk("ei", s - 2, 48), idb, True, True)])
                        if C["ahead"][h] == "S":
                            act(ap("re" + H, p1=48), ap(PB, 256, 384, p1=48), scale=-1.0)
                        else:
                            ts(ap("re" + H, p1=48), ap(PB, 256, 384, p1=48), -1.0, A.mult)
                    lst = [(bit(c, b), ("sel0", (b, k, every), 0, 48), ap("re" + H, p1=48)) for b in range(2)]
                else:
                    lst = [(bit(c, b), blk("selp", 3 * b + k - 1), rin) for b in range(2)]
                if str(k) in C["res"][t > 0]:
                    mm([x + (j == 0, False) for j, x in enumerate(lst)])
                    mm([(c, idb, blk("mcg" + H, k, 256), False, True)])
                elif t and (k < C["early"][h] or C["ahead"]):
                    mm([(c, idb, blk("mcg" + H, k, 256), True, False)])
                    mm([x + (False, j == 1) for j, x in enumerate(lst)])
                else:
                    mm([(c, idb, blk("mcg" + H, k, 256), True, False)] + [x + (False, j == 1) for j, x in enumerate(lst)])
                if k == 0:
                    low = ap("c0s" + H)
                    (act if C["c0"][h] == "S" else cp)(low, c)
                else:
                    tt(ap("m%d" % k + H), c, low, A.min)
                    low = ap("m%d" % k + H)
                for x in costs if k == 1 and H in C["c1b"] else ():
                    mm([x])
            if C["ahead"] and s == 1:
                for b in range(2):
                    paint(apx("sel0", b, slice(1, 3), every), [[0, 256]], 0, -160.0)
            HI = ap(PC, 256, 320)
            act(ap("ofl" + H), ap(lb, l0, l0 + 64), bias=-U / 2)
            mm([(HI, ap("idq"), ap("ofl" + H), True, False)])
            mm([(blk(PB, 2 + b), bit(ap("m3" + H), b), idb, False, b == 1) for b in range(2)])
            scan(ap("rr" + H, 1, 257), ap("z16"), SC, A.add, A.min)
            tt(ap("ff" + H), ap("rr" + H, 0, 256), SC, A.is_gt)
            scan(ap("tp" + H), ap("p16"), ap("ff" + H), A.subtract, A.max)
            for b in range(2):
                {"S": act, "V": cp, "G": gcp}[C["zh"][b] if t else "V"](ap("zh" + H, 16 + b, 144, 16), ap("tp" + H, 128 * b + 15, 128 * b + 128, 16))
            mm([(bit(ap(PA, 0, 256), b), blk("ff" + H, b), idb, True, True) for b in range(2)])
            on = C["on"][h]
            if "f" in on:
                ts(ap("ft" + H), ap(PA, 0, 256), col(8), A.mult, col(12), A.add)
            else:
                act(ap("ft" + H), ap(PA, 0, 256), scale=col(8), bias=col(12))
            mm([(HI, ap("zh" + H, 16 - 2 * x, 144 - 2 * x), blk("hsel", x, 64), False, x == 7) for x in range(8)])
            if "2" in on:
                ts(ap("of2" + H), HI, U / 2, A.add)
            else:
                act(ap("of2" + H), HI, bias=U / 2)
            mm([(ap(PA, 256, 512), ap("lm"), ap("ft" + H), True, True)])
            um = C["um"][h]
            if "k" in on:
                ts(ap("msk" + H), ap(PA, 256, 512), 0.0, A.max, 2.0 ** 33, A.mult)
            else:
                act(ap("msk" + H), ap(PA, 256, 512), F.Relu, scale=2.0 ** 33)
            if um:
                act(ap(PA, 256, 512), ap(PA, 256, 512), F.Relu, scale=2.0 ** 33)
            for k in um:
                act(blk("gm" + H, int(k), 256), ind(ap("xt"), blk("of2" + H, int(k), 16)))
            for k in um:
                tt(blk("gm" + H, int(k), 256), ap(PA, 256, 512), blk("gm" + H, int(k), 256), A.min)
            if t and C["late"][h][t - 1] == "1":
                payload(t - 1, h, True)
                cur[2] = "walk"
            K, AA = ap(PA, 0, 128), ap(PB, 256, 384)
            mm([(AA, ap("one", p1=1), ap("ca", p1=1), True, False)])
            if t == 0:
                mm([(K, ap("r0", 0, 128), ap("uc"), True, False)]
                   + [(K, bit(ap("r0", p1=64), b), ap("rm0", 8 + 144 * h - 8 * b, 136 + 144 * h - 8 * b, p1=64), False, False) for b in range(2)])
            else:
                mm([(K, rin, ap("rm"), True, False)])
            for k in range(4):
                if str(k) not in um:
                    tt(blk("gm" + H, k, 256), ind(ap("xt"), blk("of2" + H, k, 16)), ap("msk" + H), A.min)
                mm([(ap(PB, 256 + k, 384, 4), bit(blk("gm" + H, k, 256), b), ap("bo2", 2 - 2 * b, 34 - 2 * b), False, k == 3 and b == 1)
                    for b in range(2)])
            for n, v in (("af", WHOLE - LIFT * U), ("cst", 0.5 - U / 2)):
                if n[0] in on:
                    ts(ap(n + H), AA, v, A.add)
                else:
                    act(ap(n + H), AA, bias=v)
            mm([(K, idf, ap("af" + H), False, False)])
            mm([(K, ap("idc"), ap("cst" + H), False, True)])
            if h == 1:
                take_up(t)
            tt(ap("ds" + H), AA, ap("cst" + H), A.subtract)
            xx = "xx" + H
            to, early = nxt if t < NV - 1 else last, C["early"][h]

            def send(k0, k1, e, sem):
                x = ap("mo", 64 * s + 16 * k0, 64 * s + 16 * k1)
                if e == "S":
                    act(x, ap(PB, 16 * k0, 16 * k1), bias=U / 2)
                elif e:
                    ts(x, ap(PB, 16 * k0, 16 * k1), U / 2, A.add)
                if sem:
                    write(to, x, ap("mi", 64 * s + 16 * k0, 64 * s + 16 * k1), sem)

            cost = dict(scale=-1.0 / (STEP * U), bias=130 + TOP / STEP - 0.25)
            for k in range(4):
                d = apx("sall" + H, k, every)
                scan(blk("so" + H, k), ap("z8"), K, A.min, A.max, 2 * TOP * U)
                ts(d, ap("so" + H, 128 * k + 7, 128 * k + 128, 8), int(U) - 1, an)
                if k < 3:
                    tt(ap("eq" + H), ind(d, L1), ap("ds" + H), A.not_equal)
                    tt(K, K, ap("eq" + H), A.mult)
                for k0, k1 in C["conv"]:
                    if k1 != k + 1:
                        continue
                    pair = str(k) in C["pair"][h]
                    for e in range(2 if pair else 1):
                        o, i0 = ap("zl" + H, 16 + 2 * e + 128 * k0, 16 + 128 * k1, 8), apx("sall" + H, slice(k0, k1), every)
                        if C["z3"][h][k] == "S":
                            act(o, i0, **(dict(scale=col(16 + 2 * e), bias=col(10 + 9 * e)) if pair else dict(bias=-U / 2)))
                        elif pair:
                            ts(o, i0, -U / 2, A.add, col(16 + 2 * e), A.mult)
                        else:
                            ts(o, i0, -U / 2, A.add)
                    for j in range(k0, k1):
                        n, pick = (4, "id2") if pair else (8, "idq")
                        mm([(ap(PB, 16 * j, 16 * j + 16), ap("zl" + H, 16 + 128 * j - 16 // n * x, 144 + 128 * j - 16 // n * x),
                             ap(pick, x, 16 * n, n), x == 0, x == n - 1) for x in range(n)])
                if k == early - 1:
                    both = C["ahead"] and t < NV - 1
                    send(0, early, C["eng"][h], None if both else "er%d" % s)
                    if C["ahead"]:
                        act(ap(xx, 64, 112), ap("so" + H, 7, 384, 8), scale=-cost["scale"], bias=-cost["bias"])
                    if both:
                        tt(apx("eo", s, slice(16, 48)), ap(xx, 80, 112), ap(xx, 0, 32), A.add)
                        two(to, [(ap("mo", 64 * s, 64 * s + 48), ap("mi", 64 * s, 64 * s + 48)), (apx("eo", s, every), blk("ei", s, 48))], "er%d" % s)
                if k == 0:
                    act(ap(xx, 0, 64), ind(ap("so" + H, 0, 128), LX), **cost)
            k = 3 if C["ahead"] else 0
            if "x" in on:
                ts(ap(xx, 64 + 16 * k, 128), ap("so" + H, 128 * k + 7, 512, 8), -cost["scale"], A.mult, -cost["bias"], A.add)
            else:
                act(ap(xx, 64 + 16 * k, 128), ap("so" + H, 128 * k + 7, 512, 8), scale=-cost["scale"], bias=-cost["bias"])
            rows_first = H in C["rf"][t == NV - 1]
            send(early, 4, "S" if H in C["sx"] else "V", None if rows_first else "ar%d" % s)
            first = len(ops) - 1
            o = ap(PA if C["rb"] == "A" else PC, 128, 256)
            mm([(o[:2] + (p, p + 64), ap(xx, c0, c0 + 64), idb, c0 == 0, c0 == 64) for p in (0, 64) for c0 in (0, 64)])
            if "r" in on:
                ts(blk("ro", s), o, RB, A.add, 0.0, A.max)
            else:
                act(blk("ro", s), o, F.Relu, bias=RB)
            write(to, blk("ro", s), blk("ri", s), "br%d" % s)
            if not rows_first:
                ops[-1]["soft"] = [first]
            else:
                send(early, 4, None, "ar%d" % s)
            if t < NV - 1 and C["late"][h][t] == "0":
                payload(t, h, False)
    take_up(NV)
    for h in range(2):
        cur[:] = [h, NV - 1, "home"]
        payload(NV - 1, h, False)
    r = 16 * NV % 128
    for h in range(2):
        cur[:] = [h, NV - 1, "end"]
        for k, o in enumerate((T.ys, T.ym)):
            a = blk("yo", 2 * h + k, 256)
            b = blk("smo", 4 * (2 * NV - 2 + h) + 3, 256) if k == 0 and str(h) in C["pet"] else blk("loc%d" % h, k, 256)
            if str(h) in C["pe3"]:
                act(a, blk("py%d" % h, k, 256))
            elif k or str(h) not in C["pre"]:
                tt(a, blk("py%d" % h, k, 256), b, A.add)

            def store(o=o, j=2 * h + k, h=h):
                q[C["st"][j]].dma_start(o[128 - r:128, 256 * h:256 * h + 256], R(blk("yo", j, 256, p1=r))).then_inc(T.sem.stored, 16)
                q[C["st"][j]].dma_start(o[0:128 - r, 256 * h:256 * h + 256], R(blk("yo", j, 256, p0=r))).then_inc(T.sem.stored, 16)
            op(C["st"][2 * h + k], store, [a], [], None, dma=("stored", 128), by=1 << 17, nd=2)
    return ops, q, sent[0]


def link(ops):
    wr = {n: np.full(int(np.prod(v[1][1:])), -1) for n, v in SCRATCH.items()}
    rd = {n: [] for n in SCRATCH}
    bank = {n: [None, [], []] for n, v in SCRATCH.items() if v[0] == "psum"}
    for i, o in enumerate(ops):
        d = set()
        for a in o["rd"] + o["wr"]:
            d.update(int(x) for x in np.unique(wr[a[0]][cols(a)]) if x >= 0)
        for n in {a[0] for a in o["rd"] + o["wr"] if a[0] in bank}:
            b = bank[n]
            if b[0] != o["eng"]:
                b[:] = [o["eng"], [], b[1]]
            d.update(b[2] + (b[1][-1:] if o["eng"] == "P" else []))
            b[1].append(i)
        for a in o["wr"]:
            cs = set(cols(a).tolist())
            d.update(j for (j, c) in rd[a[0]] if not cs.isdisjoint(c))
            rd[a[0]] = [(j, c - cs) for (j, c) in rd[a[0]] if c - cs]
        for a in o["rd"]:
            rd[a[0]].append((i, set(cols(a).tolist())))
        for a in o["wr"]:
            wr[a[0]][cols(a)] = i
        d.discard(i)
        o["far"] = sorted(j for j in d if not (o["eng"] == "P" and ops[j]["eng"] == "P"))
        o["own"] = [j for j in o["far"] if ops[j]["eng"] == o["eng"] and "dma" not in ops[j]]
        o["other"] = [j for j in o["far"] if j not in o["own"]]
        o["deps"] = sorted(d | set(o.get("soft", [])))


KEPT = {}


def times(ops, m):
    dur, pre, wire, post = [], [], [], []
    for o in ops:
        if "by" in o:
            x = (m["di"] * o["nd"], m["di"] + 0.6 * m["dl"], o["by"] / m["rate"], 0.4 * m["dl"])
        elif "rows" in o:
            n = o["cost"][2]
            n = n * m["g"] + (m["once"] if o["visit"] < 0 else 0)
            x = (n, n + 0.6 * m["net"], o["rows"][0] * m["row"] + o["rows"][1] / m["rate"], 0.4 * m["net"])
        else:
            c, ga, n, ns, two = o["cost"]
            c += ga * max(m["ga"], m["tti"] if two else 0)
            x = (c * m["cy"] + n * m[{"V": "v", "S": "s", "P": "m", "G": "g"}[o["eng"]]] + ns, 0.0, 0.0, m["hop"])
        for lst, v in zip((dur, pre, wire, post), x):
            lst.append(v)
    return dur, pre, wire, post, m["hop"] - m["hs"]


def replay(ops, seq, tm, at=None, why=None):
    dur, pre, wire, post, near = tm
    free, done, line, end, once = {e: 0.0 for e in "VSPGY"}, [0.0] * len(ops), 0.0, 0.0, ONCE
    before = {e: None for e in free}
    for i in seq:
        o = ops[i]
        e = o["eng"]
        a, w = free[e], before[e]
        for j in o["other"]:
            if done[j] > a:
                a, w = done[j], j
        for j in o["own"]:
            if done[j] - near > a:
                a, w = done[j] - near, j
        if at is not None:
            at[i], before[e] = a, i
            if why is not None:
                why[i] = w
        if once and "rows" in o:
            a, once = a + once, 0.0
        free[e] = b = a + dur[i]
        if wire[i]:
            line = max(a + pre[i], line) + wire[i]
            b = max(b, line)
        done[i] = b = b + post[i]
        if b > end:
            end = b
    return end


def order(ops, tries=TRIES):
    n = len(ops)
    kids = [[] for _ in ops]
    for i, o in enumerate(ops):
        for j in o["deps"]:
            kids[j].append(i)
    eng = [o["eng"] for o in ops]
    waits = [len(o["deps"]) for o in ops]
    tms = [times(ops, m) for m in GUESS]
    dur, pre, wire, post, near = tms[0]
    tail = [0.0] * n
    for i in range(n - 1, -1, -1):
        tail[i] = max(dur[i], pre[i] + wire[i]) + post[i] + max([tail[k] for k in kids[i]], default=0.0)
    ref = [i for i, o in enumerate(ops) if o["kind"][1:] in (("walk", "V", "rr0", 1), ("walk", "V", "rr1", 1)) and o["visit"] == 2]
    for i, o in enumerate(ops):
        tail[i] += tail[ref[0]] - tail[ref[1]] if o["half"] == 1 else 0.0
    aside = [o["kind"][1] == "sum" or o["kind"][1] in ("first", "late", "now") and o["eng"] in "VG" for o in ops]
    loose = [i for i, o in enumerate(ops) if o["kind"][1] in ("first", "late", "now", "sum")]
    for i in range(n):
        tail[i] -= CFG["fit"][0] if aside[i] else 0.0
    fixed = [1e9 - 1e6 * i if "soon" in o or "by" in o and not o["deps"] else 0.0 for i, o in enumerate(ops)]

    def run(pri, slack):
        left = [len(o["deps"]) for o in ops]
        rdy = [0.0] * n
        ready = {e: [] for e in "VSPGY"}
        for i in range(n):
            if not left[i]:
                ready[eng[i]].append(i)
        free, seq, at, line, once = {e: 0.0 for e in ready}, [], [0.0] * n, 0.0, ONCE
        for _ in range(n):
            t0, e = min((max(free[e], min([rdy[i] for i in r])), e) for e, r in ready.items() if r)
            r = ready[e]
            i = max([j for j in r if rdy[j] <= t0], key=pri.get)
            lim = t0 + (1.2 * (dur[i] + wire[i]) if e == "G" else CFG["fit"][1] * dur[i] if aside[i] else min(slack, 0.5 * dur[i]))
            soon = [j for j in r if t0 < rdy[j] <= lim and pri[j] > pri[i]]
            if soon:
                i = max(soon, key=pri.get)
            r.remove(i)
            seq.append(i)
            a = at[i] = max(t0, rdy[i])
            if once and "rows" in ops[i]:
                a, once = a + once, 0.0
            free[e] = done = a + dur[i]
            if wire[i]:
                line = max(a + pre[i], line) + wire[i]
                done = max(done, line)
            done += post[i]
            for k in kids[i]:
                rdy[k] = max(rdy[k], done if i in ops[k]["other"] else done - near if i in ops[k]["own"] else a + dur[i])
                left[k] -= 1
                if not left[k]:
                    ready[eng[k]].append(k)
        ends = [replay(ops, seq, tm) for tm in tms]
        return sum(ends) / len(ends), seq, at, ends

    def shake(lag):
        best = None
        for slack in (0.0, 130.0, 300.0, 600.0):
            pri = {i: tail[i] + fixed[i] - (lag if ops[i]["half"] == 1 else 0.0) for i in range(n)}
            got = run(pri, slack)
            if best is None or got[0] < best[0][0]:
                best = (got, pri, slack)
        for trial in range(tries):
            got, pri, slack = best
            t = rng.random() * got[3][0]
            new = dict(pri)
            span, amp = rng.choice([2000.0, 6000.0, 15000.0]), rng.choice([300.0, 1500.0, 6000.0])
            shift = {0: rng.normal() * amp, 1: 0.0, None: 0.0}
            for i in range(n):
                if t <= got[2][i] < t + span:
                    new[i] += shift[ops[i]["half"]] + rng.normal() * amp * 0.3
            tried = run(new, slack)
            if tried[0] <= got[0]:
                best = (tried, new, slack)
        return best[0][1]

    queue = ["VSPGY".index(e) for e in eng]
    other, own, far = [o["other"] for o in ops], [o["own"] for o in ops], ["rows" in o for o in ops]
    deps = [o["deps"] for o in ops]

    def play(seq, tm, s0, marks, done):
        dur, pre, wire, post, near = tm
        free, line, end, once = marks[s0]
        free, marks, done = list(free), marks[:s0 + 1], list(done)
        for c in range(s0 * 48, n, 48):
            if c > s0 * 48:
                marks.append((tuple(free), line, end, once))
            for i in seq[c:c + 48]:
                e = queue[i]
                a = free[e]
                for j in other[i]:
                    if done[j] > a:
                        a = done[j]
                for j in own[i]:
                    if done[j] - near > a:
                        a = done[j] - near
                if wire[i]:
                    if once and far[i]:
                        a, once = a + once, 0.0
                    free[e] = b = a + dur[i]
                    line = max(a + pre[i], line) + wire[i]
                    b = max(b, line)
                else:
                    free[e] = b = a + dur[i]
                done[i] = b = b + post[i]
                if b > end:
                    end = b
        return end, marks, done

    walk = [i for i, o in enumerate(ops) if o["kind"][1:3] == ("walk", "V") and o["half"] is not None]

    def worth(state):
        return sum((s[0] + CFG["side"][1] * sum([s[2][i] for i in walk]) / len(walk)) / z for s, z in zip(state, size))

    def along(first, near, inside, other_end):
        move, todo = [first], [first]
        while todo and len(move) < 10:
            for j in near[todo.pop()]:
                if inside(j) and j not in move:
                    move.append(j)
                    todo.append(j)
        return None if todo or other_end in move else move

    def swap(seq, count):
        zero = [((0.0,) * 5, 0.0, 0.0, ONCE)]
        keep = None
        for trial in range(count):
            if trial % 8 == 0:
                tm, at, why = tms[rng.integers(len(tms))], [0.0] * n, [None] * n
                replay(ops, seq, tm, at, why)
                i, pairs = int(np.argmax(at)) if rng.random() < CFG["side"][0] else walk[rng.integers(len(walk))], []
                while why[i] is not None:
                    if why[i] not in deps[i]:
                        pairs.append((why[i], i))
                    i = why[i]
                pairs = pairs[:30] if i < 0 or rng.random() < 0.3 else pairs
                if trial % 80 == 0:
                    seq = sorted(seq, key=lambda j: at[j])
                    state = [play(seq, tm, 0, zero, [0.0] * n) for tm in tms]
                    total = worth(state)
                    if keep is None or total < keep[0]:
                        keep = (total, seq)
                pos = [0] * n
                for j, x in enumerate(seq):
                    pos[x] = j
            if not pairs:
                continue
            p, i = pairs[rng.integers(len(pairs))]
            up = rng.random() < 0.6
            if rng.random() < CFG["fit"][2]:
                x = loose[rng.integers(len(loose))]
                waits = [j for j in seq[max(0, pos[x] - 200):pos[x] + 200] if eng[j] == eng[x] and j != x and why[j] in deps[j]]
                if not waits:
                    continue
                j = waits[rng.integers(len(waits))]
                up = pos[j] < pos[x]
                p, i = (j, x) if up else (x, seq[pos[j] - 1])
            a, b = pos[p], pos[i]
            if a >= b:
                continue
            more = int(rng.random() * 12) if rng.random() < 0.3 else 0
            if up:
                a = min(a, max([a - more, 0] + [pos[j] + 1 for j in deps[i]]))
                move = along(i, deps, lambda j: pos[j] >= a, p)
                if not move:
                    continue
                new = seq[:a] + sorted(move, key=lambda x: pos[x]) + [x for x in seq[a:b + 1] if x not in move] + seq[b + 1:]
            else:
                b = max(b, min([b + more, n - 1] + [pos[k] - 1 for k in kids[p]]))
                move = along(p, kids, lambda j: pos[j] <= b, i)
                if not move:
                    continue
                new = seq[:a] + [x for x in seq[a:b + 1] if x not in move] + sorted(move, key=lambda x: pos[x]) + seq[b + 1:]
            got = [play(new, tm, a // 48, s[1], s[2]) for tm, s in zip(tms, state)]
            tried = worth(got)
            if tried <= total + CFG["heat"] * (1 - trial / count) * rng.random():
                seq, total, state = new, tried, got
                for j in range(a, b + 1):
                    pos[seq[j]] = j
        return keep

    if "best" not in KEPT:
        rng = np.random.default_rng(7)
        first = [shake(lag) for lag in CFG["lags"]]
        size = [replay(ops, first[0], m) for m in tms]
        seq = swap(min(swap(x, CFG["swaps"][0]) for x in first)[1], CFG["swaps"][1])[1]
        at = [0.0] * n
        replay(ops, seq, tms[0], at)
        KEPT["best"] = (seq, at, [replay(ops, seq, m) for m in tms])
    seq, at, ends = KEPT["best"]
    for i in range(n):
        ops[i]["at"] = at[i]
    return seq, ends


def rank_program(g, core, T, topo):
    rank = T.rank_of(core)
    if rank is None:
        return
    ops, q, sent = build(g, T, topo, rank)
    link(ops)
    seq, _ = order(ops)
    used = set()
    for o in ops:
        used.update(o["far"])
    count, seen = {}, {e: {} for e in q}
    for i in seq:
        o = ops[i]
        e = o["eng"]
        know = seen[e]
        need = {}
        for j in o["far"]:
            sem, val = ops[j]["sig"]
            if know.get(sem, 0) < val and need.get(sem, (0, 0))[0] < val:
                need[sem] = (val, j)
        for sem, (val, j) in sorted(need.items(), key=lambda kv: -ops[kv[1][1]]["at"]):
            if know.get(sem, 0) < val:
                q[e].wait_ge(T.sem[sem], val)
                know[sem] = val
                for s2, v2 in ops[j]["knew"].items():
                    if know.get(s2, 0) < v2:
                        know[s2] = v2
        h = o["fn"]()
        o["knew"] = dict(know)
        if "dma" in o:
            o["sig"] = o["dma"]
            if e == "G":
                o["knew"] = {}
        elif i in used:
            count["c" + e] = count.get("c" + e, 0) + 1
            h.then_inc(T.sem["c" + e], 1)
            o["sig"] = ("c" + e, count["c" + e])
    for sem, val in sorted(count.items()):
        g.wait_ge(T.sem[sem], val)
    g.wait_ge(T.sem.sent, sent)
    g.sync.wait_ge(T.sem.stored, 128)
